import numpy as np, ml_dtypes
CORES = [9,25,41,57]
N = 4
BF = ml_dtypes.bfloat16
def gentries(a):
    return np.ascontiguousarray(a.reshape(8, 16, -1).transpose(0, 2, 1)).reshape(8, -1)
def gtable(e):
    e = np.asarray(e); return np.ascontiguousarray(e.reshape(8, -1, 16).transpose(0, 2, 1)).reshape(128, -1).astype(np.int32)
M, L, S, ST = 512, 5, 512, 10
LPR, C, W = 4, 2628, 10528
LEV = [(16, LPR, 0), (32, 16 * LPR, LPR)] + [(288 + d * N * M, M, 17 * LPR + d * M) for d in range(L)]
START = np.array([v[0] for v in LEV]); SIZE = np.array([v[1] for v in LEV])
A8 = np.arange(8)[:, None]
def grow(rng, bias):
    tri = np.zeros((N, 8, 16, C), np.int64); par = np.zeros((N, 8, C - LPR), np.int64); let = np.zeros((N, 8, C - LPR), np.int64)
    G = np.zeros((8, 16, W), np.int64); G[:, :, 0] = 16 + np.arange(16)
    D = [np.repeat(G[:, :, :1], LPR, axis=2) for r in range(N)]
    for d in range(len(LEV)):
        b, m, o = LEV[d]; new = []
        for r in range(N):
            own = tri[r, :, :, o:o + m]
            if d + 1 < len(LEV):
                b2, m2, o2 = LEV[d + 1]
                n = D[r].transpose(0, 2, 1); lev = np.searchsorted(START, n, side="right"); who = (n - START[lev - 1]) // SIZE[lev - 1]
                key = rng.random((8, m, 16)) + bias(d, r, lev, who)
                pick = rng.permuted(np.argsort(key.reshape(8, -1), axis=1)[:, :m2], axis=1)
                p = pick >> 4; c = pick & 15
                par[r, :, o2 - LPR:o2 - LPR + m2] = p; let[r, :, o2 - LPR:o2 - LPR + m2] = c
                own[A8, c, p] = b2 + r * m2 + np.arange(m2)
                new.append(D[r][A8, c, p])
            G[:, :, b + r * m:b + (r + 1) * m] = np.where(own != 0, own, D[r])
        D = [np.take_along_axis(G, fl[:, None, :], 2) for fl in new]
    return tri, par, let, G
def walk(rng, G, go):
    txt = np.zeros((N, 8, ST, S), np.int64); s = np.zeros((N, 8, S), np.int64)
    for t in range(ST):
        col = G[np.arange(8)[None, :, None], :, s]
        c = np.argmax(rng.random(col.shape) + (col > s[..., None]) * (rng.random((N, 8, S, 1)) < go[..., None]), axis=-1)
        txt[:, :, t] = c; s = np.take_along_axis(col, c[..., None], 3)[..., 0]
    return txt
def pack(tri, par, let, txt):
    return {"tri": np.ascontiguousarray(tri.reshape(N, 128, C)).astype(np.int32), "par": np.stack([gtable(a) for a in par]),
            "let": let.astype(np.int32), "txt": np.ascontiguousarray(txt.reshape(N, 8, ST * S)).astype(np.int32)}
def setup_inputs(rng):
    pull = rng.choice(np.array([0.0, 0.2, 0.5, 2.0]), (N, 8, 1, 1))
    tri, par, let, G = grow(rng, lambda d, r, lev, who: -pull[r] * lev)
    return pack(tri, par, let, walk(rng, G, rng.choice(np.array([0.3, 0.7, 0.95]), (N, 8, S))))
def setup_inputs_depth(rng):
    pull = np.where(rng.permutation(8) < 4, 4.0, -4.0).reshape(8, 1, 1)
    tri, par, let, G = grow(rng, lambda d, r, lev, who: -pull * lev)
    return pack(tri, par, let, walk(rng, G, rng.choice(np.array([0.5, 1.0, 1.0]), (N, 8, S))))
def setup_inputs_bushy(rng):
    def bias(d, r, lev, who):
        v = np.zeros(lev.shape); m = lev.shape[1]
        v[0::2] = 10.0 * np.argsort(rng.random((4, m)), axis=1)[:, :, None]
        v[1::2] = 10.0 * np.argsort(rng.random((4, m, 16)), axis=2)
        return v
    tri, par, let, G = grow(rng, bias)
    txt = walk(rng, G, rng.choice(np.array([0.2, 0.8, 1.0]), (N, 8, S)))
    for r in range(N):
        g = 2 * rng.permutation(4) + 1
        txt[r, g[0]] = (np.add.accumulate(rng.integers(1, 16, ST)) & 15)[:, None]
        txt[r, g[1]] = LPR * ((r + 1 + int(rng.integers(0, N - 1))) % N) + rng.integers(0, LPR, (ST, S))
    return pack(tri, par, let, txt)
def setup_inputs_ends(rng):
    def bias(d, r, lev, who):
        v = np.zeros(lev.shape); m = lev.shape[1]; p = np.arange(m); c = np.arange(16)
        v[0::2] = 100.0 * np.minimum(p, m - 1 - p)[None, :, None]
        v[1::2] = 10.0 * ((c != 0) & (c != 15))[None, None, :] - 0.5 * lev[1::2]
        return v
    tri, par, let, G = grow(rng, bias)
    txt = walk(rng, G, rng.choice(np.array([0.3, 0.7, 1.0]), (N, 8, S))); q = S >> 3
    txt[..., :q] = 0; txt[..., q:2 * q] = 15
    txt[..., 2 * q:3 * q] = (15 * (np.arange(ST) & 1))[None, None, :, None]
    txt[..., 3 * q:4 * q] = rng.integers(0, 16, (N, 8, 1, q)); txt[..., 4 * q:5 * q] = txt[..., 7 * q:7 * q + 1]
    return pack(tri, par, let, txt)
def setup_inputs_spread(rng):
    wt = np.stack([0.15 * rng.permutation(16) ** np.exp2(rng.integers(-1, 2)) for g in range(8)])[:, None, :]
    pull = rng.choice(np.array([-0.5, 0.0, 0.5, 3.0]), (len(LEV), N, 8, 1, 1)); q = int(rng.integers(0, N))
    tri, par, let, G = grow(rng, lambda d, r, lev, who: wt - pull[d, r] * lev + (100.0 if d == 2 else 0.0) * (who != q))
    txt = walk(rng, G, rng.random((N, 8, S)))
    odd = np.minimum((16 * rng.random((N, 8, ST, S)) ** np.exp2(rng.integers(-3, 4, (N, 8, 1, S)))).astype(np.int64), 15)
    return pack(tri, par, let, np.where(rng.random((N, 8, 1, S)) < 0.4, odd, txt))
def check_inputs(d):
    bad = []
    for k in ("let", "txt"):
        if np.min(d[k]) < 0 or np.max(d[k]) > 15: bad.append("range of " + k)
    par = np.stack([gentries(a) for a in d["par"]]).astype(np.int64); let = d["let"].astype(np.int64)
    for i in range(1, len(LEV)):
        m, o = LEV[i][1:]; part = par[:, :, o - LPR:o - LPR + m]
        if np.min(part) < 0 or np.max(part) >= LEV[i - 1][1]: bad.append("range of par on level " + str(i + 1))
    if bad: return bad
    want = np.zeros((N, 8, 16, C), np.int64)
    for i in range(1, len(LEV)):
        b, m, o = LEV[i]
        for r in range(N):
            want[r][A8, let[r, :, o - LPR:o - LPR + m], LEV[i - 1][2] + par[r, :, o - LPR:o - LPR + m]] = b + r * m + np.arange(m)
    if np.count_nonzero(want) != N * 8 * (C - LPR): bad.append("two states with one parent and letter")
    if not np.array_equal(want.reshape(N, 128, C), d["tri"]): bad.append("tri against par and let")
    return bad
def reference(tri, par, let, txt):
    t4 = tri.astype(np.int64).reshape(N, 8, 16, C); pl = np.stack([gentries(a) for a in par]).astype(np.int64)
    ll = let.astype(np.int64); tx = txt.astype(np.int64).reshape(N, 8, ST, S)
    G = np.zeros((8, 16, W), np.int64); G[:, :, 0] = 16 + np.arange(16)
    fail = np.zeros((8, W), np.int64)
    yg = np.zeros((N, 8, 16, C), np.int64); yf = np.zeros((N, 8, C), np.int64)
    for i in range(len(LEV)):
        b, m, o = LEV[i]
        for r in range(N):
            fl = np.zeros((8, m), np.int64)
            if i > 0:
                pb, pm = LEV[i - 1][:2]
                fp = np.take_along_axis(fail, pb + r * pm + pl[r, :, o - LPR:o - LPR + m], 1)
                fl = G[A8, ll[r, :, o - LPR:o - LPR + m], fp]
            own = t4[r, :, :, o:o + m]
            full = np.where(own != 0, own, np.take_along_axis(G, fl[:, None, :], 2))
            fail[:, b + r * m:b + (r + 1) * m] = fl; G[:, :, b + r * m:b + (r + 1) * m] = full
            yf[r, :, o:o + m] = fl; yg[r, :, :, o:o + m] = full
    s = np.zeros((N, 8, S), np.int64); big = np.zeros((N, 8, S), np.int64)
    for t in range(ST):
        s = G[np.arange(8)[None, :, None], tx[:, :, t], s]
        big = np.maximum(big, s)
    return {"yg": yg.reshape(N, 128, C).astype(np.float32), "yf": yf.astype(np.float32), "yl": s.astype(np.float32), "ym": big.astype(np.float32)}

@@ -1,0 +1,601 @@
+from concourse.bass import DstId, RemoteDMATransfer
+from concourse.mybir import AluOpType as A, ActivationFunctionType as F
+
+K = 0.008435
+A0 = 5256
+NONE = 6e-20
+MAGIC = 12582912
+SIZE = {1: 4, 2: 64, 3: 512, 4: 512, 5: 512, 6: 512, 7: 512}
+OWN = {1: 0, 2: 4, 3: 68, 4: 580, 5: 1092, 6: 1604, 7: 2116}
+BASE = {1: 0, 2: 16, 3: 272, 4: 2320, 5: 4368, 6: 6416, 7: 8464}
+SLOT = 72
+PAD = {3: 0, 4: 0, 5: 0, 6: 16}
+
+SCRATCH = {
+    "tab": ("sbuf", [128, 8464], "bfloat16"), "raw": ("sbuf", [128, 4 * SLOT], "int32"),
+    "c1f": ("sbuf", [128, 16], "float32"), "c2f": ("sbuf", [128, 256], "float32"), "c2": ("sbuf", [128, 256], "bfloat16"),
+    "leti": ("sbuf", [128, 164], "int32"), "letb": ("sbuf", [128, 164], "bfloat16"), "maskl": ("sbuf", [128, 2624], "bfloat16"),
+    "pari": ("sbuf", [128, 164], "int32"), "pu": ("sbuf", [128, 164], "uint16"),
+    "vi": ("sbuf", [128, 320], "int32"), "vb": ("sbuf", [128, 320], "bfloat16"),
+    "vq": ("sbuf", [128, 320], "bfloat16"), "maskt": ("sbuf", [128, 4608], "bfloat16"),
+    "fl2": ("sbuf", [128, 16], "uint16"), "d2": ("sbuf", [128, 64], "bfloat16"),
+    "lt": ("sbuf", [128, 320], "uint16"), "ltp": ("sbuf", [128, 320], "uint16"), "flp": ("sbuf", [128, 32], "uint16"),
+    "lnf": ("sbuf", [128, 164], "float32"), "lnt": ("sbuf", [128, 320], "float32"), "lnp": ("sbuf", [128, 320], "float32"),
+    "rm": ("sbuf", [128, 32], "float32"), "last": ("sbuf", [128, 64], "float32"), "lastm": ("sbuf", [128, 64], "float32"),
+    "oy": ("sbuf", [128, 64], "float32"),
+    "nf": ("sbuf", [128, 164], "float32"), "tr1": ("sbuf", [128, 128], "float32"), "tr2": ("sbuf", [128, 128], "float32"),
+    "zz": ("sbuf", [128, 4], "float32"), "g6": ("sbuf", [128, 512], "bfloat16"),
+    "h7": ("sbuf", [128, 512], "bfloat16"), "g7": ("sbuf", [128, 512], "bfloat16"),
+    "ya": ("sbuf", [128, 2628], "float32"), "yb": ("sbuf", [128, 2628], "float32"), "yo": ("sbuf", [128, 2628], "float32"),
+    "ones": ("sbuf", [128, 128], "bfloat16"), "blk0": ("sbuf", [128, 128], "bfloat16"), "blk": ("sbuf", [128, 128], "bfloat16"),
+    "blk2": ("sbuf", [128, 128], "bfloat16"), "row2": ("sbuf", [128, 128], "bfloat16"),
+    "onesf": ("sbuf", [128, 128], "float32"), "ident": ("sbuf", [128, 128], "float32"),
+    "pcol": ("sbuf", [128, 1], "int32"), "cci": ("sbuf", [128, 1], "int32"), "ccf": ("sbuf", [128, 1], "float32"),
+    "cc2": ("sbuf", [128, 1], "float32"), "bq": ("sbuf", [128, 1], "float32"),
+    "row16": ("sbuf", [128, 16], "float32"), "ee": ("sbuf", [128, 16], "float32"),
+    "brd": ("sbuf", [128, 2048], "bfloat16"), "br2": ("sbuf", [128, 2048], "bfloat16"), "sel": ("sbuf", [128, 2048], "bfloat16"),
+}
+for _d in range(3, 7):
+    SCRATCH["ti%d" % _d] = ("sbuf", [128, 512], "int32")
+    SCRATCH["cf%d" % _d] = ("sbuf", [128, 512], "float32")
+    SCRATCH["tc%d" % _d] = ("sbuf", [128, PAD[_d] + 2048], "bfloat16")
+for _d in range(3, 6):
+    SCRATCH["d%d" % _d] = ("sbuf", [128, 512], "bfloat16")
+for _d in range(3, 8):
+    SCRATCH["fl%d" % _d] = ("sbuf", [128, 128], "uint16")
+    SCRATCH["xf%d" % _d] = ("sbuf", [128, 512], "bfloat16")
+for _t in range(1, 10):
+    SCRATCH["xt%d" % _t] = ("sbuf", [128, 512], "bfloat16")
+for _t in range(6, 10):
+    SCRATCH["xp%d" % _t] = ("sbuf", [128, 512], "bfloat16")
+for _b in ("pm0", "pm1", "pt0", "pt1", "pf0", "pf1", "px0", "px1"):
+    SCRATCH[_b] = ("psum", [128, 512], "float32")
+
+LOADS = ["ti12", "let", "ti3", "par", "txt", "ti4", "ti5", "ti6"]
+SEMAPHORES = (["v", "s", "p", "gc", "out", "sent", "a_raw"] + ["ld_" + n for n in LOADS]
+              + ["a_t%d" % d for d in range(3, 7)] + ["a_f%d" % d for d in range(3, 7)] + ["h%d" % d for d in range(4, 7)])
+
+
+def helper_of(core, ranks, topo):
+    for h in topo.cores_of(core):
+        if h != core and topo.die(h) != topo.die(core) and all(topo.may_write(h, r) for r in ranks if r != core):
+            return h
+    return None
+
+
+def bits(engines):
+    m = 0
+    for e in engines:
+        m |= 1 << e
+    return m
+
+
+def dst_id(c, topo):
+    rid, pid, _ = topo.addr(c)
+    return DstId(rid=rid, pnc=pid)
+
+
+def send(g, T, topo, core, dsts, ap, sem):
+    g.remote_dma_fused([RemoteDMATransfer(dst_ids=[dst_id(c, topo) for c in dsts], dma_engine_mask=topo.mask(core, dsts[0]),
+                                          remote_sem=T.sem[sem], srcs=[ap], dsts=[ap for c in dsts], alu_op=0)],
+                       local_sem=T.sem["sent"])
+    return len(topo.engines(core, dsts[0]))
+
+
+def helper_program(g, core, T, topo, r):
+    own = T.cores[r]
+    others = [c for c in T.cores if c != own]
+    near = spare_engines(own, core, others[0], topo)
+    n = 0
+    for d in range(4, 7):
+        g.wait_ge(T.sem["h%d" % d], len(near))
+        n += send(g, T, topo, core, others, T["tc%d" % d][:, PAD[d] + 512 * r:PAD[d] + 512 * r + 512], "a_t%d" % d)
+    g.wait_ge(T.sem["sent"], n)
+
+
+def spare_engines(core, helper, other, topo):
+    far = set(topo.engines(core, other))
+    return [e for e in topo.engines(core, helper) if e not in far]
+
+
+def rank_program(g, core, T, topo):
+    rank = T.rank_of(core)
+    if rank is None:
+        for i, c in enumerate(T.cores):
+            if helper_of(c, T.cores, topo) == core:
+                helper_program(g, core, T, topo, i)
+        return
+    R = rank
+    others = [c for c in T.cores if c != core]
+    helper = helper_of(core, T.cores, topo)
+    queue = {"v": g.vector, "s": g.scalar, "p": g.tensor, "gc": g, "y": g.sync}
+    cnt = {"v": 0, "s": 0, "p": 0, "gc": 0, "out": 0, "sent": 0}
+    seen = {}
+
+    def wait(q, *hs):
+        for h in hs:
+            if h is None:
+                continue
+            sem, val = h
+            if seen.get((q, sem), 0) < val:
+                queue[q].wait_ge(T.sem[sem], val)
+                seen[(q, sem)] = val
+
+    def fin(q, ins):
+        cnt[q] += 1
+        ins.then_inc(T.sem[q], 1)
+        return (q, cnt[q])
+
+    V, S, P = g.vector, g.scalar, g.tensor
+    H = {}
+
+    def load(name, pairs):
+        for out, in_ in pairs:
+            g.sync.dma_start(out, in_).then_inc(T.sem["ld_" + name], 16)
+        H["ld_" + name] = ("ld_" + name, 16 * len(pairs))
+
+    slot = SLOT * R
+    load("ti12", [(T.raw[:, slot:slot + 68], T.tri[:, 0:68])]
+         + [(T.raw[:, slot + 68 + j:slot + 69 + j], T.let[:, 16 * j:16 * j + 16]) for j in range(4)])
+    load("ti3", [(T.ti3[:, :], T.tri[:, OWN[3]:OWN[4]])])
+    load("let", [(T.leti[:, :], T.let[:, :])])
+    load("par", [(T.pari[:, :], T.par[:, :])])
+    for d in range(4, 7):
+        load("ti%d" % d, [(T["ti%d" % d][:, :], T.tri[:, OWN[d]:OWN[d + 1]])])
+    load("txt", [(T.vi[:, 32 * t:32 * t + 32], T.txt[:, 512 * t:512 * t + 512]) for t in range(10)])
+
+    def store(out, in_, *hs):
+        wait("y", *hs)
+        g.sync.dma_start(out, in_).then_inc(T.sem["out"], 16)
+        cnt["out"] += 16
+
+    H["ones"] = fin("v", V.memset(T.ones[:, :], 1.0))
+    H["pcol"] = fin("gc", g.iota(T.pcol[:, :], [[0, 1]], 0, 1))
+    H["row16"] = fin("gc", g.iota(T.row16[:, :], [[1, 16]], 0, 0, allow_small_or_imprecise_dtypes=True))
+    wait("gc", H["ones"])
+    H["blk0"] = fin("gc", g.affine_select(T.blk0[:, :], T.ones[:, :], [[-16, 8], [0, 16]], A.is_ge, 0.0, 0, 1))
+    wait("gc", H["blk0"])
+    H["blk"] = fin("gc", g.affine_select(T.blk[:, :], T.blk0[:, :], [[16, 8], [0, 16]], A.is_ge, 0.0, 15, -1))
+    H["row2"] = fin("gc", g.iota(T.row2[:, :], [[0, 8], [-2, 16]], 0, 0, allow_small_or_imprecise_dtypes=True))
+    H["sel0"] = fin("v", V.memset(T.sel[:, :], 0.0))
+    wait("v", H["pcol"])
+    h = fin("v", V.tensor_scalar(T.cci[:, :], T.pcol[:, :], 15, None, A.bitwise_and))
+    wait("v", h)
+    H["ccf"] = fin("v", V.tensor_copy(T.ccf[:, :], T.cci[:, :]))
+    wait("v", H["ccf"], H["row16"])
+    H["ee"] = fin("v", V.tensor_scalar(T.ee[:, :], T.row16[:, :], T.ccf[:, 0:1], None, A.is_equal))
+    h = fin("v", V.tensor_tensor(T.cc2[:, :], T.ccf[:, :], T.ccf[:, :], A.mult))
+    wait("v", h, H["ee"], H["blk"])
+    H["bq"] = fin("v", V.tensor_scalar(T.bq[:, :], T.cc2[:, :], -1.0, 1.0, A.mult, A.add))
+    wait("s", H["sel0"], H["blk"])
+    for i in range(16):
+        H["sel"] = fin("s", S.activation(T.sel[:, 129 * i:128 * (i + 1):16], T.blk[:, i:128:16], F.Copy))
+    for i in range(16):
+        H["brd"] = fin("v", V.tensor_scalar(T.brd[:, 128 * i:128 * i + 128], T.blk[:, :], T.ee[:, i:i + 1], None, A.mult))
+    wait("v", H["row2"])
+    h2 = fin("v", V.tensor_tensor(T.blk2[:, :], T.blk[:, :], T.row2[:, :], A.mult))
+    H["fill"] = fin("v", V.memset(T.tc6[:, 0:PAD[6]], NONE))
+    wait("v", h2)
+    for i in range(16):
+        H["br2"] = fin("v", V.tensor_scalar(T.br2[:, 128 * i:128 * i + 128], T.blk2[:, :], T.ee[:, i:i + 1], None, A.mult))
+
+    def code(out, in_, *hs):
+        wait("s", *hs)
+        return fin("s", S.activation(out, in_, F.Exp, bias=-K * (16 + A0), scale=K))
+
+    def out_to_ranks(ap, sem, *hs):
+        wait("gc", *hs)
+        cnt["sent"] += send(g, T, topo, core, others, ap, sem)
+        H[sem] = (sem, len(others) * len(topo.engines(core, others[0])))
+
+    def own_tc(d):
+        return T["tc%d" % d][:, PAD[d] + 512 * R:PAD[d] + 512 * R + 512]
+
+    def pointers(d):
+        wait("v", H["ld_ti%d" % d])
+        h = fin("v", V.tensor_copy(T["cf%d" % d][:, :], T["ti%d" % d][:, :]))
+        H["e%d" % d] = code(own_tc(d), T["cf%d" % d][:, :], h)
+
+    def to_helper(d):
+        eng = spare_engines(core, helper, others[0], topo)
+        wait("gc", H["e%d" % d])
+        rid, pid, _ = topo.addr(helper)
+        g.remote_dma(own_tc(d), own_tc(d), T.sem["h%d" % d], T.sem["sent"], pid, rid, bits(eng))
+        cnt["sent"] += len(eng)
+        H["a_t%d" % d] = ("a_t%d" % d, len(others) * len(topo.engines(helper, others[0])))
+
+    out_to_ranks(T.raw[:, slot:slot + SLOT], "a_raw", H["ld_ti12"])
+    pointers(3)
+    out_to_ranks(own_tc(3), "a_t3", H["e3"])
+
+    last = {}
+
+    wait("v", H["ld_let"])
+    H["letb"] = fin("v", V.tensor_copy(T.letb[:, :], T.leti[:, :]))
+    wait("v", H["ld_par"])
+    H["pu"] = fin("v", V.tensor_copy(T.pu[:, :], T.pari[:, :]))
+    LB = ["pm0", "pm1", "px0", "px1", "pm0", "pm1"]
+
+    def let_pe(k):
+        b = LB[k]
+        wait("p", H["brd"], H["letb"], last.get(b))
+        for n, i in enumerate(range(3 * k, min(3 * k + 3, 16))):
+            H["letp%d" % k] = fin("p", P.matmul(T[b][:, 164 * n:164 * n + 164], T.brd[:, 128 * i:128 * i + 128], T.letb[:, :], True, True))
+
+    def let_mask(k):
+        b = LB[k]
+        n = 164 * (min(3 * k + 3, 16) - 3 * k)
+        wait("v", H["letp%d" % k], H["ccf"])
+        last[b] = H["ml%d" % k] = fin("v", V.tensor_scalar(T.maskl[:, 492 * k:492 * k + n], T[b][:, 0:n], T.ccf[:, 0:1], None, A.is_equal))
+
+    def let_seg(d):
+        lo, hi = OWN[d] - 4, OWN[d] - 4 + 512
+        return [H["ml%d" % k] for k in range(6) if 492 * k < hi and 492 * (k + 1) > lo]
+
+    tn = [0]
+
+    def masks_pe(lo, hi, t0, t1):
+        b = "pt%d" % (tn[0] % 2)
+        tn[0] += 1
+        n = 32 * (t1 - t0)
+        wait("p", H["br2"], H["brd"], H["vb"], H["vq"], last.get(b))
+        for m, i in enumerate(range(lo, hi)):
+            ap = T[b][:, m * n:m * n + n]
+            P.matmul(ap, T.br2[:, 128 * i:128 * i + 128], T.vb[:, 32 * t0:32 * t1], True, False).then_inc(T.sem["p"], 1)
+            cnt["p"] += 1
+            h = fin("p", P.matmul(ap, T.brd[:, 128 * i:128 * i + 128], T.vq[:, 32 * t0:32 * t1], False, True))
+        return (b, h, lo, hi, t0, n)
+
+    def masks_out(made):
+        b, h, lo, hi, t0, n = made
+        wait("s", h, H["bq"])
+        o = 512 * (t0 - 1)
+        for m, i in enumerate(range(lo, hi)):
+            last[b] = H["mt%d" % t0] = fin("s", S.activation(T.maskt[:, o + i:o + 16 * n:16], T[b][:, m * n:m * n + n], F.Relu,
+                                                             bias=T.bq[:, 0:1], scale=-1.0))
+
+    def text_masks(*which):
+        masks_out(masks_pe(*which))
+
+    let_pe(0)
+    let_pe(1)
+    let_pe(2)
+    let_pe(3)
+    pointers(4)
+    to_helper(4)
+    let_mask(0)
+    let_mask(1)
+    pointers(5)
+    to_helper(5)
+    pointers(6)
+    to_helper(6)
+
+    def sums(bank, x, hx):
+        wait("p", hx, H["sel"], last.get(bank))
+        for i in range(16):
+            h = fin("p", P.matmul(T[bank][:, 0:32], T.sel[:, 128 * i:128 * i + 128], T[x][:, i:512:16], i == 0, i == 15))
+        return h
+
+    def fail_cols(d):
+        if d == 6:
+            return T.tab[:, BASE[6] + 512 * R:BASE[6] + 512 * R + 512]
+        return T["d%d" % d][:, :]
+
+    def fail_gather(d):
+        q = OWN[d] - 4
+        wait("v", H["d%d" % (d - 1)], H["pu"], *let_seg(d))
+        h = fin("v", V.tensor_tensor(T["xf%d" % d][:, :], fail_cols(d - 1).indirect(T.pu[:, q // 16:q // 16 + 32]),
+                                     T.maskl[:, q:q + 512], A.mult))
+        H["xf%d" % d] = sums("pf%d" % (d % 2), "xf%d" % d, h)
+
+    def fail_ln(d):
+        j = (OWN[d] - 4) // 16
+        wait("s", H["xf%d" % d])
+        last["pf%d" % (d % 2)] = H["lnf%d" % d] = fin("s", S.activation(T.lnf[:, j:j + 32], T["pf%d" % (d % 2)][:, 0:32], F.Ln))
+
+    def own_list(d):
+        return T["fl%d" % d][:, 32 * R:32 * R + 32]
+
+    def fail_list(d):
+        j = (OWN[d] - 4) // 16
+        wait("v", H["lnf%d" % d])
+        H["fl%d" % d] = fin("v", V.tensor_scalar(own_list(d), T.lnf[:, j:j + 32], 1.0 / K, float(A0), A.mult, A.add))
+        if d < 7:
+            out_to_ranks(own_list(d), "a_f%d" % d, H["fl%d" % d])
+        else:
+            H["flp"] = fin("v", V.tensor_scalar(T.flp[:, :], T.lnf[:, j:j + 32], 1.0 / K, float(A0 - BASE[6] + PAD[6]), A.mult, A.add))
+
+    def text_gather(t):
+        d = min(t, 6)
+        wait("v", H["lt%d" % (t - 1)], H["mt1" if t < 4 else "mt4"], *H["tab%d" % d])
+        h = fin("v", V.tensor_tensor(T["xt%d" % t][:, :], T.tab[:, 0:BASE[d + 1]].indirect(T.lt[:, 32 * t - 32:32 * t]),
+                                     T.maskt[:, 512 * t - 512:512 * t], A.mult))
+        H["xt%d" % t] = sums("px%d" % (t % 2), "xt%d" % t, h)
+
+    def text_ln(t):
+        wait("s", H["xt%d" % t])
+        last["px%d" % (t % 2)] = H["lnt%d" % t] = fin("s", S.activation(T.lnt[:, 32 * t:32 * t + 32], T["px%d" % (t % 2)][:, 0:32], F.Ln))
+
+    def text_list(t):
+        c = slice(32 * t, 32 * t + 32)
+        wait("v", H["lnt%d" % t])
+        H["lt%d" % t] = fin("v", V.tensor_scalar(T.lt[:, c], T.lnt[:, c], 1.0 / K, float(A0), A.mult, A.add))
+
+    def deep_list(t):
+        c = slice(32 * t, 32 * t + 32)
+        wait("v", H["lnt%d" % t])
+        H["ltp%d" % t] = fin("v", V.tensor_scalar(T.ltp[:, c], T.lnt[:, c], 1.0 / K, float(A0 - BASE[6] + PAD[6]), A.mult, A.add))
+
+    DB = {6: "pt0", 7: "pt1", 8: "pf0", 9: "pf1"}
+
+    def deep_gather(t):
+        wait("v", H["ltp%d" % (t - 1)], H["a_t6"], H["e6"], H["fill"])
+        h = fin("v", V.tensor_tensor(T["xp%d" % t][:, :], T.tc6[:, :].indirect(T.ltp[:, 32 * t - 32:32 * t]),
+                                     T.maskt[:, 512 * t - 512:512 * t], A.mult))
+        H["xp%d" % t] = sums(DB[t], "xp%d" % t, h)
+
+    def deep_ln(t):
+        wait("s", H["xp%d" % t])
+        last[DB[t]] = H["lnp%d" % t] = fin("s", S.activation(T.lnp[:, 32 * t:32 * t + 32], T[DB[t]][:, 0:32], F.Ln))
+
+    def running(*names):
+        for buf, t in names:
+            ap = T[buf][:, 32 * t:32 * t + 32]
+            wait("v", H["%s%d" % (buf, t)], H.get("rm"))
+            if "rm" in H:
+                H["rm"] = fin("v", V.tensor_tensor(T.rm[:, :], T.rm[:, :], ap, A.max))
+            else:
+                H["rm"] = fin("v", V.tensor_copy(T.rm[:, :], ap))
+
+    def fail_columns(d):
+        wait("s", *H["tab%d" % (d - 1)])
+        wait("s", H["fl%d" % d])
+        off = T.fl2[:, 4 * R:4 * R + 4] if d == 2 else own_list(d)
+        out = T.d2[:, :] if d == 2 else fail_cols(d)
+        H["d%d" % d] = fin("s", S.activation(out, T.tab[:, 0:BASE[d]].indirect(off), F.Copy))
+
+    def complete(d, c0, c1):
+        if c0 < c1:
+            wait("v", *H["tab%d" % (d - 1)])
+            return [fin("v", V.tensor_tensor(T.tab[:, BASE[d] + 16 * c0:BASE[d] + 16 * c1],
+                                             T.tab[:, 0:BASE[d]].indirect(T["fl%d" % d][:, c0:c1]),
+                                             T["tc%d" % d][:, 16 * c0:16 * c1], A.max))]
+        return []
+
+    def complete_own(d):
+        wait("v", H["fl%d" % d], H["e%d" % d])
+        H["tab%d" % d] = complete(d, 32 * R, 32 * R + 32)
+        H["own%d" % d] = H["tab%d" % d][0]
+
+    def complete_others(d, part):
+        wait("v", H["a_f%d" % d], H["a_t%d" % d])
+        cuts = [(0, 16), (16, 32 * R), (32 * R + 32, 128)] if R else [(32, 48), (48, 128)]
+        for c in (cuts[:1] if part == 0 else cuts[1:]):
+            H["tab%d" % d] += complete(d, *c)
+
+    def plain(q, r):
+        off = T.fl6[:, 32 * r:32 * r + 32]
+        out = T.tab[:, BASE[6] + 512 * r:BASE[6] + 512 * r + 512]
+        src = T.tab[:, 0:BASE[6]].indirect(off)
+        wait(q, *H["tab5"])
+        wait(q, H["a_f6"])
+        if q == "s":
+            h = fin("s", S.activation(out, src, F.Copy))
+        else:
+            h = fin("v", V.tensor_copy(out, src))
+        H["tab6"].append(h)
+
+    def own_ap(d):
+        if d >= 6:
+            return T["g%d" % d][:, :]
+        return T.tab[:, BASE[d] + SIZE[d] * R:BASE[d] + SIZE[d] * R + SIZE[d]]
+
+    def yg_ln(d):
+        c = slice(OWN[d], OWN[d] + SIZE[d])
+        wait("s", H["own%d" % d])
+        H["ya%d" % d] = fin("s", S.activation(T.ya[:, c], own_ap(d), F.Ln))
+
+    def yg_cols(d):
+        return slice(0 if d == 2 else OWN[d], OWN[d] + SIZE[d])
+
+    def yg_round(d):
+        wait("s", H["ya%d" % d])
+        H["yb%d" % d] = fin("s", S.activation(T.yb[:, yg_cols(d)], T.ya[:, yg_cols(d)], F.Identity, bias=float(MAGIC + A0), scale=1.0 / K))
+
+    def yg_out(d):
+        wait("s", H["yb%d" % d])
+        h = fin("s", S.activation(T.yo[:, yg_cols(d)], T.yb[:, yg_cols(d)], F.Identity, bias=16.0 - MAGIC))
+        store(T.yg[:, yg_cols(d)], T.yo[:, yg_cols(d)], h)
+
+    def yf_numbers(d):
+        j = (OWN[d] - 4) // 16
+        wait("v", H["fl%d" % d])
+        H["nf%d" % d] = fin("v", V.tensor_scalar(T.nf[:, j:j + 32], own_list(d), 16.0, None, A.add))
+
+    def yf_turn(bank, j0, j1, hs):
+        wait("p", *hs)
+        wait("p", H["ident"], last.get(bank))
+        return fin("p", P.transpose(T[bank][0:j1 - j0, 0:128], T.nf[:, j0:j1], T.ident[:, :]))
+
+    def yf_out(bank, buf, j0, j1, h):
+        n = j1 - j0
+        wait("s", h)
+        h = fin("s", S.activation(T[buf][0:n, :], T[bank][0:n, 0:128], F.Copy))
+        for k in range(8):
+            store(T.yf[k:k + 1, 4 + 16 * j0:4 + 16 * j1], T[buf][0:n, 16 * k:16 * k + 16], h)
+
+    wait("v", H["a_raw"], H["ld_ti12"])
+    for r in range(4):
+        h = fin("v", V.tensor_copy(T.c1f[:, 4 * r:4 * r + 4], T.raw[:, SLOT * r:SLOT * r + 4]))
+    H["tab1"] = [code(T.tab[:, 0:16], T.c1f[:, :], h)]
+    for r in range(4):
+        H["fl2"] = fin("v", V.tensor_copy(T.fl2[:, 4 * r:4 * r + 4], T.raw[:, SLOT * r + 68:SLOT * r + 72]))
+    fail_columns(2)
+    for r in range(4):
+        h = fin("v", V.tensor_copy(T.c2f[:, 64 * r:64 * r + 64], T.raw[:, SLOT * r + 4:SLOT * r + 68]))
+    H["c2"] = code(T.c2[:, :], T.c2f[:, :], h)
+    H["own1"] = H["tab1"][0]
+    yg_ln(1)
+    fail_gather(3)
+    wait("v", H["ld_txt"])
+    H["vb"] = fin("v", V.tensor_copy(T.vb[:, :], T.vi[:, :]))
+    wait("s", H["vb"])
+    H["vq"] = fin("s", S.activation(T.vq[:, :], T.vb[:, :], F.Square))
+    wait("v", H["c2"], *H["tab1"])
+    H["own2"] = fin("v", V.tensor_tensor(T.tab[:, 16:272], T.tab[:, 0:16].indirect(T.fl2[:, :]), T.c2[:, :], A.max))
+    H["tab2"] = [H["own2"]]
+    H["lt0"] = fin("v", V.tensor_copy(T.lt[:, 0:32], T.vi[:, 0:32]))
+    fail_ln(3)
+    fail_list(3)
+    fail_columns(3)
+    text_masks(0, 5, 1, 4)
+    text_masks(5, 10, 1, 4)
+    text_masks(10, 15, 1, 4)
+    text_masks(15, 16, 1, 4)
+    complete_own(3)
+    let_mask(2)
+    fail_gather(4)
+    let_mask(3)
+    let_pe(4)
+    let_pe(5)
+    m0 = masks_pe(0, 2, 4, 10)
+    m1 = masks_pe(2, 4, 4, 10)
+    complete_others(3, 0)
+    text_gather(1)
+    fail_ln(4)
+    fail_list(4)
+    masks_out(m0)
+    masks_out(m1)
+    text_ln(1)
+    complete_others(3, 1)
+    text_list(1)
+    fail_columns(4)
+    text_masks(4, 6, 4, 10)
+    text_masks(6, 8, 4, 10)
+    text_gather(2)
+    let_mask(4)
+    fail_gather(5)
+    text_ln(2)
+    text_masks(8, 10, 4, 10)
+    m0 = masks_pe(10, 12, 4, 10)
+    m1 = masks_pe(12, 14, 4, 10)
+    complete_own(4)
+    let_mask(5)
+    complete_others(4, 0)
+    text_list(2)
+    text_gather(3)
+    fail_ln(5)
+    masks_out(m0)
+    fail_list(5)
+    masks_out(m1)
+    text_ln(3)
+    text_masks(14, 16, 4, 10)
+    complete_others(4, 1)
+    text_list(3)
+    H["nf2"] = fin("v", V.tensor_scalar(T.nf[:, 0:4], T.raw[:, slot + 68:slot + 72], 16.0, None, A.add))
+    yf_numbers(3)
+    fail_columns(5)
+    text_gather(4)
+    H["zz"] = fin("v", V.memset(T.zz[0:8, :], 0.0))
+    store(T.yf[:, 0:4], T.zz[0:8, :], H["zz"])
+    fail_gather(6)
+    complete_own(5)
+    running(("lnt", 1))
+    text_ln(4)
+    text_list(4)
+    running(("lnt", 2))
+    complete_others(5, 0)
+    yf_numbers(4)
+    running(("lnt", 3))
+    fail_ln(6)
+    fail_list(6)
+    running(("lnt", 4))
+    yf_numbers(5)
+    complete_others(5, 1)
+    yg_ln(2)
+    yg_round(2)
+    yg_out(2)
+    yg_ln(3)
+    yg_round(3)
+    H["onesf"] = fin("v", V.memset(T.onesf[:, :], 1.0))
+    wait("gc", H["onesf"])
+    H["ident"] = fin("gc", g.affine_select(T.ident[:, :], T.onesf[:, :], [[-1, 128]], A.is_equal, 0.0, 0, 1))
+    h = yf_turn("pm0", 0, 100, [H["nf%d" % d] for d in (2, 3, 4, 5)])
+    fail_columns(6)
+    H["tab6"] = [H["d6"]]
+    rest = [r for r in range(4) if r != R]
+    text_gather(5)
+    fail_gather(7)
+    plain("s", rest[0])
+    plain("v", rest[2])
+    text_ln(5)
+    text_list(5)
+    plain("s", rest[1])
+    fail_ln(7)
+    deep_list(5)
+    text_gather(6)
+    fail_list(7)
+    deep_gather(6)
+    yf_out("pm0", "tr1", 0, 100, h)
+    wait("s", *H["tab6"])
+    wait("s", H["fl7"])
+    text_ln(6)
+    yf_numbers(6)
+    yf_numbers(7)
+    running(("lnt", 5))
+    H["h7"] = fin("s", S.activation(T.h7[:, :], T.tab[:, :].indirect(own_list(7)), F.Copy))
+    text_list(6)
+    text_gather(7)
+    wait("v", H["fl6"], H["e6"], *H["tab5"])
+    H["own6"] = fin("v", V.tensor_tensor(T.g6[:, :], T.tab[:, 0:BASE[6]].indirect(own_list(6)), own_tc(6), A.max))
+    deep_list(6)
+    running(("lnt", 6))
+    yg_out(3)
+    deep_ln(6)
+    text_ln(7)
+    h7 = yf_turn("pm1", 100, 164, [H["nf6"], H["nf7"]])
+    yg_ln(6)
+    yg_round(6)
+    yg_out(6)
+    running(("lnp", 6))
+    text_list(7)
+    text_gather(8)
+    wait("v", H["h7"], H["flp"], H["a_t6"], H["fill"])
+    H["own7"] = fin("v", V.tensor_tensor(T.g7[:, :], T.tc6[:, :].indirect(T.flp[:, :]), T.h7[:, :], A.max))
+    deep_list(7)
+    running(("lnt", 7))
+    text_ln(8)
+    yf_out("pm1", "tr2", 100, 164, h7)
+    yg_ln(4)
+    yg_round(4)
+    yg_out(4)
+    text_list(8)
+    text_gather(9)
+    deep_list(8)
+    deep_gather(9)
+    deep_gather(7)
+    running(("lnt", 8))
+    deep_gather(8)
+    text_ln(9)
+    yg_ln(7)
+    yg_round(7)
+    deep_ln(9)
+    yg_out(7)
+    deep_ln(7)
+    running(("lnp", 7))
+    deep_ln(8)
+    yg_ln(5)
+    yg_round(5)
+    yg_out(5)
+    running(("lnp", 8))
+    wait("v", H["lnt9"], H["lnp9"])
+    h = fin("v", V.tensor_tensor(T.last[:, 0:32], T.lnt[:, 288:320], T.lnp[:, 288:320], A.max))
+    wait("v", h, H["rm"])
+    h = fin("v", V.tensor_tensor(T.last[:, 32:64], T.rm[:, :], T.last[:, 0:32], A.max))
+    wait("v", h)
+    h = fin("v", V.tensor_scalar(T.lastm[:, :], T.last[:, :], 1.0 / K, float(MAGIC + A0), A.mult, A.add))
+    wait("v", h)
+    h = fin("v", V.tensor_scalar(T.oy[:, :], T.lastm[:, :], 16.0 - MAGIC, None, A.add))
+    store(T.yl[:, :], T.oy[:, 0:32], h)
+    store(T.ym[:, :], T.oy[:, 32:64], h)
+    wait("gc", ("v", cnt["v"]), ("s", cnt["s"]), ("p", cnt["p"]), ("gc", cnt["gc"]), ("out", cnt["out"]), ("sent", cnt["sent"]))

@@ -2,58 +2,74 @@ from concourse.bass import DstId, RemoteDMATransfer
 from concourse.mybir import AluOpType as A, ActivationFunctionType as F
 
 K = 0.008435
-A0 = 5256
-NONE = 6e-20
+A0 = 5248
+FIRST = 32
 MAGIC = 12582912
+TINY = 1e-25
 SIZE = {1: 4, 2: 64, 3: 512, 4: 512, 5: 512, 6: 512, 7: 512}
 OWN = {1: 0, 2: 4, 3: 68, 4: 580, 5: 1092, 6: 1604, 7: 2116}
-BASE = {1: 0, 2: 16, 3: 272, 4: 2320, 5: 4368, 6: 6416, 7: 8464}
+BASE = {2: 0, 3: 256, 4: 2304, 5: 4352, 6: 6400, 7: 8448}
 SLOT = 72
+WSLOT = 40
 PAD = {3: 0, 4: 0, 5: 0, 6: 16}
+BLOCK = {"t1": 0, "t2": 1, "t3": 2, "t4": 3, "t5": 4, "t6": 5, "t7": 6, "t8": 7, "p6": 8, "p7": 9, "p8": 10, "t9": 11, "p9": 12}
+ORDER = """
+maskc first float.3 code.3 send3 words weights letters.l squares.l wordlist wordsout wordc
+float.4 code.4 helper.4 pe.l4 pe.l5 letters.t mask.l4 own_pe.3 float.5 squares.t code.5 helper.5 pe.t2 float.6 mask.l5 pe.t3
+code.6 helper.6 twords yf12 mask.t2 pe.l6
+g2w D.3 y1 mask.t3.v pe.t4 fail.4 yg.1.0 own.3 own_pe.4 text.2 fln.4 flist.4 text1 sums.t1.t2 mask.l6.v pe.l7 level2.3 level2.0 level2.1
+level2.2 other.3.0 ln.t1 fail3 rows.3 rows.4 other.3.1 tlist.2 other.3.2 mask.t4 pe.t5
+D.4 text.3 sums.t3 fail.5 mask.l7 pe.t6 ln.t3 own.4 own_pe.5 fln.5 flist.5 tlist.3 mask.t5 pe.t7 mask.t6 pe.t8 rows.5
+yg.2.0 yg.3.0 other.4.0 other.4.1 other.4.2 mask.t7 pe.t9
+D.5 text.4 sums.t4 fail.6 mask.t8 ln.t4 own.5 own_pe.6 fln.6 flist.6 tlist.4 rows.6 mask.t9 yg.3.1 yg.3.2 yg.4.0
+other.5.0 other.5.1 other.5.2
+D.6 text.5 sums.t5 plain.s.0 fail.7 ln.t5 plain.s.1 plain.v.2 tlist.5 text.6 sums.t6 fln.7 dlist.5 flist.7 rows.7 own.6
+yg.4.1 ln.t6 tlist.6 text.7 sums.t7 h7 deep.6 dlist.6 yg.4.2 ln.t7 tlist.7 text.8 sums.t8 yg.5.0 yg.5.1 g7 dlist.7 ln.t8 tlist.8 dlist.8
+deep.7 sums.p6.p7 deep.8 sums.p8 yg.5.2 yg.6.0 text.9 deep.9 sums.t9.p9 ln.p6 ln.p8 max.1 max.2 max.3 max.4 max.5 yg.7.0 ln.t9 out
+yg.7.1 yg.7.2 yg.6.1.v yf.0 yg.6.2.v yf.1 yf.2
+"""
+
+
+def _sb(cols, dtype):
+    return ("sbuf", [128, cols], dtype)
+
 
 SCRATCH = {
-    "tab": ("sbuf", [128, 8464], "bfloat16"), "raw": ("sbuf", [128, 4 * SLOT], "int32"),
-    "c1f": ("sbuf", [128, 16], "float32"), "c2f": ("sbuf", [128, 256], "float32"), "c2": ("sbuf", [128, 256], "bfloat16"),
-    "leti": ("sbuf", [128, 164], "int32"), "letb": ("sbuf", [128, 164], "bfloat16"), "maskl": ("sbuf", [128, 2624], "bfloat16"),
-    "pari": ("sbuf", [128, 164], "int32"), "pu": ("sbuf", [128, 164], "uint16"),
-    "vi": ("sbuf", [128, 320], "int32"), "vb": ("sbuf", [128, 320], "bfloat16"),
-    "vq": ("sbuf", [128, 320], "bfloat16"), "maskt": ("sbuf", [128, 4608], "bfloat16"),
-    "fl2": ("sbuf", [128, 16], "uint16"), "d2": ("sbuf", [128, 64], "bfloat16"),
-    "lt": ("sbuf", [128, 320], "uint16"), "ltp": ("sbuf", [128, 320], "uint16"), "flp": ("sbuf", [128, 32], "uint16"),
-    "lnf": ("sbuf", [128, 164], "float32"), "lnt": ("sbuf", [128, 320], "float32"), "lnp": ("sbuf", [128, 320], "float32"),
-    "rm": ("sbuf", [128, 32], "float32"), "last": ("sbuf", [128, 64], "float32"), "lastm": ("sbuf", [128, 64], "float32"),
-    "oy": ("sbuf", [128, 64], "float32"),
-    "nf": ("sbuf", [128, 164], "float32"), "tr1": ("sbuf", [128, 128], "float32"), "tr2": ("sbuf", [128, 128], "float32"),
-    "zz": ("sbuf", [128, 4], "float32"), "g6": ("sbuf", [128, 512], "bfloat16"),
-    "h7": ("sbuf", [128, 512], "bfloat16"), "g7": ("sbuf", [128, 512], "bfloat16"),
-    "ya": ("sbuf", [128, 2628], "float32"), "yb": ("sbuf", [128, 2628], "float32"), "yo": ("sbuf", [128, 2628], "float32"),
-    "ones": ("sbuf", [128, 128], "bfloat16"), "blk0": ("sbuf", [128, 128], "bfloat16"), "blk": ("sbuf", [128, 128], "bfloat16"),
-    "blk2": ("sbuf", [128, 128], "bfloat16"), "row2": ("sbuf", [128, 128], "bfloat16"),
-    "onesf": ("sbuf", [128, 128], "float32"), "ident": ("sbuf", [128, 128], "float32"),
-    "pcol": ("sbuf", [128, 1], "int32"), "cci": ("sbuf", [128, 1], "int32"), "ccf": ("sbuf", [128, 1], "float32"),
-    "cc2": ("sbuf", [128, 1], "float32"), "bq": ("sbuf", [128, 1], "float32"),
-    "row16": ("sbuf", [128, 16], "float32"), "ee": ("sbuf", [128, 16], "float32"),
-    "brd": ("sbuf", [128, 2048], "bfloat16"), "br2": ("sbuf", [128, 2048], "bfloat16"), "sel": ("sbuf", [128, 2048], "bfloat16"),
+    "tab": _sb(8448, "bfloat16"), "msg": _sb(4 * SLOT, "bfloat16"), "g2w": _sb(256, "bfloat16"), "y1": _sb(256, "bfloat16"),
+    "ti12": _sb(68, "int32"), "cf12": _sb(68, "float32"), "l1": _sb(4, "uint16"), "l2": _sb(4, "uint16"),
+    "lr": _sb(576, "int32"), "w1": _sb(16, "bfloat16"), "w2": _sb(64, "bfloat16"), "xw": _sb(576, "bfloat16"),
+    "wl": _sb(4 * WSLOT, "uint16"), "pari": _sb(164, "int32"), "pu": _sb(164, "uint16"),
+    "li": _sb(768, "int32"), "lb": _sb(768, "bfloat16"), "lq": _sb(768, "bfloat16"),
+    "maskl": _sb(2048, "bfloat16"), "maskt": _sb(4096, "bfloat16"),
+    "vi": _sb(64, "int32"), "vf": _sb(64, "float32"),
+    "lt": _sb(320, "uint16"), "ltp": _sb(320, "uint16"), "flp": _sb(32, "uint16"),
+    "xt": _sb(13 * 512, "bfloat16"), "ln": _sb(13 * 32, "float32"), "lnf": _sb(128, "float32"),
+    "rm": _sb(256, "float32"), "last": _sb(64, "float32"), "lastm": _sb(64, "float32"), "oy": _sb(64, "float32"),
+    "zz": _sb(16, "float32"), "yf12": _sb(68, "float32"), "fa": _sb(512, "float32"), "fb": _sb(512, "float32"), "fo": _sb(512, "float32"),
+    "g6": _sb(512, "bfloat16"), "h7": _sb(512, "bfloat16"), "g7": _sb(512, "bfloat16"),
+    "ya": _sb(2628, "float32"), "yb": _sb(2628, "float32"), "yo": _sb(2628, "float32"),
+    "pi": _sb(8, "int32"), "pf": _sb(8, "float32"), "pd": _sb(8, "float32"),
+    "rown": _sb(144, "bfloat16"), "rowc": _sb(256, "bfloat16"), "colg": _sb(128, "bfloat16"), "cl2i": _sb(16, "int32"),
+    "cl0": _sb(4, "uint16"), "cl1": _sb(2, "uint16"), "c1": _sb(32, "bfloat16"), "cl2": _sb(16, "uint16"), "zs": _sb(144, "bfloat16"), "ident": _sb(128, "bfloat16"),
+    "eet": _sb(256, "bfloat16"), "e2": _sb(8, "float32"), "blk": _sb(128, "bfloat16"), "b0": _sb(128, "bfloat16"),
+    "b1": _sb(128, "bfloat16"), "wr": _sb(1024, "bfloat16"),
 }
 for _d in range(3, 7):
-    SCRATCH["ti%d" % _d] = ("sbuf", [128, 512], "int32")
-    SCRATCH["cf%d" % _d] = ("sbuf", [128, 512], "float32")
-    SCRATCH["tc%d" % _d] = ("sbuf", [128, PAD[_d] + 2048], "bfloat16")
+    SCRATCH["ti%d" % _d] = _sb(512, "int32")
+    SCRATCH["cf%d" % _d] = _sb(512, "float32")
+    SCRATCH["tc%d" % _d] = _sb(PAD[_d] + 2048, "bfloat16")
 for _d in range(3, 6):
-    SCRATCH["d%d" % _d] = ("sbuf", [128, 512], "bfloat16")
+    SCRATCH["d%d" % _d] = _sb(512, "bfloat16")
 for _d in range(3, 8):
-    SCRATCH["fl%d" % _d] = ("sbuf", [128, 128], "uint16")
-    SCRATCH["xf%d" % _d] = ("sbuf", [128, 512], "bfloat16")
-for _t in range(1, 10):
-    SCRATCH["xt%d" % _t] = ("sbuf", [128, 512], "bfloat16")
-for _t in range(6, 10):
-    SCRATCH["xp%d" % _t] = ("sbuf", [128, 512], "bfloat16")
-for _b in ("pm0", "pm1", "pt0", "pt1", "pf0", "pf1", "px0", "px1"):
+    SCRATCH["xf%d" % _d] = _sb(512, "bfloat16")
+for _d in range(4, 8):
+    SCRATCH["fl%d" % _d] = _sb(128, "uint16")
+for _b in ("pm0", "pm1", "po", "pa", "px0", "px1", "py", "pw"):
     SCRATCH[_b] = ("psum", [128, 512], "float32")
 
-LOADS = ["ti12", "let", "ti3", "par", "txt", "ti4", "ti5", "ti6"]
-SEMAPHORES = (["v", "s", "p", "gc", "out", "sent", "a_raw"] + ["ld_" + n for n in LOADS]
-              + ["a_t%d" % d for d in range(3, 7)] + ["a_f%d" % d for d in range(3, 7)] + ["h%d" % d for d in range(4, 7)])
+LOADS = ["ti12", "ti3", "par", "lr", "ti4", "ti5", "ti6", "ll", "lt", "vi"]
+SEMAPHORES = (["v", "s", "p", "gc", "out", "sent", "a_msg", "a_wl"] + ["ld_" + n for n in LOADS]
+              + ["a_t%d" % d for d in range(3, 7)] + ["a_f%d" % d for d in range(4, 7)] + ["h%d" % d for d in range(4, 7)])
 
 
 def helper_of(core, ranks, topo):
@@ -107,16 +123,20 @@ def rank_program(g, core, T, topo):
         return
     R = rank
     others = [c for c in T.cores if c != core]
+    rest = [r for r in range(4) if r != R]
     helper = helper_of(core, T.cores, topo)
-    queue = {"v": g.vector, "s": g.scalar, "p": g.tensor, "gc": g, "y": g.sync}
+    V, S, P = g.vector, g.scalar, g.tensor
+    queue = {"v": V, "s": S, "p": P, "gc": g, "y": g.sync}
     cnt = {"v": 0, "s": 0, "p": 0, "gc": 0, "out": 0, "sent": 0}
     seen = {}
+    H = {}
+    last = {}
 
     def wait(q, *hs):
         for h in hs:
             if h is None:
                 continue
-            sem, val = h
+            sem, val = H[h] if isinstance(h, str) else h
             if seen.get((q, sem), 0) < val:
                 queue[q].wait_ge(T.sem[sem], val)
                 seen[(q, sem)] = val
@@ -126,62 +146,94 @@ def rank_program(g, core, T, topo):
         ins.then_inc(T.sem[q], 1)
         return (q, cnt[q])
 
-    V, S, P = g.vector, g.scalar, g.tensor
-    H = {}
+    def ts(out, in_, s1, s2, op0, op1, *hs):
+        wait("v", *hs)
+        return fin("v", V.tensor_scalar(out, in_, s1, None, op0) if op1 is None else V.tensor_scalar(out, in_, s1, s2, op0, op1))
 
-    def load(name, pairs):
+    def tt(out, a, b, op, *hs):
+        wait("v", *hs)
+        return fin("v", V.tensor_tensor(out, a, b, op))
+
+    def copy(out, in_, *hs):
+        wait("v", *hs)
+        return fin("v", V.tensor_copy(out, in_))
+
+    def act(out, in_, func, hs, **kw):
+        wait("s", *hs)
+        return fin("s", S.activation(out, in_, func, **kw))
+
+    def load(q, name, pairs):
         for out, in_ in pairs:
-            g.sync.dma_start(out, in_).then_inc(T.sem["ld_" + name], 16)
+            queue[q].dma_start(out, in_).then_inc(T.sem["ld_" + name], 16)
         H["ld_" + name] = ("ld_" + name, 16 * len(pairs))
-
-    slot = SLOT * R
-    load("ti12", [(T.raw[:, slot:slot + 68], T.tri[:, 0:68])]
-         + [(T.raw[:, slot + 68 + j:slot + 69 + j], T.let[:, 16 * j:16 * j + 16]) for j in range(4)])
-    load("ti3", [(T.ti3[:, :], T.tri[:, OWN[3]:OWN[4]])])
-    load("let", [(T.leti[:, :], T.let[:, :])])
-    load("par", [(T.pari[:, :], T.par[:, :])])
-    for d in range(4, 7):
-        load("ti%d" % d, [(T["ti%d" % d][:, :], T.tri[:, OWN[d]:OWN[d + 1]])])
-    load("txt", [(T.vi[:, 32 * t:32 * t + 32], T.txt[:, 512 * t:512 * t + 512]) for t in range(10)])
 
     def store(out, in_, *hs):
         wait("y", *hs)
         g.sync.dma_start(out, in_).then_inc(T.sem["out"], 16)
         cnt["out"] += 16
 
-    H["ones"] = fin("v", V.memset(T.ones[:, :], 1.0))
-    H["pcol"] = fin("gc", g.iota(T.pcol[:, :], [[0, 1]], 0, 1))
-    H["row16"] = fin("gc", g.iota(T.row16[:, :], [[1, 16]], 0, 0, allow_small_or_imprecise_dtypes=True))
-    wait("gc", H["ones"])
-    H["blk0"] = fin("gc", g.affine_select(T.blk0[:, :], T.ones[:, :], [[-16, 8], [0, 16]], A.is_ge, 0.0, 0, 1))
-    wait("gc", H["blk0"])
-    H["blk"] = fin("gc", g.affine_select(T.blk[:, :], T.blk0[:, :], [[16, 8], [0, 16]], A.is_ge, 0.0, 15, -1))
-    H["row2"] = fin("gc", g.iota(T.row2[:, :], [[0, 8], [-2, 16]], 0, 0, allow_small_or_imprecise_dtypes=True))
-    H["sel0"] = fin("v", V.memset(T.sel[:, :], 0.0))
-    wait("v", H["pcol"])
-    h = fin("v", V.tensor_scalar(T.cci[:, :], T.pcol[:, :], 15, None, A.bitwise_and))
-    wait("v", h)
-    H["ccf"] = fin("v", V.tensor_copy(T.ccf[:, :], T.cci[:, :]))
-    wait("v", H["ccf"], H["row16"])
-    H["ee"] = fin("v", V.tensor_scalar(T.ee[:, :], T.row16[:, :], T.ccf[:, 0:1], None, A.is_equal))
-    h = fin("v", V.tensor_tensor(T.cc2[:, :], T.ccf[:, :], T.ccf[:, :], A.mult))
-    wait("v", h, H["ee"], H["blk"])
-    H["bq"] = fin("v", V.tensor_scalar(T.bq[:, :], T.cc2[:, :], -1.0, 1.0, A.mult, A.add))
-    wait("s", H["sel0"], H["blk"])
-    for i in range(16):
-        H["sel"] = fin("s", S.activation(T.sel[:, 129 * i:128 * (i + 1):16], T.blk[:, i:128:16], F.Copy))
-    for i in range(16):
-        H["brd"] = fin("v", V.tensor_scalar(T.brd[:, 128 * i:128 * i + 128], T.blk[:, :], T.ee[:, i:i + 1], None, A.mult))
-    wait("v", H["row2"])
-    h2 = fin("v", V.tensor_tensor(T.blk2[:, :], T.blk[:, :], T.row2[:, :], A.mult))
-    H["fill"] = fin("v", V.memset(T.tc6[:, 0:PAD[6]], NONE))
-    wait("v", h2)
-    for i in range(16):
-        H["br2"] = fin("v", V.tensor_scalar(T.br2[:, 128 * i:128 * i + 128], T.blk2[:, :], T.ee[:, i:i + 1], None, A.mult))
+    H["zz"] = fin("v", V.memset(T.zz[:, :], 0.0))
+    H["lr0"] = fin("v", V.memset(T.lr[:, :], 0))
+    load("y", "ti12", [(T.ti12[:, :], T.tri[:, 0:68])])
+    load("y", "ti3", [(T.ti3[:, :], T.tri[:, OWN[3]:OWN[4]])])
+    load("y", "par", [(T.pari[:, :], T.par[:, :])])
+    wait("y", "lr0")
+    load("y", "lr", [(T.lr[0:128:16, :], T.let[:, 0:576])])
+    load("y", "ll", [(T.li[k:128:2, 512:768], T.let[:, 576:2624]) for k in range(2)])
+    load("y", "ti4", [(T.ti4[:, :], T.tri[:, OWN[4]:OWN[5]])])
+    load("y", "lt", [(T.li[k:128:2, 0:512], T.txt[:, 1024:5120]) for k in range(2)])
+    for d in (5, 6):
+        load("y", "ti%d" % d, [(T["ti%d" % d][:, :], T.tri[:, OWN[d]:OWN[d + 1]])])
+    load("y", "vi", [(T.vi[:, 32 * t:32 * t + 32], T.txt[:, 512 * t:512 * t + 512]) for t in range(2)])
 
     def code(out, in_, *hs):
-        wait("s", *hs)
-        return fin("s", S.activation(out, in_, F.Exp, bias=-K * (16 + A0), scale=K))
+        return act(out, in_, F.Exp, hs, bias=-K * (FIRST + A0), scale=K)
+
+    H["fill"] = code(T.tc6[:, 0:PAD[6]], T.zz[:, :], "zz")
+
+    flag = {"allow_small_or_imprecise_dtypes": True}
+    H["pcol"] = fin("gc", g.iota(T.pi[:, 0:1], [[0, 1]], 0, 1))
+    H["rown"] = fin("gc", g.iota(T.rown[:, :], [[1, 144]], 0, 0, **flag))
+    H["rowc"] = fin("gc", g.iota(T.rowc[:, :], [[0, 16], [1, 16]], 0, 0, **flag))
+    H["cl2i"] = fin("gc", g.iota(T.cl2i[:, :], [[SLOT, 4], [1, 4]], 0, 0))
+    H["w1"] = fin("gc", g.iota(T.w1[:, :], [[1, 16]], 4 * R, 0, **flag))
+    p0 = T.pi[:, 0:1]
+    ts(T.pi[:, 1:2], p0, 15, None, A.bitwise_and, None, "pcol")
+    ts(T.pi[:, 2:3], p0, 4, None, A.logical_shift_right, None)
+    ts(T.pi[:, 3:4], p0, 15, 1, A.bitwise_and, A.logical_shift_right)
+    ts(T.pi[:, 4:5], p0, 1, None, A.bitwise_and, None)
+    h = ts(T.pi[:, 5:6], p0, 15, 2, A.bitwise_and, A.logical_shift_right)
+    H["pf"] = copy(T.pf[:, 0:6], T.pi[:, 0:6], h)
+    pp, cc, pg, half, odd, quad = [T.pf[:, k:k + 1] for k in range(6)]
+    h = ts(T.pd[:, 3:4], odd, 2.0, -1.0, A.mult, A.add, "pf")
+    h0 = ts(T.pd[:, 0:1], pg, 16.0, 15.0, A.mult, A.add)
+    h = ts(T.b0[:, :], T.rowc[:, 0:128], T.pd[:, 3:4], odd, A.mult, A.add, h, "rowc")
+    H["e2"] = ts(T.e2[:, :], T.rowc[:, 0:8], half, None, A.is_equal, None)
+    wait("gc", h)
+    h = fin("gc", g.affine_select(T.blk[:, :], T.b0[:, :], [[-16, 8], [0, 16]], A.is_ge, 0.0, 0, 1))
+    wait("gc", h)
+    H["b1"] = fin("gc", g.affine_select(T.b1[:, :], T.blk[:, :], [[16, 8], [0, 16]], A.is_ge, 0.0, 15, -1))
+    H["zs"] = ts(T.zs[:, :], T.rown[:, :], T.pd[:, 0:1], None, A.is_equal, None, h0, "rown")
+
+    def mask_constants():
+        H["even"] = ts(T.pd[:, 4:5], odd, -1.0, 1.0, A.mult, A.add)
+        H["cq"] = ts(T.pd[:, 5:6], cc, 1.0, cc, A.add, A.mult)
+        H["h1"] = ts(T.pd[:, 1:2], quad, float(SLOT - 4), cc, A.mult, A.add)
+        H["bq"] = ts(T.pd[:, 6:7], T.pd[:, 5:6], -1.0, 1.0, A.mult, A.add, "cq")
+
+    def word_constants():
+        ts(T.cl0[:, :], T.zz[:, 0:4], cc, None, A.add, None, "zz")
+        H["cl1"] = ts(T.cl1[:, :], T.zz[:, 0:2], T.pd[:, 1:2], None, A.add, None, "h1")
+        H["cl2"] = copy(T.cl2[:, :], T.cl2i[:, :], "cl2i")
+        H["eet"] = ts(T.eet[:, :], T.rowc[:, :], cc, None, A.is_equal, None, "rowc")
+        H["ident"] = ts(T.ident[:, :], T.rown[:, 0:128], pp, None, A.is_equal, None, "rown")
+
+    def mask_weights():
+        for r in range(8):
+            H["wr"] = act(T.wr[:, 128 * r:128 * r + 128], T.b1[:, :], F.Copy, ["b1", "e2"], scale=T.e2[:, r:r + 1])
+
+    def sel(i):
+        return T.zs[:, 15 - i:143 - i]
 
     def out_to_ranks(ap, sem, *hs):
         wait("gc", *hs)
@@ -191,411 +243,294 @@ def rank_program(g, core, T, topo):
     def own_tc(d):
         return T["tc%d" % d][:, PAD[d] + 512 * R:PAD[d] + 512 * R + 512]
 
-    def pointers(d):
-        wait("v", H["ld_ti%d" % d])
-        h = fin("v", V.tensor_copy(T["cf%d" % d][:, :], T["ti%d" % d][:, :]))
-        H["e%d" % d] = code(own_tc(d), T["cf%d" % d][:, :], h)
+    def to_float(d):
+        H["cf%d" % d] = copy(T["cf%d" % d][:, :], T["ti%d" % d][:, :], "ld_ti%d" % d)
+
+    def to_code(d):
+        H["e%d" % d] = code(own_tc(d), T["cf%d" % d][:, :], "cf%d" % d)
 
     def to_helper(d):
         eng = spare_engines(core, helper, others[0], topo)
-        wait("gc", H["e%d" % d])
+        wait("gc", "e%d" % d)
         rid, pid, _ = topo.addr(helper)
         g.remote_dma(own_tc(d), own_tc(d), T.sem["h%d" % d], T.sem["sent"], pid, rid, bits(eng))
         cnt["sent"] += len(eng)
         H["a_t%d" % d] = ("a_t%d" % d, len(others) * len(topo.engines(helper, others[0])))
 
-    out_to_ranks(T.raw[:, slot:slot + SLOT], "a_raw", H["ld_ti12"])
-    pointers(3)
-    out_to_ranks(own_tc(3), "a_t3", H["e3"])
+    def first_message():
+        slot = SLOT * R
+        h1 = ts(T.l1[:, :], T.ti12[:, 0:4], float(4 - FIRST - 64 * R), None, A.add, None, "ld_ti12")
+        H["cf12"] = copy(T.cf12[:, :], T.ti12[:, :])
+        code(T.msg[:, slot + 64:slot + 72], T.cf12[:, 0:8], "cf12")
+        H["e12"] = code(T.msg[:, slot:slot + 64], T.cf12[:, :].indirect(T.l1[:, :]), h1)
+        out_to_ranks(T.msg[:, slot:slot + SLOT], "a_msg", "e12")
 
-    last = {}
-
-    wait("v", H["ld_let"])
-    H["letb"] = fin("v", V.tensor_copy(T.letb[:, :], T.leti[:, :]))
-    wait("v", H["ld_par"])
-    H["pu"] = fin("v", V.tensor_copy(T.pu[:, :], T.pari[:, :]))
-    LB = ["pm0", "pm1", "px0", "px1", "pm0", "pm1"]
-
-    def let_pe(k):
-        b = LB[k]
-        wait("p", H["brd"], H["letb"], last.get(b))
-        for n, i in enumerate(range(3 * k, min(3 * k + 3, 16))):
-            H["letp%d" % k] = fin("p", P.matmul(T[b][:, 164 * n:164 * n + 164], T.brd[:, 128 * i:128 * i + 128], T.letb[:, :], True, True))
-
-    def let_mask(k):
-        b = LB[k]
-        n = 164 * (min(3 * k + 3, 16) - 3 * k)
-        wait("v", H["letp%d" % k], H["ccf"])
-        last[b] = H["ml%d" % k] = fin("v", V.tensor_scalar(T.maskl[:, 492 * k:492 * k + n], T[b][:, 0:n], T.ccf[:, 0:1], None, A.is_equal))
-
-    def let_seg(d):
-        lo, hi = OWN[d] - 4, OWN[d] - 4 + 512
-        return [H["ml%d" % k] for k in range(6) if 492 * k < hi and 492 * (k + 1) > lo]
-
-    tn = [0]
-
-    def masks_pe(lo, hi, t0, t1):
-        b = "pt%d" % (tn[0] % 2)
-        tn[0] += 1
-        n = 32 * (t1 - t0)
-        wait("p", H["br2"], H["brd"], H["vb"], H["vq"], last.get(b))
-        for m, i in enumerate(range(lo, hi)):
-            ap = T[b][:, m * n:m * n + n]
-            P.matmul(ap, T.br2[:, 128 * i:128 * i + 128], T.vb[:, 32 * t0:32 * t1], True, False).then_inc(T.sem["p"], 1)
-            cnt["p"] += 1
-            h = fin("p", P.matmul(ap, T.brd[:, 128 * i:128 * i + 128], T.vq[:, 32 * t0:32 * t1], False, True))
-        return (b, h, lo, hi, t0, n)
-
-    def masks_out(made):
-        b, h, lo, hi, t0, n = made
-        wait("s", h, H["bq"])
-        o = 512 * (t0 - 1)
-        for m, i in enumerate(range(lo, hi)):
-            last[b] = H["mt%d" % t0] = fin("s", S.activation(T.maskt[:, o + i:o + 16 * n:16], T[b][:, m * n:m * n + n], F.Relu,
-                                                             bias=T.bq[:, 0:1], scale=-1.0))
-
-    def text_masks(*which):
-        masks_out(masks_pe(*which))
-
-    let_pe(0)
-    let_pe(1)
-    let_pe(2)
-    let_pe(3)
-    pointers(4)
-    to_helper(4)
-    let_mask(0)
-    let_mask(1)
-    pointers(5)
-    to_helper(5)
-    pointers(6)
-    to_helper(6)
-
-    def sums(bank, x, hx):
-        wait("p", hx, H["sel"], last.get(bank))
+    def sums(bank, x, n, *hs):
+        wait("p", "zs", last.get(bank), *hs)
         for i in range(16):
-            h = fin("p", P.matmul(T[bank][:, 0:32], T.sel[:, 128 * i:128 * i + 128], T[x][:, i:512:16], i == 0, i == 15))
+            h = fin("p", P.matmul(T[bank][:, 0:n], sel(i), x(i), i == 0, i == 15))
         return h
 
-    def fail_cols(d):
-        if d == 6:
-            return T.tab[:, BASE[6] + 512 * R:BASE[6] + 512 * R + 512]
-        return T["d%d" % d][:, :]
+    def word_list(r, d):
+        return T.wl[:, WSLOT * r:WSLOT * r + 4] if d == 2 else T.wl[:, WSLOT * r + 4:WSLOT * r + 36]
 
-    def fail_gather(d):
-        q = OWN[d] - 4
-        wait("v", H["d%d" % (d - 1)], H["pu"], *let_seg(d))
-        h = fin("v", V.tensor_tensor(T["xf%d" % d][:, :], fail_cols(d - 1).indirect(T.pu[:, q // 16:q // 16 + 32]),
-                                     T.maskl[:, q:q + 512], A.mult))
-        H["xf%d" % d] = sums("pf%d" % (d % 2), "xf%d" % d, h)
+    def words():
+        H["pu"] = copy(T.pu[:, :], T.pari[:, :], "ld_par")
+        h = ts(T.w2[:, :], T.lr[:, 0:64], 16.0, None, A.mult, None, "ld_lr")
+        tt(T.xw[:, 64:576], T.w2[:, :].indirect(T.pu[:, 4:36]), T.lr[:, 64:576], A.add, h, "pu")
+        h = tt(T.xw[:, 0:64], T.w1[:, :].indirect(T.pu[:, 0:4]), T.lr[:, 0:64], A.add, "w1")
+        H["xw"] = sums("pw", lambda i: T.xw[:, i:576:16], 36, h)
 
-    def fail_ln(d):
-        j = (OWN[d] - 4) // 16
-        wait("s", H["xf%d" % d])
-        last["pf%d" % (d % 2)] = H["lnf%d" % d] = fin("s", S.activation(T.lnf[:, j:j + 32], T["pf%d" % (d % 2)][:, 0:32], F.Ln))
+    def words_list():
+        last["pw"] = H["wl"] = copy(T.wl[:, WSLOT * R:WSLOT * R + 36], T.pw[:, 0:36], "xw")
 
-    def own_list(d):
-        return T["fl%d" % d][:, 32 * R:32 * R + 32]
+    def words_out():
+        out_to_ranks(T.wl[:, WSLOT * R:WSLOT * R + 36], "a_wl", "wl")
 
-    def fail_list(d):
-        j = (OWN[d] - 4) // 16
-        wait("v", H["lnf%d" % d])
-        H["fl%d" % d] = fin("v", V.tensor_scalar(own_list(d), T.lnf[:, j:j + 32], 1.0 / K, float(A0), A.mult, A.add))
-        if d < 7:
-            out_to_ranks(own_list(d), "a_f%d" % d, H["fl%d" % d])
+    mn = [0]
+
+    PART = {"l": slice(512, 768), "t": slice(0, 512)}
+
+    def letters(k):
+        H["lb" + k] = copy(T.lb[:, PART[k]], T.li[:, PART[k]], "ld_l" + k)
+
+    def squares(k):
+        H["lq" + k] = act(T.lq[:, PART[k]], T.lb[:, PART[k]], F.Square, ["lb" + k, "even"], bias=T.pd[:, 4:5])
+
+    def mask_pe(name):
+        b = "pm%d" % (mn[0] % 2)
+        mn[0] += 1
+        k = int(name[1])
+        wait("p", "wr", "lq" + name[0], last.get(b))
+        if name[0] == "l":
+            for u in range(2):
+                r = 2 * (k - 4) + u
+                h = fin("p", P.matmul(T[b][:, 256 * u:256 * u + 256], T.wr[:, 128 * r:128 * r + 128], T.lq[:, 512:768], True, True))
         else:
-            H["flp"] = fin("v", V.tensor_scalar(T.flp[:, :], T.lnf[:, j:j + 32], 1.0 / K, float(A0 - BASE[6] + PAD[6]), A.mult, A.add))
+            r = k - 2
+            for i in range(16):
+                h = fin("p", P.matmul(T[b][:, i:512:16], T.wr[:, 128 * r:128 * r + 128], T.lq[:, 32 * i:32 * i + 32], True, True))
+        H["pm" + name] = (b, h)
 
-    def text_gather(t):
-        d = min(t, 6)
-        wait("v", H["lt%d" % (t - 1)], H["mt1" if t < 4 else "mt4"], *H["tab%d" % d])
-        h = fin("v", V.tensor_tensor(T["xt%d" % t][:, :], T.tab[:, 0:BASE[d + 1]].indirect(T.lt[:, 32 * t - 32:32 * t]),
-                                     T.maskt[:, 512 * t - 512:512 * t], A.mult))
-        H["xt%d" % t] = sums("px%d" % (t % 2), "xt%d" % t, h)
+    def mask_ap(name):
+        k = int(name[1])
+        return T.maskl[:, 512 * (k - 4):512 * (k - 3)] if name[0] == "l" else T.maskt[:, 512 * (k - 2):512 * (k - 1)]
 
-    def text_ln(t):
-        wait("s", H["xt%d" % t])
-        last["px%d" % (t % 2)] = H["lnt%d" % t] = fin("s", S.activation(T.lnt[:, 32 * t:32 * t + 32], T["px%d" % (t % 2)][:, 0:32], F.Ln))
+    def mask_out(name, q="s"):
+        b, h = H["pm" + name]
+        if q == "s":
+            h = act(mask_ap(name), T[b][:, :], F.Relu, [h, "bq"], bias=T.pd[:, 6:7], scale=-1.0)
+        else:
+            h = ts(mask_ap(name), T[b][:, :], T.pd[:, 5:6], 0.0, A.add, A.is_equal, h, "cq")
+        last[b] = H["m" + name] = h
 
-    def text_list(t):
-        c = slice(32 * t, 32 * t + 32)
-        wait("v", H["lnt%d" % t])
-        H["lt%d" % t] = fin("v", V.tensor_scalar(T.lt[:, c], T.lnt[:, c], 1.0 / K, float(A0), A.mult, A.add))
+    def word_table():
+        h = copy(T.c1[:, :], T.msg[:, 64:4 * SLOT].indirect(T.cl1[:, 0:2]), "a_msg", "e12", "cl1")
+        for r in range(4):
+            H["g2w"] = tt(T.g2w[:, 64 * r:64 * r + 64], T.c1[:, :].indirect(T.cl0[:, :]), T.msg[:, SLOT * r:SLOT * r + 64], A.max, h)
 
-    def deep_list(t):
-        c = slice(32 * t, 32 * t + 32)
-        wait("v", H["lnt%d" % t])
-        H["ltp%d" % t] = fin("v", V.tensor_scalar(T.ltp[:, c], T.lnt[:, c], 1.0 / K, float(A0 - BASE[6] + PAD[6]), A.mult, A.add))
+    def word_states():
+        H["y1"] = tt(T.y1[:, :], T.msg[:, 64:4 * SLOT].indirect(T.cl2[:, :]), T.eet[:, :], A.mult, "cl2", "a_msg", "e12", "eet")
 
-    DB = {6: "pt0", 7: "pt1", 8: "pf0", 9: "pf1"}
+    def level2(r):
+        h = act(T.tab[:, 64 * r:64 * r + 64], T.g2w[:, :].indirect(word_list(r, 2)), F.Copy, ["g2w", "wl" if r == R else "a_wl"])
+        H.setdefault("tab2", []).append(h)
+        if r == R:
+            H["own2"] = h
 
-    def deep_gather(t):
-        wait("v", H["ltp%d" % (t - 1)], H["a_t6"], H["e6"], H["fill"])
-        h = fin("v", V.tensor_tensor(T["xp%d" % t][:, :], T.tc6[:, :].indirect(T.ltp[:, 32 * t - 32:32 * t]),
-                                     T.maskt[:, 512 * t - 512:512 * t], A.mult))
-        H["xp%d" % t] = sums(DB[t], "xp%d" % t, h)
+    def tabs(d):
+        return [h for k in range(2, d + 1) for h in H["tab%d" % k]]
 
-    def deep_ln(t):
-        wait("s", H["xp%d" % t])
-        last[DB[t]] = H["lnp%d" % t] = fin("s", S.activation(T.lnp[:, 32 * t:32 * t + 32], T[DB[t]][:, 0:32], F.Ln))
+    def source(d, r):
+        if d == 3:
+            return T.g2w[:, :].indirect(word_list(r, 3)), ["g2w", "wl" if r == R else "a_wl"]
+        return (T.tab[:, 0:BASE[d]].indirect(T["fl%d" % d][:, 32 * r:32 * r + 32]),
+                tabs(d - 1) + ["fl%d" % d if r == R else "a_f%d" % d])
 
-    def running(*names):
-        for buf, t in names:
-            ap = T[buf][:, 32 * t:32 * t + 32]
-            wait("v", H["%s%d" % (buf, t)], H.get("rm"))
-            if "rm" in H:
-                H["rm"] = fin("v", V.tensor_tensor(T.rm[:, :], T.rm[:, :], ap, A.max))
-            else:
-                H["rm"] = fin("v", V.tensor_copy(T.rm[:, :], ap))
+    def level_cols(d, r):
+        return T.tab[:, BASE[d] + 512 * r:BASE[d] + 512 * r + 512]
+
+    def fail_cols(d):
+        return level_cols(6, R) if d == 6 else T["d%d" % d][:, :]
 
     def fail_columns(d):
-        wait("s", *H["tab%d" % (d - 1)])
-        wait("s", H["fl%d" % d])
-        off = T.fl2[:, 4 * R:4 * R + 4] if d == 2 else own_list(d)
-        out = T.d2[:, :] if d == 2 else fail_cols(d)
-        H["d%d" % d] = fin("s", S.activation(out, T.tab[:, 0:BASE[d]].indirect(off), F.Copy))
+        src, hs = source(d, R)
+        H["d%d" % d] = act(fail_cols(d), src, F.Copy, hs)
+        if d == 6:
+            H.setdefault("tab6", []).append(H["d6"])
 
-    def complete(d, c0, c1):
-        if c0 < c1:
-            wait("v", *H["tab%d" % (d - 1)])
-            return [fin("v", V.tensor_tensor(T.tab[:, BASE[d] + 16 * c0:BASE[d] + 16 * c1],
-                                             T.tab[:, 0:BASE[d]].indirect(T["fl%d" % d][:, c0:c1]),
-                                             T["tc%d" % d][:, 16 * c0:16 * c1], A.max))]
-        return []
+    def own_pe(d):
+        wait("p", "ident", "e%d" % d, last.get("po"))
+        H["po%d" % d] = fin("p", P.matmul(T.po[:, :], T.ident[:, :], own_tc(d), True, True))
 
     def complete_own(d):
-        wait("v", H["fl%d" % d], H["e%d" % d])
-        H["tab%d" % d] = complete(d, 32 * R, 32 * R + 32)
-        H["own%d" % d] = H["tab%d" % d][0]
+        out = T.g6[:, :] if d == 6 else level_cols(d, R)
+        last["po"] = H["own%d" % d] = tt(out, fail_cols(d), T.po[:, :], A.max, "d%d" % d, "po%d" % d)
+        if d < 6:
+            H.setdefault("tab%d" % d, []).append(H["own%d" % d])
 
-    def complete_others(d, part):
-        wait("v", H["a_f%d" % d], H["a_t%d" % d])
-        cuts = [(0, 16), (16, 32 * R), (32 * R + 32, 128)] if R else [(32, 48), (48, 128)]
-        for c in (cuts[:1] if part == 0 else cuts[1:]):
-            H["tab%d" % d] += complete(d, *c)
+    def complete(d, r):
+        src, hs = source(d, r)
+        h = tt(level_cols(d, r), src, T["tc%d" % d][:, 512 * r:512 * r + 512], A.max, "a_t%d" % d, *hs)
+        H.setdefault("tab%d" % d, []).append(h)
 
     def plain(q, r):
-        off = T.fl6[:, 32 * r:32 * r + 32]
-        out = T.tab[:, BASE[6] + 512 * r:BASE[6] + 512 * r + 512]
-        src = T.tab[:, 0:BASE[6]].indirect(off)
-        wait(q, *H["tab5"])
-        wait(q, H["a_f6"])
-        if q == "s":
-            h = fin("s", S.activation(out, src, F.Copy))
+        src, hs = source(6, r)
+        h = act(level_cols(6, r), src, F.Copy, hs) if q == "s" else copy(level_cols(6, r), src, *hs)
+        H.setdefault("tab6", []).append(h)
+
+    def fail_rows(d):
+        wait("p", "xg%d" % d)
+        H["py"] = fin("p", P.matmul(T.py[:, :], sel(d - 3), T["xf%d" % d][:, :], d == 3, d == 7))
+
+    def fail3():
+        H["xg3"] = act(T.xf3[:, :], T.y1[:, :].indirect(word_list(R, 3)), F.Copy, ["y1", "wl"])
+
+    def fail_gather(d):
+        j = (OWN[d] - 4) // 16
+        x = T["xf%d" % d]
+        H["xg%d" % d] = tt(x[:, :], fail_cols(d - 1).indirect(T.pu[:, j:j + 32]), mask_ap("l%d" % d), A.mult,
+                           "d%d" % (d - 1), "pu", "ml%d" % d)
+        H["xf%d" % d] = sums("pa", lambda i: x[:, i:512:16], 32, "xg%d" % d)
+
+    def fail_ln(d):
+        last["pa"] = H["lnf%d" % d] = act(T.lnf[:, 32 * (d - 4):32 * (d - 3)], T.pa[:, 0:32], F.Ln, ["xf%d" % d])
+
+    def index(out, in_, shift, *hs):
+        return ts(out, in_, 1.0 / K, float(A0 + shift), A.mult, A.add, *hs)
+
+    def fail_list(d):
+        own = T["fl%d" % d][:, 32 * R:32 * R + 32]
+        src = T.lnf[:, 32 * (d - 4):32 * (d - 3)]
+        H["fl%d" % d] = index(own, src, 0, "lnf%d" % d)
+        if d < 7:
+            out_to_ranks(own, "a_f%d" % d, "fl%d" % d)
         else:
-            h = fin("v", V.tensor_copy(out, src))
-        H["tab6"].append(h)
+            H["flp"] = index(T.flp[:, :], src, PAD[6] - BASE[6])
+
+    def xblock(name, n=1):
+        return T.xt[:, 512 * BLOCK[name]:512 * (BLOCK[name] + n)]
+
+    def lnblock(name, n=1):
+        return T.ln[:, 32 * BLOCK[name]:32 * (BLOCK[name] + n)]
+
+    def text_words():
+        h = ts(T.vf[:, 0:32], T.vi[:, 0:32], 16.0, None, A.mult, None, "ld_vi")
+        h = tt(T.vf[:, 32:64], T.vf[:, 0:32], T.vi[:, 32:64], A.add, h)
+        H["lt1"] = copy(T.lt[:, 32:64], T.vf[:, 32:64], h)
+
+    def text1():
+        H["xt1"] = act(xblock("t1"), T.y1[:, :].indirect(T.lt[:, 32:64]), F.Copy, ["y1", "lt1"])
+
+    def text_gather(t):
+        off = T.lt[:, 32 * t - 32:32 * t]
+        d = min(t, 6)
+        src, hs = (T.g2w[:, :], ["g2w"]) if t == 2 else (T.tab[:, 0:BASE[d + 1]], tabs(d))
+        H["xt%d" % t] = tt(xblock("t%d" % t), src.indirect(off), mask_ap("t%d" % t), A.mult, "lt%d" % (t - 1), "mt%d" % t, *hs)
+
+    def deep_gather(t):
+        H["xp%d" % t] = tt(xblock("p%d" % t), T.tc6[:, :].indirect(T.ltp[:, 32 * t - 32:32 * t]), mask_ap("t%d" % t), A.mult,
+                           "ltp%d" % (t - 1), "a_t6", "e6", "fill", "mt%d" % t)
+
+    xn = [0]
+
+    def text_sums(*names):
+        b = ("px0", "px1", "pw")[xn[0] % 3]
+        xn[0] += 1
+        o = 512 * BLOCK[names[0]]
+        h = sums(b, lambda i: T.xt[:, o + i:o + 512 * len(names):16], 32 * len(names), *["x" + n for n in names])
+        H["s" + names[0]] = (b, h, names)
+
+    def text_ln(name):
+        b, h, names = H["s" + name]
+        last[b] = h = act(lnblock(name, len(names)), T[b][:, 0:32 * len(names)], F.Ln, [h])
+        for n in names:
+            H["ln" + n] = h
+
+    def text_list(t):
+        H["lt%d" % t] = index(T.lt[:, 32 * t:32 * t + 32], lnblock("t%d" % t), 0, "lnt%d" % t)
+
+    def deep_list(t):
+        H["ltp%d" % t] = index(T.ltp[:, 32 * t:32 * t + 32], lnblock("t%d" % t), PAD[6] - BASE[6], "lnt%d" % t)
 
     def own_ap(d):
         if d >= 6:
             return T["g%d" % d][:, :]
+        if d == 1:
+            return T.msg[:, SLOT * R + 64:SLOT * R + 68]
         return T.tab[:, BASE[d] + SIZE[d] * R:BASE[d] + SIZE[d] * R + SIZE[d]]
 
-    def yg_ln(d):
-        c = slice(OWN[d], OWN[d] + SIZE[d])
-        wait("s", H["own%d" % d])
-        H["ya%d" % d] = fin("s", S.activation(T.ya[:, c], own_ap(d), F.Ln))
+    def number_step(q, k, out, in_, *hs):
+        if k == 1:
+            if q == "s":
+                return act(out, in_, F.Identity, hs, bias=float(MAGIC + A0), scale=1.0 / K)
+            return index(out, in_, MAGIC, *hs)
+        if q == "s":
+            return act(out, in_, F.Identity, hs, bias=float(FIRST - MAGIC))
+        return ts(out, in_, float(FIRST - MAGIC), None, A.add, None, *hs)
 
-    def yg_cols(d):
-        return slice(0 if d == 2 else OWN[d], OWN[d] + SIZE[d])
+    def yg_step(d, k, q="s"):
+        c = slice(0 if d == 3 and k else OWN[d], OWN[d] + SIZE[d])
+        if k == 0:
+            H["ya%d" % d] = act(T.ya[:, c], own_ap(d), F.Ln, ["e12" if d == 1 else "own%d" % d])
+        elif k == 1:
+            H["yb%d" % d] = number_step(q, 1, T.yb[:, c], T.ya[:, c], *(["ya1", "ya2", "ya3"] if d == 3 else ["ya%d" % d]))
+        else:
+            store(T.yg[:, c], T.yo[:, c], number_step(q, 2, T.yo[:, c], T.yb[:, c], "yb%d" % d))
 
-    def yg_round(d):
-        wait("s", H["ya%d" % d])
-        H["yb%d" % d] = fin("s", S.activation(T.yb[:, yg_cols(d)], T.ya[:, yg_cols(d)], F.Identity, bias=float(MAGIC + A0), scale=1.0 / K))
+    def yf_low():
+        h = copy(T.yf12[:, 0:4], T.zz[:, 0:4], "zz")
+        h = ts(T.yf12[:, 4:68], T.lr[:, 0:64], 16.0, None, A.add, None, "ld_lr")
+        store(T.yf[:, 0:68], T.yf12[0:128:16, :], h)
 
-    def yg_out(d):
-        wait("s", H["yb%d" % d])
-        h = fin("s", S.activation(T.yo[:, yg_cols(d)], T.yb[:, yg_cols(d)], F.Identity, bias=16.0 - MAGIC))
-        store(T.yg[:, yg_cols(d)], T.yo[:, yg_cols(d)], h)
+    def yf_step(k, q="s"):
+        if k == 0:
+            H["fa"] = act(T.fa[:, :], T.py[:, :], F.Ln, ["py"], bias=TINY)
+        elif k == 1:
+            H["fb"] = number_step(q, 1, T.fb[:, :], T.fa[:, :], "fa")
+        else:
+            h = number_step(q, 2, T.fo[:, :], T.fb[:, :], "fb")
+            for d in range(3, 8):
+                store(T.yf[:, OWN[d]:OWN[d] + 512], T.fo[d - 3:128:16, :], h)
 
-    def yf_numbers(d):
-        j = (OWN[d] - 4) // 16
-        wait("v", H["fl%d" % d])
-        H["nf%d" % d] = fin("v", V.tensor_scalar(T.nf[:, j:j + 32], own_list(d), 16.0, None, A.add))
+    def level7_plain():
+        H["h7"] = act(T.h7[:, :], T.tab[:, :].indirect(T.fl7[:, 32 * R:32 * R + 32]), F.Copy, tabs(6) + ["fl7"])
 
-    def yf_turn(bank, j0, j1, hs):
-        wait("p", *hs)
-        wait("p", H["ident"], last.get(bank))
-        return fin("p", P.transpose(T[bank][0:j1 - j0, 0:128], T.nf[:, j0:j1], T.ident[:, :]))
+    def level7():
+        H["own7"] = tt(T.g7[:, :], T.tc6[:, :].indirect(T.flp[:, :]), T.h7[:, :], A.max, "h7", "flp", "a_t6", "e6", "fill")
 
-    def yf_out(bank, buf, j0, j1, h):
-        n = j1 - j0
-        wait("s", h)
-        h = fin("s", S.activation(T[buf][0:n, :], T[bank][0:n, 0:128], F.Copy))
-        for k in range(8):
-            store(T.yf[k:k + 1, 4 + 16 * j0:4 + 16 * j1], T[buf][0:n, 16 * k:16 * k + 16], h)
+    def largest(k):
+        if k == 1:
+            H["rm"] = tt(T.rm[:, 0:128], T.ln[:, 0:128], T.ln[:, 128:256], A.max, *["lnt%d" % t for t in range(1, 9)])
+        elif k == 2:
+            H["rm"] = tt(T.rm[:, 128:192], T.rm[:, 0:64], T.rm[:, 64:128], A.max, "rm")
+        elif k == 3:
+            H["rm"] = tt(T.rm[:, 0:64], T.rm[:, 128:192], lnblock("p6", 2), A.max, "rm", "lnp6", "lnp7")
+        elif k == 4:
+            H["rm"] = tt(T.rm[:, 64:96], T.rm[:, 0:32], T.rm[:, 32:64], A.max, "rm")
+        else:
+            H["rm"] = tt(T.rm[:, 96:128], T.rm[:, 64:96], lnblock("p8"), A.max, "rm", "lnp8")
 
-    wait("v", H["a_raw"], H["ld_ti12"])
-    for r in range(4):
-        h = fin("v", V.tensor_copy(T.c1f[:, 4 * r:4 * r + 4], T.raw[:, SLOT * r:SLOT * r + 4]))
-    H["tab1"] = [code(T.tab[:, 0:16], T.c1f[:, :], h)]
-    for r in range(4):
-        H["fl2"] = fin("v", V.tensor_copy(T.fl2[:, 4 * r:4 * r + 4], T.raw[:, SLOT * r + 68:SLOT * r + 72]))
-    fail_columns(2)
-    for r in range(4):
-        h = fin("v", V.tensor_copy(T.c2f[:, 64 * r:64 * r + 64], T.raw[:, SLOT * r + 4:SLOT * r + 68]))
-    H["c2"] = code(T.c2[:, :], T.c2f[:, :], h)
-    H["own1"] = H["tab1"][0]
-    yg_ln(1)
-    fail_gather(3)
-    wait("v", H["ld_txt"])
-    H["vb"] = fin("v", V.tensor_copy(T.vb[:, :], T.vi[:, :]))
-    wait("s", H["vb"])
-    H["vq"] = fin("s", S.activation(T.vq[:, :], T.vb[:, :], F.Square))
-    wait("v", H["c2"], *H["tab1"])
-    H["own2"] = fin("v", V.tensor_tensor(T.tab[:, 16:272], T.tab[:, 0:16].indirect(T.fl2[:, :]), T.c2[:, :], A.max))
-    H["tab2"] = [H["own2"]]
-    H["lt0"] = fin("v", V.tensor_copy(T.lt[:, 0:32], T.vi[:, 0:32]))
-    fail_ln(3)
-    fail_list(3)
-    fail_columns(3)
-    text_masks(0, 5, 1, 4)
-    text_masks(5, 10, 1, 4)
-    text_masks(10, 15, 1, 4)
-    text_masks(15, 16, 1, 4)
-    complete_own(3)
-    let_mask(2)
-    fail_gather(4)
-    let_mask(3)
-    let_pe(4)
-    let_pe(5)
-    m0 = masks_pe(0, 2, 4, 10)
-    m1 = masks_pe(2, 4, 4, 10)
-    complete_others(3, 0)
-    text_gather(1)
-    fail_ln(4)
-    fail_list(4)
-    masks_out(m0)
-    masks_out(m1)
-    text_ln(1)
-    complete_others(3, 1)
-    text_list(1)
-    fail_columns(4)
-    text_masks(4, 6, 4, 10)
-    text_masks(6, 8, 4, 10)
-    text_gather(2)
-    let_mask(4)
-    fail_gather(5)
-    text_ln(2)
-    text_masks(8, 10, 4, 10)
-    m0 = masks_pe(10, 12, 4, 10)
-    m1 = masks_pe(12, 14, 4, 10)
-    complete_own(4)
-    let_mask(5)
-    complete_others(4, 0)
-    text_list(2)
-    text_gather(3)
-    fail_ln(5)
-    masks_out(m0)
-    fail_list(5)
-    masks_out(m1)
-    text_ln(3)
-    text_masks(14, 16, 4, 10)
-    complete_others(4, 1)
-    text_list(3)
-    H["nf2"] = fin("v", V.tensor_scalar(T.nf[:, 0:4], T.raw[:, slot + 68:slot + 72], 16.0, None, A.add))
-    yf_numbers(3)
-    fail_columns(5)
-    text_gather(4)
-    H["zz"] = fin("v", V.memset(T.zz[0:8, :], 0.0))
-    store(T.yf[:, 0:4], T.zz[0:8, :], H["zz"])
-    fail_gather(6)
-    complete_own(5)
-    running(("lnt", 1))
-    text_ln(4)
-    text_list(4)
-    running(("lnt", 2))
-    complete_others(5, 0)
-    yf_numbers(4)
-    running(("lnt", 3))
-    fail_ln(6)
-    fail_list(6)
-    running(("lnt", 4))
-    yf_numbers(5)
-    complete_others(5, 1)
-    yg_ln(2)
-    yg_round(2)
-    yg_out(2)
-    yg_ln(3)
-    yg_round(3)
-    H["onesf"] = fin("v", V.memset(T.onesf[:, :], 1.0))
-    wait("gc", H["onesf"])
-    H["ident"] = fin("gc", g.affine_select(T.ident[:, :], T.onesf[:, :], [[-1, 128]], A.is_equal, 0.0, 0, 1))
-    h = yf_turn("pm0", 0, 100, [H["nf%d" % d] for d in (2, 3, 4, 5)])
-    fail_columns(6)
-    H["tab6"] = [H["d6"]]
-    rest = [r for r in range(4) if r != R]
-    text_gather(5)
-    fail_gather(7)
-    plain("s", rest[0])
-    plain("v", rest[2])
-    text_ln(5)
-    text_list(5)
-    plain("s", rest[1])
-    fail_ln(7)
-    deep_list(5)
-    text_gather(6)
-    fail_list(7)
-    deep_gather(6)
-    yf_out("pm0", "tr1", 0, 100, h)
-    wait("s", *H["tab6"])
-    wait("s", H["fl7"])
-    text_ln(6)
-    yf_numbers(6)
-    yf_numbers(7)
-    running(("lnt", 5))
-    H["h7"] = fin("s", S.activation(T.h7[:, :], T.tab[:, :].indirect(own_list(7)), F.Copy))
-    text_list(6)
-    text_gather(7)
-    wait("v", H["fl6"], H["e6"], *H["tab5"])
-    H["own6"] = fin("v", V.tensor_tensor(T.g6[:, :], T.tab[:, 0:BASE[6]].indirect(own_list(6)), own_tc(6), A.max))
-    deep_list(6)
-    running(("lnt", 6))
-    yg_out(3)
-    deep_ln(6)
-    text_ln(7)
-    h7 = yf_turn("pm1", 100, 164, [H["nf6"], H["nf7"]])
-    yg_ln(6)
-    yg_round(6)
-    yg_out(6)
-    running(("lnp", 6))
-    text_list(7)
-    text_gather(8)
-    wait("v", H["h7"], H["flp"], H["a_t6"], H["fill"])
-    H["own7"] = fin("v", V.tensor_tensor(T.g7[:, :], T.tc6[:, :].indirect(T.flp[:, :]), T.h7[:, :], A.max))
-    deep_list(7)
-    running(("lnt", 7))
-    text_ln(8)
-    yf_out("pm1", "tr2", 100, 164, h7)
-    yg_ln(4)
-    yg_round(4)
-    yg_out(4)
-    text_list(8)
-    text_gather(9)
-    deep_list(8)
-    deep_gather(9)
-    deep_gather(7)
-    running(("lnt", 8))
-    deep_gather(8)
-    text_ln(9)
-    yg_ln(7)
-    yg_round(7)
-    deep_ln(9)
-    yg_out(7)
-    deep_ln(7)
-    running(("lnp", 7))
-    deep_ln(8)
-    yg_ln(5)
-    yg_round(5)
-    yg_out(5)
-    running(("lnp", 8))
-    wait("v", H["lnt9"], H["lnp9"])
-    h = fin("v", V.tensor_tensor(T.last[:, 0:32], T.lnt[:, 288:320], T.lnp[:, 288:320], A.max))
-    wait("v", h, H["rm"])
-    h = fin("v", V.tensor_tensor(T.last[:, 32:64], T.rm[:, :], T.last[:, 0:32], A.max))
-    wait("v", h)
-    h = fin("v", V.tensor_scalar(T.lastm[:, :], T.last[:, :], 1.0 / K, float(MAGIC + A0), A.mult, A.add))
-    wait("v", h)
-    h = fin("v", V.tensor_scalar(T.oy[:, :], T.lastm[:, :], 16.0 - MAGIC, None, A.add))
-    store(T.yl[:, :], T.oy[:, 0:32], h)
-    store(T.ym[:, :], T.oy[:, 32:64], h)
+    def text_out():
+        h = tt(T.last[:, 0:32], lnblock("t9"), lnblock("p9"), A.max, "lnt9", "lnp9")
+        h = tt(T.last[:, 32:64], T.rm[:, 96:128], T.last[:, 0:32], A.max, h, "rm")
+        h = number_step("v", 1, T.lastm[:, :], T.last[:, :], h)
+        h = number_step("v", 2, T.oy[:, :], T.lastm[:, :], h)
+        store(T.yl[:, :], T.oy[:, 0:32], h)
+        store(T.ym[:, :], T.oy[:, 32:64], h)
+
+    steps = {
+        "first": first_message, "maskc": mask_constants, "wordc": word_constants, "weights": mask_weights,
+        "float": to_float, "code": to_code, "helper": to_helper, "send3": lambda: out_to_ranks(own_tc(3), "a_t3", "e3"),
+        "words": words, "wordlist": words_list, "wordsout": words_out, "letters": letters, "squares": squares, "pe": mask_pe, "mask": mask_out,
+        "g2w": word_table, "y1": word_states, "level2": lambda k: level2((rest + [R])[k]), "D": fail_columns, "own_pe": own_pe,
+        "own": complete_own, "other": lambda d, k: complete(d, rest[k]), "plain": lambda q, k: plain(q, rest[k]),
+        "rows": fail_rows, "fail3": fail3, "fail": fail_gather, "fln": fail_ln, "flist": fail_list,
+        "twords": text_words, "text1": text1, "text": text_gather, "deep": deep_gather, "sums": text_sums, "ln": text_ln,
+        "tlist": text_list, "dlist": deep_list, "yg": yg_step, "yf12": yf_low, "yf": yf_step,
+        "h7": level7_plain, "g7": level7, "max": largest, "out": text_out,
+    }
+    for step in ORDER.split():
+        name, *args = step.split(".")
+        steps[name](*[int(a) if a.isdigit() else a for a in args])
     wait("gc", ("v", cnt["v"]), ("s", cnt["s"]), ("p", cnt["p"]), ("gc", cnt["gc"]), ("out", cnt["out"]), ("sent", cnt["sent"]))

@@ -10,23 +10,14 @@ SIZE = {1: 4, 2: 64, 3: 512, 4: 512, 5: 512, 6: 512, 7: 512}
 OWN = {1: 0, 2: 4, 3: 68, 4: 580, 5: 1092, 6: 1604, 7: 2116}
 BASE = {2: 0, 3: 256, 4: 2304, 5: 4352, 6: 6400, 7: 8448}
 SLOT = 72
-WSLOT = 40
-PAD = {3: 0, 4: 0, 5: 0, 6: 16}
+EARLY = 0
+WE = EARLY // 16
+SLOT3 = WE + EARLY
+PAD = {4: 0, 5: 0, 6: 16}
+DIRECT = {4: 256, 5: 0, 6: 0}
 BLOCK = {"t1": 0, "t2": 1, "t3": 2, "t4": 3, "t5": 4, "t6": 5, "t7": 6, "t8": 7, "p6": 8, "p7": 9, "p8": 10, "t9": 11, "p9": 12}
 ORDER = """
-maskc first float.3 code.3 send3 words weights letters.l squares.l wordlist wordsout wordc
-float.4 code.4 helper.4 pe.l4 pe.l5 letters.t mask.l4 own_pe.3 float.5 squares.t code.5 helper.5 pe.t2 float.6 mask.l5 pe.t3
-code.6 helper.6 twords yf12 mask.t2 pe.l6
-g2w D.3 y1 mask.t3.v pe.t4 fail.4 yg.1.0 own.3 own_pe.4 text.2 fln.4 flist.4 text1 sums.t1.t2 mask.l6.v pe.l7 level2.3 level2.0 level2.1
-level2.2 other.3.0 ln.t1 fail3 rows.3 rows.4 other.3.1 tlist.2 other.3.2 mask.t4 pe.t5
-D.4 text.3 sums.t3 fail.5 mask.l7 pe.t6 ln.t3 own.4 own_pe.5 fln.5 flist.5 tlist.3 mask.t5 pe.t7 mask.t6 pe.t8 rows.5
-yg.2.0 yg.3.0 other.4.0 other.4.1 other.4.2 mask.t7 pe.t9
-D.5 text.4 sums.t4 fail.6 mask.t8 ln.t4 own.5 own_pe.6 fln.6 flist.6 tlist.4 rows.6 mask.t9 yg.3.1 yg.3.2 yg.4.0
-other.5.0 other.5.1 other.5.2
-D.6 text.5 sums.t5 plain.s.0 fail.7 ln.t5 plain.s.1 plain.v.2 tlist.5 text.6 sums.t6 fln.7 dlist.5 flist.7 rows.7 own.6
-yg.4.1 ln.t6 tlist.6 text.7 sums.t7 h7 deep.6 dlist.6 yg.4.2 ln.t7 tlist.7 text.8 sums.t8 yg.5.0 yg.5.1 g7 dlist.7 ln.t8 tlist.8 dlist.8
-deep.7 sums.p6.p7 deep.8 sums.p8 yg.5.2 yg.6.0 text.9 deep.9 sums.t9.p9 ln.p6 ln.p8 max.1 max.2 max.3 max.4 max.5 yg.7.0 ln.t9 out
-yg.7.1 yg.7.2 yg.6.1.v yf.0 yg.6.2.v yf.1 yf.2
+first maskc float.3 words float.4 weights code.3 letters.l wordlist words4 float.5 wordc code.4 squares.l helper.4 float.6 pe.l4 code.5 send.4 pe.l5 mask.l4 own_pe.4 wordlist4 letters.t code.6 squares.t pe.l6 g2w yg.1.0 pe.t2 helper.5 late3 helper.6 pe.l7 fail.4 twords y1 mask.t2 fln.4 pe.t3 text1 text.2 mask.l6 pe.t4 mask.l5 list2 sums.t1.t2 flist.4 mask.l7 level2 pe.t5 ln.t1 mask.t4.v mask.t3 yg.2.0 pe.t6 pe.t8 mask.t5.v tlist.2 mask.t6.v yf12 yg.3.0 yg.3.1.v pe.t7 fail3 rows.3 text.3 D.4 sums.t3 mask.t8 fail.5 own.4 sgather.4.0 ln.t3 other.4.1 rows.4 fln.5 flist.5 mask.t7 own_pe.5 other.4.2 smax.4.0 tlist.3 yg.4.0 yg.3.2 pe.t9 D.5 mask.t9 text.4 yg.4.1 sums.t4 fail.6 own.5 ln.t4 fln.6 tlist.4 yg.5.0 rows.5 flist.6 sgather.5.0 own_pe.6 other.5.2 other.5.1 yg.5.1 smax.5.0 D.6 text.5 yg.4.2 sums.t5 fail.7 own.6 plain.v.0 ln.t5 plain.s.1 dlist.5 tlist.5 fln.7 plain.s.2 rows.6 flist.7 yg.5.2 text.6 deep.6 sums.t6 yg.6.0 ln.t6 tlist.6 rows.7 h7 text.7 g7 sums.t7 ln.t7 tlist.7 text.8 yg.6.1 yg.7.0 sums.t8 dlist.6.2 ln.t8 deep.7 yg.7.1 tlist.8 yg.6.2 yf.0 dlist.8 yg.7.2 text.9 deep.9 deep.8 yf.1 max.1 sums.t9.p9 sums.p6.p7.p8 max.2 ln.p6 max.3 ln.t9 max.4 max.5 yf.2 out
 """
 
 
@@ -36,9 +27,9 @@ def _sb(cols, dtype):
 
 SCRATCH = {
     "tab": _sb(8448, "bfloat16"), "msg": _sb(4 * SLOT, "bfloat16"), "g2w": _sb(256, "bfloat16"), "y1": _sb(256, "bfloat16"),
-    "ti12": _sb(68, "int32"), "cf12": _sb(68, "float32"), "l1": _sb(4, "uint16"), "l2": _sb(4, "uint16"),
-    "lr": _sb(576, "int32"), "w1": _sb(16, "bfloat16"), "w2": _sb(64, "bfloat16"), "xw": _sb(576, "bfloat16"),
-    "wl": _sb(4 * WSLOT, "uint16"), "pari": _sb(164, "int32"), "pu": _sb(164, "uint16"),
+    "ti12": _sb(68, "int32"), "cf12": _sb(68, "float32"), "l1": _sb(4, "uint16"), "l2f": _sb(32, "float32"), "l2": _sb(16, "uint16"),
+    "lr": _sb(576, "int32"), "w2": _sb(64, "bfloat16"), "xw": _sb(512, "bfloat16"), "wl": _sb(32, "uint16"),
+    "xw4": _sb(512, "bfloat16"), "wl4": _sb(32, "uint16"), "pari": _sb(164, "int32"), "pu": _sb(164, "uint16"),
     "li": _sb(768, "int32"), "lb": _sb(768, "bfloat16"), "lq": _sb(768, "bfloat16"),
     "maskl": _sb(2048, "bfloat16"), "maskt": _sb(4096, "bfloat16"),
     "vi": _sb(64, "int32"), "vf": _sb(64, "float32"),
@@ -46,30 +37,33 @@ SCRATCH = {
     "xt": _sb(13 * 512, "bfloat16"), "ln": _sb(13 * 32, "float32"), "lnf": _sb(128, "float32"),
     "rm": _sb(256, "float32"), "last": _sb(64, "float32"), "lastm": _sb(64, "float32"), "oy": _sb(64, "float32"),
     "zz": _sb(16, "float32"), "yf12": _sb(68, "float32"), "fa": _sb(512, "float32"), "fb": _sb(512, "float32"), "fo": _sb(512, "float32"),
+    "tc3": _sb(4 * SLOT3 or 16, "bfloat16"), "tc3b": _sb(512 - EARLY or 16, "bfloat16"), "w3f": _sb(4 * WE or 16, "float32"),
+    "w3": _sb(4 * WE or 16, "uint16"), "cl3": _sb(WE // 4 or 4, "uint16"), "cl3i": _sb(WE // 4 or 4, "int32"),
+    "d4": _sb(512, "bfloat16"), "d5": _sb(512, "bfloat16"), "dx": _sb(512, "bfloat16"),
     "g6": _sb(512, "bfloat16"), "h7": _sb(512, "bfloat16"), "g7": _sb(512, "bfloat16"),
     "ya": _sb(2628, "float32"), "yb": _sb(2628, "float32"), "yo": _sb(2628, "float32"),
     "pi": _sb(8, "int32"), "pf": _sb(8, "float32"), "pd": _sb(8, "float32"),
-    "rown": _sb(144, "bfloat16"), "rowc": _sb(256, "bfloat16"), "colg": _sb(128, "bfloat16"), "cl2i": _sb(16, "int32"),
-    "cl0": _sb(4, "uint16"), "cl1": _sb(2, "uint16"), "c1": _sb(32, "bfloat16"), "cl2": _sb(16, "uint16"), "zs": _sb(144, "bfloat16"), "ident": _sb(128, "bfloat16"),
-    "eet": _sb(256, "bfloat16"), "e2": _sb(8, "float32"), "blk": _sb(128, "bfloat16"), "b0": _sb(128, "bfloat16"),
-    "b1": _sb(128, "bfloat16"), "wr": _sb(1024, "bfloat16"),
+    "rown": _sb(144, "bfloat16"), "rowc": _sb(256, "bfloat16"), "cl2i": _sb(16, "int32"),
+    "cl0": _sb(4, "uint16"), "cl1": _sb(4, "uint16"), "cl2": _sb(16, "uint16"), "c1": _sb(32, "bfloat16"),
+    "zs": _sb(144, "bfloat16"), "ident": _sb(128, "bfloat16"), "eet": _sb(256, "bfloat16"), "e2": _sb(8, "float32"),
+    "b0": _sb(128, "bfloat16"), "blk": _sb(128, "bfloat16"), "b1": _sb(128, "bfloat16"), "wr": _sb(1024, "bfloat16"),
 }
 for _d in range(3, 7):
     SCRATCH["ti%d" % _d] = _sb(512, "int32")
     SCRATCH["cf%d" % _d] = _sb(512, "float32")
+for _d in range(4, 7):
     SCRATCH["tc%d" % _d] = _sb(PAD[_d] + 2048, "bfloat16")
-for _d in range(3, 6):
-    SCRATCH["d%d" % _d] = _sb(512, "bfloat16")
 for _d in range(3, 8):
     SCRATCH["xf%d" % _d] = _sb(512, "bfloat16")
 for _d in range(4, 8):
     SCRATCH["fl%d" % _d] = _sb(128, "uint16")
-for _b in ("pm0", "pm1", "po", "pa", "px0", "px1", "py", "pw"):
+BANKS = ("pm0", "pm1", "pm2", "pm3", "pm4", "po", "pa", "py")
+for _b in BANKS:
     SCRATCH[_b] = ("psum", [128, 512], "float32")
 
 LOADS = ["ti12", "ti3", "par", "lr", "ti4", "ti5", "ti6", "ll", "lt", "vi"]
-SEMAPHORES = (["v", "s", "p", "gc", "out", "sent", "a_msg", "a_wl"] + ["ld_" + n for n in LOADS]
-              + ["a_t%d" % d for d in range(3, 7)] + ["a_f%d" % d for d in range(4, 7)] + ["h%d" % d for d in range(4, 7)])
+SEMAPHORES = (["v", "s", "p", "gc", "out", "sent", "a_msg", "a_g3", "a_t3"] + ["ld_" + n for n in LOADS]
+              + ["a_t%d" % d for d in range(4, 7)] + ["a_f%d" % d for d in range(4, 7)] + ["h%d" % d for d in range(4, 7)])
 
 
 def helper_of(core, ranks, topo):
@@ -77,6 +71,16 @@ def helper_of(core, ranks, topo):
         if h != core and topo.die(h) != topo.die(core) and all(topo.may_write(h, r) for r in ranks if r != core):
             return h
     return None
+
+
+def others_of(T, r):
+    n = len(T.cores)
+    return [T.cores[(r + k) % n] for k in range(1, n)]
+
+
+def part(T, d, r, relayed):
+    o = PAD[d] + 512 * r
+    return T["tc%d" % d][:, o + DIRECT[d]:o + 512] if relayed else T["tc%d" % d][:, o:o + DIRECT[d]]
 
 
 def bits(engines):
@@ -100,12 +104,12 @@ def send(g, T, topo, core, dsts, ap, sem):
 
 def helper_program(g, core, T, topo, r):
     own = T.cores[r]
-    others = [c for c in T.cores if c != own]
+    others = others_of(T, r)
     near = spare_engines(own, core, others[0], topo)
     n = 0
     for d in range(4, 7):
         g.wait_ge(T.sem["h%d" % d], len(near))
-        n += send(g, T, topo, core, others, T["tc%d" % d][:, PAD[d] + 512 * r:PAD[d] + 512 * r + 512], "a_t%d" % d)
+        n += send(g, T, topo, core, others, part(T, d, r, True), "a_t%d" % d)
     g.wait_ge(T.sem["sent"], n)
 
 
@@ -122,7 +126,7 @@ def rank_program(g, core, T, topo):
                 helper_program(g, core, T, topo, i)
         return
     R = rank
-    others = [c for c in T.cores if c != core]
+    others = others_of(T, R)
     rest = [r for r in range(4) if r != R]
     helper = helper_of(core, T.cores, topo)
     V, S, P = g.vector, g.scalar, g.tensor
@@ -130,7 +134,10 @@ def rank_program(g, core, T, topo):
     cnt = {"v": 0, "s": 0, "p": 0, "gc": 0, "out": 0, "sent": 0}
     seen = {}
     H = {}
-    last = {}
+    last = {b: None for b in BANKS}
+
+    def free_bank():
+        return [b for b in last if b.startswith("pm")][0]
 
     def wait(q, *hs):
         for h in hs:
@@ -162,9 +169,9 @@ def rank_program(g, core, T, topo):
         wait("s", *hs)
         return fin("s", S.activation(out, in_, func, **kw))
 
-    def load(q, name, pairs):
+    def load(name, pairs):
         for out, in_ in pairs:
-            queue[q].dma_start(out, in_).then_inc(T.sem["ld_" + name], 16)
+            g.sync.dma_start(out, in_).then_inc(T.sem["ld_" + name], 16)
         H["ld_" + name] = ("ld_" + name, 16 * len(pairs))
 
     def store(out, in_, *hs):
@@ -174,17 +181,17 @@ def rank_program(g, core, T, topo):
 
     H["zz"] = fin("v", V.memset(T.zz[:, :], 0.0))
     H["lr0"] = fin("v", V.memset(T.lr[:, :], 0))
-    load("y", "ti12", [(T.ti12[:, :], T.tri[:, 0:68])])
-    load("y", "ti3", [(T.ti3[:, :], T.tri[:, OWN[3]:OWN[4]])])
-    load("y", "par", [(T.pari[:, :], T.par[:, :])])
+    load("ti12", [(T.ti12[:, :], T.tri[:, 0:68])])
+    load("ti3", [(T.ti3[:, :], T.tri[:, OWN[3]:OWN[4]])])
+    load("par", [(T.pari[:, :], T.par[:, :])])
     wait("y", "lr0")
-    load("y", "lr", [(T.lr[0:128:16, :], T.let[:, 0:576])])
-    load("y", "ll", [(T.li[k:128:2, 512:768], T.let[:, 576:2624]) for k in range(2)])
-    load("y", "ti4", [(T.ti4[:, :], T.tri[:, OWN[4]:OWN[5]])])
-    load("y", "lt", [(T.li[k:128:2, 0:512], T.txt[:, 1024:5120]) for k in range(2)])
+    load("lr", [(T.lr[0:128:16, :], T.let[:, 0:576])])
+    load("ll", [(T.li[k:128:2, 512:768], T.let[:, 576:2624]) for k in range(2)])
+    load("ti4", [(T.ti4[:, :], T.tri[:, OWN[4]:OWN[5]])])
+    load("lt", [(T.li[k:128:2, 0:512], T.txt[:, 1024:5120]) for k in range(2)])
     for d in (5, 6):
-        load("y", "ti%d" % d, [(T["ti%d" % d][:, :], T.tri[:, OWN[d]:OWN[d + 1]])])
-    load("y", "vi", [(T.vi[:, 32 * t:32 * t + 32], T.txt[:, 512 * t:512 * t + 512]) for t in range(2)])
+        load("ti%d" % d, [(T["ti%d" % d][:, :], T.tri[:, OWN[d]:OWN[d + 1]])])
+    load("vi", [(T.vi[:, 32 * t:32 * t + 32], T.txt[:, 512 * t:512 * t + 512]) for t in range(2)])
 
     def code(out, in_, *hs):
         return act(out, in_, F.Exp, hs, bias=-K * (FIRST + A0), scale=K)
@@ -196,7 +203,8 @@ def rank_program(g, core, T, topo):
     H["rown"] = fin("gc", g.iota(T.rown[:, :], [[1, 144]], 0, 0, **flag))
     H["rowc"] = fin("gc", g.iota(T.rowc[:, :], [[0, 16], [1, 16]], 0, 0, **flag))
     H["cl2i"] = fin("gc", g.iota(T.cl2i[:, :], [[SLOT, 4], [1, 4]], 0, 0))
-    H["w1"] = fin("gc", g.iota(T.w1[:, :], [[1, 16]], 4 * R, 0, **flag))
+    if EARLY:
+        H["cl3i"] = fin("gc", g.iota(T.cl3i[:, :], [[SLOT3, 4], [16, WE // 16]], 0, 0))
     p0 = T.pi[:, 0:1]
     ts(T.pi[:, 1:2], p0, 15, None, A.bitwise_and, None, "pcol")
     ts(T.pi[:, 2:3], p0, 4, None, A.logical_shift_right, None)
@@ -223,7 +231,10 @@ def rank_program(g, core, T, topo):
 
     def word_constants():
         ts(T.cl0[:, :], T.zz[:, 0:4], cc, None, A.add, None, "zz")
-        H["cl1"] = ts(T.cl1[:, :], T.zz[:, 0:2], T.pd[:, 1:2], None, A.add, None, "h1")
+        ts(T.cl1[:, 2:4], T.zz[:, 0:2], T.pd[:, 1:2], 4.0, A.add, A.add, "h1")
+        H["cl1"] = ts(T.cl1[:, 0:2], T.zz[:, 0:2], T.pd[:, 1:2], None, A.add, None)
+        if EARLY:
+            H["cl3"] = ts(T.cl3[:, :], T.cl3i[:, :], cc, None, A.add, None, "cl3i")
         H["cl2"] = copy(T.cl2[:, :], T.cl2i[:, :], "cl2i")
         H["eet"] = ts(T.eet[:, :], T.rowc[:, :], cc, None, A.is_equal, None, "rowc")
         H["ident"] = ts(T.ident[:, :], T.rown[:, 0:128], pp, None, A.is_equal, None, "rown")
@@ -238,56 +249,77 @@ def rank_program(g, core, T, topo):
     def out_to_ranks(ap, sem, *hs):
         wait("gc", *hs)
         cnt["sent"] += send(g, T, topo, core, others, ap, sem)
-        H[sem] = (sem, len(others) * len(topo.engines(core, others[0])))
+        arrives(sem, core)
+
+    def arrives(sem, sender):
+        H[sem] = (sem, H.get(sem, (sem, 0))[1] + len(others) * len(topo.engines(sender, others[0])))
 
     def own_tc(d):
-        return T["tc%d" % d][:, PAD[d] + 512 * R:PAD[d] + 512 * R + 512]
+        return T.tc3[:, :] if d == 3 else T["tc%d" % d][:, PAD[d] + 512 * R:PAD[d] + 512 * R + 512]
 
     def to_float(d):
         H["cf%d" % d] = copy(T["cf%d" % d][:, :], T["ti%d" % d][:, :], "ld_ti%d" % d)
 
     def to_code(d):
-        H["e%d" % d] = code(own_tc(d), T["cf%d" % d][:, :], "cf%d" % d)
+        if d > 3:
+            H["e%d" % d] = code(own_tc(d), T["cf%d" % d][:, :], "cf%d" % d)
+            return
+        if EARLY:
+            H["e3"] = code(T.tc3[:, SLOT3 * R + WE:SLOT3 * (R + 1)], T.cf3[:, 0:EARLY], "cf3")
+        if EARLY < 512:
+            H["e3"] = code(T.tc3b[:, :], T.cf3[:, EARLY:512], "cf3")
+
+    def to_ranks(d):
+        if d == 3:
+            return out_to_ranks(T.tc3[:, SLOT3 * R:SLOT3 * (R + 1)], "a_t3", "e3", "wb")
+        out_to_ranks(part(T, d, R, False), "a_t%d" % d, "e%d" % d)
+        H["direct%d" % d] = True
 
     def to_helper(d):
         eng = spare_engines(core, helper, others[0], topo)
         wait("gc", "e%d" % d)
         rid, pid, _ = topo.addr(helper)
-        g.remote_dma(own_tc(d), own_tc(d), T.sem["h%d" % d], T.sem["sent"], pid, rid, bits(eng))
+        g.remote_dma(part(T, d, R, True), part(T, d, R, True), T.sem["h%d" % d], T.sem["sent"], pid, rid, bits(eng))
         cnt["sent"] += len(eng)
-        H["a_t%d" % d] = ("a_t%d" % d, len(others) * len(topo.engines(helper, others[0])))
+        arrives("a_t%d" % d, helper)
+        H["relayed%d" % d] = True
+
+    def pointers(d):
+        assert "relayed%d" % d in H and (not DIRECT[d] or "direct%d" % d in H)
+        return "a_t%d" % d
 
     def first_message():
         slot = SLOT * R
         h1 = ts(T.l1[:, :], T.ti12[:, 0:4], float(4 - FIRST - 64 * R), None, A.add, None, "ld_ti12")
         H["cf12"] = copy(T.cf12[:, :], T.ti12[:, :])
-        code(T.msg[:, slot + 64:slot + 72], T.cf12[:, 0:8], "cf12")
+        H["i12"] = ts(T.msg[:, slot + 68:slot + 72], T.ti12[:, 0:4], -float(FIRST), None, A.add, None)
+        code(T.msg[:, slot + 64:slot + 68], T.cf12[:, 0:4], "cf12")
         H["e12"] = code(T.msg[:, slot:slot + 64], T.cf12[:, :].indirect(T.l1[:, :]), h1)
-        out_to_ranks(T.msg[:, slot:slot + SLOT], "a_msg", "e12")
+        out_to_ranks(T.msg[:, slot:slot + SLOT], "a_msg", "e12", "i12")
 
     def sums(bank, x, n, *hs):
-        wait("p", "zs", last.get(bank), *hs)
+        wait("p", "zs", last.pop(bank), *hs)
         for i in range(16):
             h = fin("p", P.matmul(T[bank][:, 0:n], sel(i), x(i), i == 0, i == 15))
         return h
 
-    def word_list(r, d):
-        return T.wl[:, WSLOT * r:WSLOT * r + 4] if d == 2 else T.wl[:, WSLOT * r + 4:WSLOT * r + 36]
-
     def words():
         H["pu"] = copy(T.pu[:, :], T.pari[:, :], "ld_par")
         h = ts(T.w2[:, :], T.lr[:, 0:64], 16.0, None, A.mult, None, "ld_lr")
-        tt(T.xw[:, 64:576], T.w2[:, :].indirect(T.pu[:, 4:36]), T.lr[:, 64:576], A.add, h, "pu")
-        h = tt(T.xw[:, 0:64], T.w1[:, :].indirect(T.pu[:, 0:4]), T.lr[:, 0:64], A.add, "w1")
-        H["xw"] = sums("pw", lambda i: T.xw[:, i:576:16], 36, h)
+        H["xw3"] = tt(T.xw[:, :], T.w2[:, :].indirect(T.pu[:, 4:36]), T.lr[:, 64:576], A.add, h, "pu")
+        H["xw"] = sums("pa", lambda i: T.xw[:, i:512:16], 32, "xw3")
 
     def words_list():
-        last["pw"] = H["wl"] = copy(T.wl[:, WSLOT * R:WSLOT * R + 36], T.pw[:, 0:36], "xw")
+        if EARLY:
+            H["wb"] = copy(T.tc3[:, SLOT3 * R:SLOT3 * R + WE], T.pa[:, 0:WE], "xw")
+        last["pa"] = H["wl"] = copy(T.wl[:, :], T.pa[:, 0:32], "xw")
 
-    def words_out():
-        out_to_ranks(T.wl[:, WSLOT * R:WSLOT * R + 36], "a_wl", "wl")
+    def words4():
+        h = act(T.xw4[:, :], T.xw[:, :].indirect(T.pu[:, 36:68]), F.Copy, ["xw3"])
+        H["xw4"] = sums("pa", lambda i: T.xw4[:, i:512:16], 32, h)
 
-    mn = [0]
+    def words4_list():
+        last["pa"] = H["wl4"] = copy(T.wl4[:, :], T.pa[:, 0:32], "xw4")
 
     PART = {"l": slice(512, 768), "t": slice(0, 512)}
 
@@ -298,10 +330,9 @@ def rank_program(g, core, T, topo):
         H["lq" + k] = act(T.lq[:, PART[k]], T.lb[:, PART[k]], F.Square, ["lb" + k, "even"], bias=T.pd[:, 4:5])
 
     def mask_pe(name):
-        b = "pm%d" % (mn[0] % 2)
-        mn[0] += 1
+        b = free_bank()
         k = int(name[1])
-        wait("p", "wr", "lq" + name[0], last.get(b))
+        wait("p", "wr", "lq" + name[0], last.pop(b))
         if name[0] == "l":
             for u in range(2):
                 r = 2 * (k - 4) + u
@@ -324,31 +355,60 @@ def rank_program(g, core, T, topo):
             h = ts(mask_ap(name), T[b][:, :], T.pd[:, 5:6], 0.0, A.add, A.is_equal, h, "cq")
         last[b] = H["m" + name] = h
 
+    def level1(off):
+        return T.msg[:, 64:4 * SLOT].indirect(off)
+
     def word_table():
-        h = copy(T.c1[:, :], T.msg[:, 64:4 * SLOT].indirect(T.cl1[:, 0:2]), "a_msg", "e12", "cl1")
+        h = copy(T.c1[:, :], level1(T.cl1[:, 0:2]), "a_msg", "e12", "cl1")
         for r in range(4):
             H["g2w"] = tt(T.g2w[:, 64 * r:64 * r + 64], T.c1[:, :].indirect(T.cl0[:, :]), T.msg[:, SLOT * r:SLOT * r + 64], A.max, h)
 
     def word_states():
-        H["y1"] = tt(T.y1[:, :], T.msg[:, 64:4 * SLOT].indirect(T.cl2[:, :]), T.eet[:, :], A.mult, "cl2", "a_msg", "e12", "eet")
+        H["y1"] = tt(T.y1[:, :], level1(T.cl2[:, :]), T.eet[:, :], A.mult, "cl2", "a_msg", "e12", "eet")
 
-    def level2(r):
-        h = act(T.tab[:, 64 * r:64 * r + 64], T.g2w[:, :].indirect(word_list(r, 2)), F.Copy, ["g2w", "wl" if r == R else "a_wl"])
-        H.setdefault("tab2", []).append(h)
-        if r == R:
-            H["own2"] = h
+    def level2_list():
+        h = ts(T.l2f[:, :], level1(T.cl1[:, 2:4]), 0.0, None, A.add, None, "a_msg", "e12", "cl1")
+        H["l2"] = copy(T.l2[:, :], T.l2f[:, 0:16], h)
 
-    def tabs(d):
-        return [h for k in range(2, d + 1) for h in H["tab%d" % k]]
-
-    def source(d, r):
-        if d == 3:
-            return T.g2w[:, :].indirect(word_list(r, 3)), ["g2w", "wl" if r == R else "a_wl"]
-        return (T.tab[:, 0:BASE[d]].indirect(T["fl%d" % d][:, 32 * r:32 * r + 32]),
-                tabs(d - 1) + ["fl%d" % d if r == R else "a_f%d" % d])
+    def level2():
+        H["own2"] = copy(T.tab[:, 0:256].indirect(T.l2[:, :]), T.g2w[:, :], "g2w", "l2")
 
     def level_cols(d, r):
         return T.tab[:, BASE[d] + 512 * r:BASE[d] + 512 * r + 512]
+
+    def cols3(r, late):
+        o = BASE[3] + 512 * r
+        return T.tab[:, o + EARLY:o + 512] if late else T.tab[:, o:o + EARLY]
+
+    def late3():
+        H["late3"] = tt(cols3(R, True), T.g2w[:, :].indirect(T.wl[:, WE:32]), T.tc3b[:, :], A.max, "e3", "g2w", "wl")
+        out_to_ranks(cols3(R, True), "a_g3", "late3")
+        if not EARLY:
+            H["own3"] = H["late3"]
+
+    def lists3():
+        h = ts(T.w3f[:, :], T.tc3[:, :].indirect(T.cl3[:, :]), 0.0, None, A.add, None, "a_t3", "e3", "wb", "cl3")
+        H["w3"] = copy(T.w3[:, :], T.w3f[:, :], h)
+
+    def early3(r):
+        off, hs = (T.wl[:, 0:WE], ["wl", "e3"]) if r == R else (T.w3[:, WE * r:WE * r + WE], ["w3"])
+        h = tt(cols3(r, False), T.g2w[:, :].indirect(off), T.tc3[:, SLOT3 * r + WE:SLOT3 * (r + 1)], A.max, "g2w", *hs)
+        made(3, h)
+        if r == R:
+            assert EARLY == 512 or "late3" in H
+            H["own3"] = h
+
+    def tabs(d):
+        levels = range(3 if EARLY else 4, d + 1)
+        assert all(len(H["tab%d" % k]) == 4 for k in levels)
+        return ["own2"] + (["late3", "a_g3"] if EARLY < 512 else []) + [h for k in levels for h in H["tab%d" % k]]
+
+    def source(d, r):
+        return (T.tab[:, 0:BASE[d]].indirect(T["fl%d" % d][:, 32 * r:32 * r + 32]),
+                tabs(d - 1) + ["fl%d" % d if r == R else "a_f%d" % d])
+
+    def made(d, h):
+        H.setdefault("tab%d" % d, []).append(h)
 
     def fail_cols(d):
         return level_cols(6, R) if d == 6 else T["d%d" % d][:, :]
@@ -357,40 +417,55 @@ def rank_program(g, core, T, topo):
         src, hs = source(d, R)
         H["d%d" % d] = act(fail_cols(d), src, F.Copy, hs)
         if d == 6:
-            H.setdefault("tab6", []).append(H["d6"])
+            made(6, H["d6"])
 
     def own_pe(d):
-        wait("p", "ident", "e%d" % d, last.get("po"))
+        wait("p", "ident", "e%d" % d, last.pop("po"))
         H["po%d" % d] = fin("p", P.matmul(T.po[:, :], T.ident[:, :], own_tc(d), True, True))
 
     def complete_own(d):
         out = T.g6[:, :] if d == 6 else level_cols(d, R)
         last["po"] = H["own%d" % d] = tt(out, fail_cols(d), T.po[:, :], A.max, "d%d" % d, "po%d" % d)
         if d < 6:
-            H.setdefault("tab%d" % d, []).append(H["own%d" % d])
+            made(d, H["own%d" % d])
 
     def complete(d, r):
         src, hs = source(d, r)
-        h = tt(level_cols(d, r), src, T["tc%d" % d][:, 512 * r:512 * r + 512], A.max, "a_t%d" % d, *hs)
-        H.setdefault("tab%d" % d, []).append(h)
+        made(d, tt(level_cols(d, r), src, T["tc%d" % d][:, 512 * r:512 * r + 512], A.max, pointers(d), *hs))
+
+    def split_gather(d, r):
+        src, hs = source(d, r)
+        h = act(T.dx[:, :], src, F.Copy, hs + [H.get("dx")])
+        b = free_bank()
+        wait("p", "ident", pointers(d), last.pop(b))
+        assert "split" not in H
+        H["split"] = (b, h, fin("p", P.matmul(T[b][:, :], T.ident[:, :], T["tc%d" % d][:, 512 * r:512 * r + 512], True, True)))
+
+    def split_max(d, r):
+        b, h1, h2 = H.pop("split")
+        last[b] = H["dx"] = tt(level_cols(d, r), T.dx[:, :], T[b][:, :], A.max, h1, h2)
+        made(d, H["dx"])
 
     def plain(q, r):
         src, hs = source(6, r)
-        h = act(level_cols(6, r), src, F.Copy, hs) if q == "s" else copy(level_cols(6, r), src, *hs)
-        H.setdefault("tab6", []).append(h)
+        made(6, act(level_cols(6, r), src, F.Copy, hs) if q == "s" else copy(level_cols(6, r), src, *hs))
 
     def fail_rows(d):
         wait("p", "xg%d" % d)
-        H["py"] = fin("p", P.matmul(T.py[:, :], sel(d - 3), T["xf%d" % d][:, :], d == 3, d == 7))
+        assert d == 3 or "py%d" % (d - 1) in H
+        H["py%d" % d] = fin("p", P.matmul(T.py[:, :], sel(d - 3), T["xf%d" % d][:, :], d == 3, d == 7))
 
     def fail3():
-        H["xg3"] = act(T.xf3[:, :], T.y1[:, :].indirect(word_list(R, 3)), F.Copy, ["y1", "wl"])
+        H["xg3"] = act(T.xf3[:, :], T.y1[:, :].indirect(T.wl[:, :]), F.Copy, ["y1", "wl"])
 
     def fail_gather(d):
         j = (OWN[d] - 4) // 16
         x = T["xf%d" % d]
-        H["xg%d" % d] = tt(x[:, :], fail_cols(d - 1).indirect(T.pu[:, j:j + 32]), mask_ap("l%d" % d), A.mult,
-                           "d%d" % (d - 1), "pu", "ml%d" % d)
+        if d == 4:
+            src, hs = T.g2w[:, :].indirect(T.wl4[:, :]), ["g2w", "wl4"]
+        else:
+            src, hs = fail_cols(d - 1).indirect(T.pu[:, j:j + 32]), ["d%d" % (d - 1), "pu"]
+        H["xg%d" % d] = tt(x[:, :], src, mask_ap("l%d" % d), A.mult, "ml%d" % d, *hs)
         H["xf%d" % d] = sums("pa", lambda i: x[:, i:512:16], 32, "xg%d" % d)
 
     def fail_ln(d):
@@ -430,13 +505,10 @@ def rank_program(g, core, T, topo):
 
     def deep_gather(t):
         H["xp%d" % t] = tt(xblock("p%d" % t), T.tc6[:, :].indirect(T.ltp[:, 32 * t - 32:32 * t]), mask_ap("t%d" % t), A.mult,
-                           "ltp%d" % (t - 1), "a_t6", "e6", "fill", "mt%d" % t)
-
-    xn = [0]
+                           "ltp%d" % (t - 1), pointers(6), "e6", "fill", "mt%d" % t)
 
     def text_sums(*names):
-        b = ("px0", "px1", "pw")[xn[0] % 3]
-        xn[0] += 1
+        b = free_bank()
         o = 512 * BLOCK[names[0]]
         h = sums(b, lambda i: T.xt[:, o + i:o + 512 * len(names):16], 32 * len(names), *["x" + n for n in names])
         H["s" + names[0]] = (b, h, names)
@@ -450,8 +522,10 @@ def rank_program(g, core, T, topo):
     def text_list(t):
         H["lt%d" % t] = index(T.lt[:, 32 * t:32 * t + 32], lnblock("t%d" % t), 0, "lnt%d" % t)
 
-    def deep_list(t):
-        H["ltp%d" % t] = index(T.ltp[:, 32 * t:32 * t + 32], lnblock("t%d" % t), PAD[6] - BASE[6], "lnt%d" % t)
+    def deep_list(t, n=1):
+        h = index(T.ltp[:, 32 * t:32 * (t + n)], lnblock("t%d" % t, n), PAD[6] - BASE[6], *["lnt%d" % k for k in range(t, t + n)])
+        for k in range(t, t + n):
+            H["ltp%d" % k] = h
 
     def own_ap(d):
         if d >= 6:
@@ -479,13 +553,13 @@ def rank_program(g, core, T, topo):
             store(T.yg[:, c], T.yo[:, c], number_step(q, 2, T.yo[:, c], T.yb[:, c], "yb%d" % d))
 
     def yf_low():
-        h = copy(T.yf12[:, 0:4], T.zz[:, 0:4], "zz")
+        copy(T.yf12[:, 0:4], T.zz[:, 0:4], "zz")
         h = ts(T.yf12[:, 4:68], T.lr[:, 0:64], 16.0, None, A.add, None, "ld_lr")
         store(T.yf[:, 0:68], T.yf12[0:128:16, :], h)
 
     def yf_step(k, q="s"):
         if k == 0:
-            H["fa"] = act(T.fa[:, :], T.py[:, :], F.Ln, ["py"], bias=TINY)
+            H["fa"] = act(T.fa[:, :], T.py[:, :], F.Ln, ["py7"], bias=TINY)
         elif k == 1:
             H["fb"] = number_step(q, 1, T.fb[:, :], T.fa[:, :], "fa")
         else:
@@ -497,23 +571,24 @@ def rank_program(g, core, T, topo):
         H["h7"] = act(T.h7[:, :], T.tab[:, :].indirect(T.fl7[:, 32 * R:32 * R + 32]), F.Copy, tabs(6) + ["fl7"])
 
     def level7():
-        H["own7"] = tt(T.g7[:, :], T.tc6[:, :].indirect(T.flp[:, :]), T.h7[:, :], A.max, "h7", "flp", "a_t6", "e6", "fill")
+        H["own7"] = tt(T.g7[:, :], T.tc6[:, :].indirect(T.flp[:, :]), T.h7[:, :], A.max, "h7", "flp", pointers(6), "e6", "fill")
 
     def largest(k):
         if k == 1:
-            H["rm"] = tt(T.rm[:, 0:128], T.ln[:, 0:128], T.ln[:, 128:256], A.max, *["lnt%d" % t for t in range(1, 9)])
+            h = tt(T.rm[:, 0:128], T.ln[:, 0:128], T.ln[:, 128:256], A.max, *["lnt%d" % t for t in range(1, 9)])
         elif k == 2:
-            H["rm"] = tt(T.rm[:, 128:192], T.rm[:, 0:64], T.rm[:, 64:128], A.max, "rm")
+            h = tt(T.rm[:, 128:192], T.rm[:, 0:64], T.rm[:, 64:128], A.max, "rm1")
         elif k == 3:
-            H["rm"] = tt(T.rm[:, 0:64], T.rm[:, 128:192], lnblock("p6", 2), A.max, "rm", "lnp6", "lnp7")
+            h = tt(T.rm[:, 0:64], T.rm[:, 128:192], lnblock("p6", 2), A.max, "rm2", "lnp6", "lnp7")
         elif k == 4:
-            H["rm"] = tt(T.rm[:, 64:96], T.rm[:, 0:32], T.rm[:, 32:64], A.max, "rm")
+            h = tt(T.rm[:, 64:96], T.rm[:, 0:32], T.rm[:, 32:64], A.max, "rm3")
         else:
-            H["rm"] = tt(T.rm[:, 96:128], T.rm[:, 64:96], lnblock("p8"), A.max, "rm", "lnp8")
+            h = tt(T.rm[:, 96:128], T.rm[:, 64:96], lnblock("p8"), A.max, "rm4", "lnp8")
+        H["rm%d" % k] = h
 
     def text_out():
         h = tt(T.last[:, 0:32], lnblock("t9"), lnblock("p9"), A.max, "lnt9", "lnp9")
-        h = tt(T.last[:, 32:64], T.rm[:, 96:128], T.last[:, 0:32], A.max, h, "rm")
+        h = tt(T.last[:, 32:64], T.rm[:, 96:128], T.last[:, 0:32], A.max, h, "rm5")
         h = number_step("v", 1, T.lastm[:, :], T.last[:, :], h)
         h = number_step("v", 2, T.oy[:, :], T.lastm[:, :], h)
         store(T.yl[:, :], T.oy[:, 0:32], h)
@@ -521,10 +596,14 @@ def rank_program(g, core, T, topo):
 
     steps = {
         "first": first_message, "maskc": mask_constants, "wordc": word_constants, "weights": mask_weights,
-        "float": to_float, "code": to_code, "helper": to_helper, "send3": lambda: out_to_ranks(own_tc(3), "a_t3", "e3"),
-        "words": words, "wordlist": words_list, "wordsout": words_out, "letters": letters, "squares": squares, "pe": mask_pe, "mask": mask_out,
-        "g2w": word_table, "y1": word_states, "level2": lambda k: level2((rest + [R])[k]), "D": fail_columns, "own_pe": own_pe,
-        "own": complete_own, "other": lambda d, k: complete(d, rest[k]), "plain": lambda q, k: plain(q, rest[k]),
+        "float": to_float, "code": to_code, "helper": to_helper, "send": to_ranks,
+        "words": words, "wordlist": words_list, "words4": words4, "wordlist4": words4_list,
+        "letters": letters, "squares": squares, "pe": mask_pe, "mask": mask_out,
+        "g2w": word_table, "y1": word_states, "list2": level2_list, "level2": level2,
+        "late3": late3, "lists3": lists3, "early3": lambda k: early3((rest + [R])[k]),
+        "D": fail_columns, "own_pe": own_pe, "own": complete_own, "other": lambda d, k: complete(d, rest[k]),
+        "sgather": lambda d, k: split_gather(d, rest[k]), "smax": lambda d, k: split_max(d, rest[k]),
+        "plain": lambda q, k: plain(q, rest[k]),
         "rows": fail_rows, "fail3": fail3, "fail": fail_gather, "fln": fail_ln, "flist": fail_list,
         "twords": text_words, "text1": text1, "text": text_gather, "deep": deep_gather, "sums": text_sums, "ln": text_ln,
         "tlist": text_list, "dlist": deep_list, "yg": yg_step, "yf12": yf_low, "yf": yf_step,

@@ -5,19 +5,30 @@ K = 0.008435
 A0 = 5248
 FIRST = 32
 MAGIC = 12582912
-TINY = 1e-25
 SIZE = {1: 4, 2: 64, 3: 512, 4: 512, 5: 512, 6: 512, 7: 512}
 OWN = {1: 0, 2: 4, 3: 68, 4: 580, 5: 1092, 6: 1604, 7: 2116}
 BASE = {2: 0, 3: 256, 4: 2304, 5: 4352, 6: 6400, 7: 8448}
 SLOT = 72
-EARLY = 0
+PAD = 16
+EARLY = 256
 WE = EARLY // 16
-SLOT3 = WE + EARLY
-PAD = {4: 0, 5: 0, 6: 16}
+HEAD = WE + EARLY + 4
 DIRECT = {4: 256, 5: 0, 6: 0}
-BLOCK = {"t1": 0, "t2": 1, "t3": 2, "t4": 3, "t5": 4, "t6": 5, "t7": 6, "t8": 7, "p6": 8, "p7": 9, "p8": 10, "t9": 11, "p9": 12}
+BLOCK = {"t1": 0, "t2": 1, "t3": 2, "t4": 3, "t5": 4, "t6": 5, "t7": 6, "t8": 7, "p6": 8, "p7": 9, "p8": 10, "p9": 11, "t9": 12}
+RUN = 12
 ORDER = """
-first maskc float.3 words float.4 weights code.3 letters.l wordlist words4 float.5 wordc code.4 squares.l helper.4 float.6 pe.l4 code.5 send.4 pe.l5 mask.l4 own_pe.4 wordlist4 letters.t code.6 squares.t pe.l6 g2w yg.1.0 pe.t2 helper.5 late3 helper.6 pe.l7 fail.4 twords y1 mask.t2 fln.4 pe.t3 text1 text.2 mask.l6 pe.t4 mask.l5 list2 sums.t1.t2 flist.4 mask.l7 level2 pe.t5 ln.t1 mask.t4.v mask.t3 yg.2.0 pe.t6 pe.t8 mask.t5.v tlist.2 mask.t6.v yf12 yg.3.0 yg.3.1.v pe.t7 fail3 rows.3 text.3 D.4 sums.t3 mask.t8 fail.5 own.4 sgather.4.0 ln.t3 other.4.1 rows.4 fln.5 flist.5 mask.t7 own_pe.5 other.4.2 smax.4.0 tlist.3 yg.4.0 yg.3.2 pe.t9 D.5 mask.t9 text.4 yg.4.1 sums.t4 fail.6 own.5 ln.t4 fln.6 tlist.4 yg.5.0 rows.5 flist.6 sgather.5.0 own_pe.6 other.5.2 other.5.1 yg.5.1 smax.5.0 D.6 text.5 yg.4.2 sums.t5 fail.7 own.6 plain.v.0 ln.t5 plain.s.1 dlist.5 tlist.5 fln.7 plain.s.2 rows.6 flist.7 yg.5.2 text.6 deep.6 sums.t6 yg.6.0 ln.t6 tlist.6 rows.7 h7 text.7 g7 sums.t7 ln.t7 tlist.7 text.8 yg.6.1 yg.7.0 sums.t8 dlist.6.2 ln.t8 deep.7 yg.7.1 tlist.8 yg.6.2 yf.0 dlist.8 yg.7.2 text.9 deep.9 deep.8 yf.1 max.1 sums.t9.p9 sums.p6.p7.p8 max.2 ln.p6 max.3 ln.t9 max.4 max.5 yf.2 out
+first maskc sumc code.3 squares.l code.4 words squares.t code.5 weights.v yf12.v wordlist helper.4 send.4 helper.5
+pe.l4 pe.l6 pe.l5 pe.t2 mask.l6 mask.l4.v pe.t3 mask.l5.v pe.t8 pe.t7 twords.s mask.t2.v words4 wordc
+g2w y1 late3 code.6 helper.6 scanc own_pe.4 wordlist4.v pe.l7 early3.3 fail.4 text.2 yg.1.0 text1 mask.l7.v mask.t3 mask.t7 fln.4
+list3 early3.0 sums.t1.t2 early3.1 list2 flist.4.s early3.2 level2 yg.3.0 ln.t1 tlist.2.s
+text.3 yg.2.0 pe.t4 D.4 sums.t3 own.4 yg.3.1 fail3 ln.t3 fail.5 yg.3.2 own_pe.5 other.4.2 tlist.3.s other.4.0 fln.5 other.4.1
+pe.t5 mask.t4 text.4 flist.5.s yg.4.0
+D.5 pe.t6 rows.3 fail.6 mask.t8 mask.t5 sums.t4 yg.4.1 fln.6 flist.6.s own.5 rows.4 rows.5 yg.5.0 ln.t4 mask.t6 other.5.2 pe.t9
+own_pe.6 yg.4.2 tlist.4.s mask.t9 other.5.0 other.5.1
+D.6 text.5 sums.t5 rows.6 plain.s.1 fail.7 plain.v.0 ln.t5 plain.s.2 fln.7 tlist.5.s rows.7 flist.7.s own.6
+text.6 plist.s h7 sums.t6 g7 yg.5.1 ln.t6 dlist.5.s tlist.6.s yg.5.2 dlist.6.s yg.6.0 text.7 yf.0 deep.7 sums.t7 ln.t7 deep.6
+tlist.7.s yg.6.1 dlist.7.s text.8 yg.7.0 deep.8 yg.6.2 sums.t8 ln.t8 dlist.8.s tlist.8.s yf.1 deep.9 yg.7.1 sums.p6.p7.p8 yf.2
+sums.p9 text.9 ln.p6 ln.p9 yg.7.2 max sums.t9 ln.t9 out
 """
 
 
@@ -26,35 +37,30 @@ def _sb(cols, dtype):
 
 
 SCRATCH = {
-    "tab": _sb(8448, "bfloat16"), "msg": _sb(4 * SLOT, "bfloat16"), "g2w": _sb(256, "bfloat16"), "y1": _sb(256, "bfloat16"),
-    "ti12": _sb(68, "int32"), "cf12": _sb(68, "float32"), "l1": _sb(4, "uint16"), "l2f": _sb(32, "float32"), "l2": _sb(16, "uint16"),
-    "lr": _sb(576, "int32"), "w2": _sb(64, "bfloat16"), "xw": _sb(512, "bfloat16"), "wl": _sb(32, "uint16"),
+    "tab": _sb(8448, "bfloat16"), "msg": ("sbuf", [128, 4, SLOT], "bfloat16"), "c1": _sb(16, "bfloat16"),
+    "g2w": _sb(256, "bfloat16"), "y1": _sb(256, "bfloat16"),
+    "ti12": _sb(68, "int32"), "l1": _sb(4, "uint16"), "l2f": _sb(16, "float32"), "l2": _sb(16, "uint16"),
+    "lr": _sb(576, "int32"), "w1": _sb(16, "bfloat16"), "w2": _sb(64, "bfloat16"), "xw": _sb(576, "bfloat16"), "wl": _sb(32, "uint16"),
     "xw4": _sb(512, "bfloat16"), "wl4": _sb(32, "uint16"), "pari": _sb(164, "int32"), "pu": _sb(164, "uint16"),
-    "li": _sb(768, "int32"), "lb": _sb(768, "bfloat16"), "lq": _sb(768, "bfloat16"),
-    "maskl": _sb(2048, "bfloat16"), "maskt": _sb(4096, "bfloat16"),
+    "li": _sb(768, "int32"), "lq": _sb(768, "bfloat16"), "maskl": _sb(2048, "bfloat16"), "maskt": _sb(4096, "bfloat16"),
     "vi": _sb(64, "int32"), "vf": _sb(64, "float32"),
-    "lt": _sb(320, "uint16"), "ltp": _sb(320, "uint16"), "flp": _sb(32, "uint16"),
-    "xt": _sb(13 * 512, "bfloat16"), "ln": _sb(13 * 32, "float32"), "lnf": _sb(128, "float32"),
-    "rm": _sb(256, "float32"), "last": _sb(64, "float32"), "lastm": _sb(64, "float32"), "oy": _sb(64, "float32"),
-    "zz": _sb(16, "float32"), "yf12": _sb(68, "float32"), "fa": _sb(512, "float32"), "fb": _sb(512, "float32"), "fo": _sb(512, "float32"),
-    "tc3": _sb(4 * SLOT3 or 16, "bfloat16"), "tc3b": _sb(512 - EARLY or 16, "bfloat16"), "w3f": _sb(4 * WE or 16, "float32"),
-    "w3": _sb(4 * WE or 16, "uint16"), "cl3": _sb(WE // 4 or 4, "uint16"), "cl3i": _sb(WE // 4 or 4, "int32"),
-    "d4": _sb(512, "bfloat16"), "d5": _sb(512, "bfloat16"), "dx": _sb(512, "bfloat16"),
+    "lt": _sb(288, "uint16"), "ltp": _sb(288, "uint16"), "flp": _sb(32, "uint16"),
+    "xt": _sb(13 * 512, "bfloat16"), "ln": _sb(13 * 32, "float32"), "xf": _sb(2560, "bfloat16"), "lnf": _sb(128, "float32"),
+    "rm": _sb(32 * RUN, "float32"), "anew": _sb(32 * RUN, "float32"),
+    "last": _sb(64, "float32"), "lastm": _sb(64, "float32"), "oy": _sb(64, "float32"),
+    "zz": _sb(16, "float32"), "yf12": _sb(68, "float32"), "fa": _sb(160, "float32"), "fb": _sb(160, "float32"), "fo": _sb(160, "float32"),
+    "w3": _sb(4 * WE, "uint16"), "tc3": _sb(512 - EARLY, "bfloat16"), "tc4": ("sbuf", [128, 4, -(-(HEAD + 512) // 8) * 8], "bfloat16"), "tc5": _sb(2048, "bfloat16"),
+    "tc6": _sb(PAD + 2048, "bfloat16"), "d4": _sb(512, "bfloat16"), "d5": _sb(512, "bfloat16"), "dx": _sb(1536, "bfloat16"),
     "g6": _sb(512, "bfloat16"), "h7": _sb(512, "bfloat16"), "g7": _sb(512, "bfloat16"),
     "ya": _sb(2628, "float32"), "yb": _sb(2628, "float32"), "yo": _sb(2628, "float32"),
-    "pi": _sb(8, "int32"), "pf": _sb(8, "float32"), "pd": _sb(8, "float32"),
+    "pi": _sb(4, "int32"), "pf": _sb(4, "float32"), "pd": _sb(8, "float32"),
     "rown": _sb(144, "bfloat16"), "rowc": _sb(256, "bfloat16"), "cl2i": _sb(16, "int32"),
-    "cl0": _sb(4, "uint16"), "cl1": _sb(4, "uint16"), "cl2": _sb(16, "uint16"), "c1": _sb(32, "bfloat16"),
+    "cl0": _sb(4, "uint16"), "cl2": _sb(16, "uint16"),
     "zs": _sb(144, "bfloat16"), "ident": _sb(128, "bfloat16"), "eet": _sb(256, "bfloat16"), "e2": _sb(8, "float32"),
     "b0": _sb(128, "bfloat16"), "blk": _sb(128, "bfloat16"), "b1": _sb(128, "bfloat16"), "wr": _sb(1024, "bfloat16"),
 }
 for _d in range(3, 7):
     SCRATCH["ti%d" % _d] = _sb(512, "int32")
-    SCRATCH["cf%d" % _d] = _sb(512, "float32")
-for _d in range(4, 7):
-    SCRATCH["tc%d" % _d] = _sb(PAD[_d] + 2048, "bfloat16")
-for _d in range(3, 8):
-    SCRATCH["xf%d" % _d] = _sb(512, "bfloat16")
 for _d in range(4, 8):
     SCRATCH["fl%d" % _d] = _sb(128, "uint16")
 BANKS = ("pm0", "pm1", "pm2", "pm3", "pm4", "po", "pa", "py")
@@ -62,7 +68,7 @@ for _b in BANKS:
     SCRATCH[_b] = ("psum", [128, 512], "float32")
 
 LOADS = ["ti12", "ti3", "par", "lr", "ti4", "ti5", "ti6", "ll", "lt", "vi"]
-SEMAPHORES = (["v", "s", "p", "gc", "out", "sent", "a_msg", "a_g3", "a_t3"] + ["ld_" + n for n in LOADS]
+SEMAPHORES = (["v", "s", "p", "gc", "out", "sent", "a_msg", "a_g3", "a_d4"] + ["ld_" + n for n in LOADS]
               + ["a_t%d" % d for d in range(4, 7)] + ["a_f%d" % d for d in range(4, 7)] + ["h%d" % d for d in range(4, 7)])
 
 
@@ -78,9 +84,15 @@ def others_of(T, r):
     return [T.cores[(r + k) % n] for k in range(1, n)]
 
 
+def pointer_cols(T, d, r, lo=0, hi=512):
+    if d == 4:
+        return T.tc4[:, r, HEAD + lo:HEAD + hi]
+    o = 512 * r + (PAD if d == 6 else 0)
+    return T["tc%d" % d][:, o + lo:o + hi]
+
+
 def part(T, d, r, relayed):
-    o = PAD[d] + 512 * r
-    return T["tc%d" % d][:, o + DIRECT[d]:o + 512] if relayed else T["tc%d" % d][:, o:o + DIRECT[d]]
+    return pointer_cols(T, d, r, DIRECT[d], 512) if relayed else pointer_cols(T, d, r, -HEAD, DIRECT[d])
 
 
 def bits(engines):
@@ -169,14 +181,19 @@ def rank_program(g, core, T, topo):
         wait("s", *hs)
         return fin("s", S.activation(out, in_, func, **kw))
 
+    def linear(q, out, in_, scale, bias, *hs):
+        if q == "s":
+            return act(out, in_, F.Identity, hs, bias=float(bias), scale=float(scale))
+        return ts(out, in_, float(scale), float(bias), A.mult, A.add, *hs)
+
     def load(name, pairs):
         for out, in_ in pairs:
             g.sync.dma_start(out, in_).then_inc(T.sem["ld_" + name], 16)
         H["ld_" + name] = ("ld_" + name, 16 * len(pairs))
 
-    def store(out, in_, *hs):
-        wait("y", *hs)
-        g.sync.dma_start(out, in_).then_inc(T.sem["out"], 16)
+    def store(out, in_, h, q="y"):
+        wait(q, h)
+        queue[q].dma_start(out, in_).then_inc(T.sem["out"], 16)
         cnt["out"] += 16
 
     H["zz"] = fin("v", V.memset(T.zz[:, :], 0.0))
@@ -196,52 +213,53 @@ def rank_program(g, core, T, topo):
     def code(out, in_, *hs):
         return act(out, in_, F.Exp, hs, bias=-K * (FIRST + A0), scale=K)
 
-    H["fill"] = code(T.tc6[:, 0:PAD[6]], T.zz[:, :], "zz")
+    H["fill"] = code(T.tc6[:, 0:PAD], T.zz[:, :], "zz")
 
     flag = {"allow_small_or_imprecise_dtypes": True}
     H["pcol"] = fin("gc", g.iota(T.pi[:, 0:1], [[0, 1]], 0, 1))
-    H["rown"] = fin("gc", g.iota(T.rown[:, :], [[1, 144]], 0, 0, **flag))
     H["rowc"] = fin("gc", g.iota(T.rowc[:, :], [[0, 16], [1, 16]], 0, 0, **flag))
-    H["cl2i"] = fin("gc", g.iota(T.cl2i[:, :], [[SLOT, 4], [1, 4]], 0, 0))
-    if EARLY:
-        H["cl3i"] = fin("gc", g.iota(T.cl3i[:, :], [[SLOT3, 4], [16, WE // 16]], 0, 0))
+    H["rown"] = fin("gc", g.iota(T.rown[:, :], [[1, 144]], 0, 0, **flag))
+    H["cl2i"] = fin("gc", g.iota(T.cl2i[:, :], [[1, 16]], 0, 0))
+    H["w1"] = fin("gc", g.iota(T.w1[:, :], [[1, 16]], 4 * R, 0, **flag))
     p0 = T.pi[:, 0:1]
     ts(T.pi[:, 1:2], p0, 15, None, A.bitwise_and, None, "pcol")
-    ts(T.pi[:, 2:3], p0, 4, None, A.logical_shift_right, None)
-    ts(T.pi[:, 3:4], p0, 15, 1, A.bitwise_and, A.logical_shift_right)
-    ts(T.pi[:, 4:5], p0, 1, None, A.bitwise_and, None)
-    h = ts(T.pi[:, 5:6], p0, 15, 2, A.bitwise_and, A.logical_shift_right)
-    H["pf"] = copy(T.pf[:, 0:6], T.pi[:, 0:6], h)
-    pp, cc, pg, half, odd, quad = [T.pf[:, k:k + 1] for k in range(6)]
+    ts(T.pi[:, 2:3], p0, 15, 1, A.bitwise_and, A.logical_shift_right)
+    h = ts(T.pi[:, 3:4], p0, 1, None, A.bitwise_and, None)
+    H["pf"] = copy(T.pf[:, :], T.pi[:, :], h)
+    pp, cc, half, odd = [T.pf[:, k:k + 1] for k in range(4)]
     h = ts(T.pd[:, 3:4], odd, 2.0, -1.0, A.mult, A.add, "pf")
-    h0 = ts(T.pd[:, 0:1], pg, 16.0, 15.0, A.mult, A.add)
     h = ts(T.b0[:, :], T.rowc[:, 0:128], T.pd[:, 3:4], odd, A.mult, A.add, h, "rowc")
-    H["e2"] = ts(T.e2[:, :], T.rowc[:, 0:8], half, None, A.is_equal, None)
     wait("gc", h)
     h = fin("gc", g.affine_select(T.blk[:, :], T.b0[:, :], [[-16, 8], [0, 16]], A.is_ge, 0.0, 0, 1))
     wait("gc", h)
     H["b1"] = fin("gc", g.affine_select(T.b1[:, :], T.blk[:, :], [[16, 8], [0, 16]], A.is_ge, 0.0, 15, -1))
-    H["zs"] = ts(T.zs[:, :], T.rown[:, :], T.pd[:, 0:1], None, A.is_equal, None, h0, "rown")
+
+    def sum_constants():
+        h = ts(T.pd[:, 0:1], pp, cc, 15.0, A.subtract, A.add)
+        H["e2"] = ts(T.e2[:, :], T.rowc[:, 0:8], half, None, A.is_equal, None)
+        H["zs"] = ts(T.zs[:, :], T.rown[:, :], T.pd[:, 0:1], None, A.is_equal, None, h, "rown")
 
     def mask_constants():
         H["even"] = ts(T.pd[:, 4:5], odd, -1.0, 1.0, A.mult, A.add)
         H["cq"] = ts(T.pd[:, 5:6], cc, 1.0, cc, A.add, A.mult)
-        H["h1"] = ts(T.pd[:, 1:2], quad, float(SLOT - 4), cc, A.mult, A.add)
         H["bq"] = ts(T.pd[:, 6:7], T.pd[:, 5:6], -1.0, 1.0, A.mult, A.add, "cq")
 
+    def scan_constants():
+        H["anew"] = fin("gc", g.iota(T.anew[:, :], [[0, 32], [2000, RUN]], -1000, 0, **flag))
+
     def word_constants():
-        ts(T.cl0[:, :], T.zz[:, 0:4], cc, None, A.add, None, "zz")
-        ts(T.cl1[:, 2:4], T.zz[:, 0:2], T.pd[:, 1:2], 4.0, A.add, A.add, "h1")
-        H["cl1"] = ts(T.cl1[:, 0:2], T.zz[:, 0:2], T.pd[:, 1:2], None, A.add, None)
-        if EARLY:
-            H["cl3"] = ts(T.cl3[:, :], T.cl3i[:, :], cc, None, A.add, None, "cl3i")
+        H["cl0"] = ts(T.cl0[:, :], T.zz[:, 0:4], cc, None, A.add, None, "zz")
         H["cl2"] = copy(T.cl2[:, :], T.cl2i[:, :], "cl2i")
         H["eet"] = ts(T.eet[:, :], T.rowc[:, :], cc, None, A.is_equal, None, "rowc")
         H["ident"] = ts(T.ident[:, :], T.rown[:, 0:128], pp, None, A.is_equal, None, "rown")
 
-    def mask_weights():
+    def mask_weights(q="s"):
         for r in range(8):
-            H["wr"] = act(T.wr[:, 128 * r:128 * r + 128], T.b1[:, :], F.Copy, ["b1", "e2"], scale=T.e2[:, r:r + 1])
+            out, col = T.wr[:, 128 * r:128 * r + 128], T.e2[:, r:r + 1]
+            if q == "s":
+                H["wr"] = act(out, T.b1[:, :], F.Copy, ["b1", "e2"], scale=col)
+            else:
+                H["wr"] = ts(out, T.b1[:, :], col, None, A.mult, None, "b1", "e2")
 
     def sel(i):
         return T.zs[:, 15 - i:143 - i]
@@ -252,28 +270,20 @@ def rank_program(g, core, T, topo):
         arrives(sem, core)
 
     def arrives(sem, sender):
-        H[sem] = (sem, H.get(sem, (sem, 0))[1] + len(others) * len(topo.engines(sender, others[0])))
+        H[sem] = (sem, len(others) * len(topo.engines(sender, others[0])))
 
     def own_tc(d):
-        return T.tc3[:, :] if d == 3 else T["tc%d" % d][:, PAD[d] + 512 * R:PAD[d] + 512 * R + 512]
-
-    def to_float(d):
-        H["cf%d" % d] = copy(T["cf%d" % d][:, :], T["ti%d" % d][:, :], "ld_ti%d" % d)
+        return pointer_cols(T, d, R)
 
     def to_code(d):
-        if d > 3:
-            H["e%d" % d] = code(own_tc(d), T["cf%d" % d][:, :], "cf%d" % d)
-            return
-        if EARLY:
-            H["e3"] = code(T.tc3[:, SLOT3 * R + WE:SLOT3 * (R + 1)], T.cf3[:, 0:EARLY], "cf3")
-        if EARLY < 512:
-            H["e3"] = code(T.tc3b[:, :], T.cf3[:, EARLY:512], "cf3")
+        if d == 3:
+            code(T.tc4[:, R, WE:WE + EARLY], T.ti3[:, 0:EARLY], "ld_ti3")
+            H["e3"] = code(T.tc3[:, :], T.ti3[:, EARLY:512])
+        else:
+            H["e%d" % d] = code(own_tc(d), T["ti%d" % d][:, :], "ld_ti%d" % d)
 
     def to_ranks(d):
-        if d == 3:
-            return out_to_ranks(T.tc3[:, SLOT3 * R:SLOT3 * (R + 1)], "a_t3", "e3", "wb")
-        out_to_ranks(part(T, d, R, False), "a_t%d" % d, "e%d" % d)
-        H["direct%d" % d] = True
+        out_to_ranks(part(T, d, R, False), "a_d%d" % d, "e3", "e%d" % d, "wb")
 
     def to_helper(d):
         eng = spare_engines(core, helper, others[0], topo)
@@ -282,20 +292,15 @@ def rank_program(g, core, T, topo):
         g.remote_dma(part(T, d, R, True), part(T, d, R, True), T.sem["h%d" % d], T.sem["sent"], pid, rid, bits(eng))
         cnt["sent"] += len(eng)
         arrives("a_t%d" % d, helper)
-        H["relayed%d" % d] = True
 
     def pointers(d):
-        assert "relayed%d" % d in H and (not DIRECT[d] or "direct%d" % d in H)
-        return "a_t%d" % d
+        return ["a_t%d" % d] + (["a_d%d" % d] if DIRECT[d] else [])
 
     def first_message():
-        slot = SLOT * R
-        h1 = ts(T.l1[:, :], T.ti12[:, 0:4], float(4 - FIRST - 64 * R), None, A.add, None, "ld_ti12")
-        H["cf12"] = copy(T.cf12[:, :], T.ti12[:, :])
-        H["i12"] = ts(T.msg[:, slot + 68:slot + 72], T.ti12[:, 0:4], -float(FIRST), None, A.add, None)
-        code(T.msg[:, slot + 64:slot + 68], T.cf12[:, 0:4], "cf12")
-        H["e12"] = code(T.msg[:, slot:slot + 64], T.cf12[:, :].indirect(T.l1[:, :]), h1)
-        out_to_ranks(T.msg[:, slot:slot + SLOT], "a_msg", "e12", "i12")
+        h = ts(T.l1[:, :], T.ti12[:, 0:4], float(4 - FIRST - 64 * R), None, A.add, None, "ld_ti12")
+        code(T.msg[:, R, 64:68], T.ti12[:, 0:4], "ld_ti12")
+        H["e12"] = code(T.msg[:, R, 0:64], T.ti12[:, :].indirect(T.l1[:, :]), h)
+        out_to_ranks(T.msg[:, R, 0:68], "a_msg", "e12")
 
     def sums(bank, x, n, *hs):
         wait("p", "zs", last.pop(bank), *hs)
@@ -305,29 +310,26 @@ def rank_program(g, core, T, topo):
 
     def words():
         H["pu"] = copy(T.pu[:, :], T.pari[:, :], "ld_par")
-        h = ts(T.w2[:, :], T.lr[:, 0:64], 16.0, None, A.mult, None, "ld_lr")
-        H["xw3"] = tt(T.xw[:, :], T.w2[:, :].indirect(T.pu[:, 4:36]), T.lr[:, 64:576], A.add, h, "pu")
-        H["xw"] = sums("pa", lambda i: T.xw[:, i:512:16], 32, "xw3")
+        H["w2"] = ts(T.w2[:, :], T.lr[:, 0:64], 16.0, None, A.mult, None, "ld_lr")
+        tt(T.xw[:, 0:64], T.w1[:, :].indirect(T.pu[:, 0:4]), T.lr[:, 0:64], A.add, "w1", "pu")
+        H["xw3"] = tt(T.xw[:, 64:576], T.w2[:, :].indirect(T.pu[:, 4:36]), T.lr[:, 64:576], A.add, "w2")
+        H["xw"] = sums("pa", lambda i: T.xw[:, i:576:16], 36, "xw3")
 
     def words_list():
-        if EARLY:
-            H["wb"] = copy(T.tc3[:, SLOT3 * R:SLOT3 * R + WE], T.pa[:, 0:WE], "xw")
-        last["pa"] = H["wl"] = copy(T.wl[:, :], T.pa[:, 0:32], "xw")
+        copy(pointer_cols(T, 4, R, -4, 0), T.pa[:, 0:4], "xw")
+        H["wb"] = copy(T.tc4[:, R, 0:WE], T.pa[:, 4:4 + WE])
+        last["pa"] = H["wl"] = copy(T.wl[:, :], T.pa[:, 4:36])
 
     def words4():
-        h = act(T.xw4[:, :], T.xw[:, :].indirect(T.pu[:, 36:68]), F.Copy, ["xw3"])
+        h = act(T.xw4[:, :], T.xw[:, 64:576].indirect(T.pu[:, 36:68]), F.Copy, ["xw3"])
         H["xw4"] = sums("pa", lambda i: T.xw4[:, i:512:16], 32, h)
 
-    def words4_list():
-        last["pa"] = H["wl4"] = copy(T.wl4[:, :], T.pa[:, 0:32], "xw4")
-
-    PART = {"l": slice(512, 768), "t": slice(0, 512)}
-
-    def letters(k):
-        H["lb" + k] = copy(T.lb[:, PART[k]], T.li[:, PART[k]], "ld_l" + k)
+    def words4_list(q="v"):
+        last["pa"] = H["wl4"] = linear(q, T.wl4[:, :], T.pa[:, 0:32], 1, 0, "xw4")
 
     def squares(k):
-        H["lq" + k] = act(T.lq[:, PART[k]], T.lb[:, PART[k]], F.Square, ["lb" + k, "even"], bias=T.pd[:, 4:5])
+        c = slice(512, 768) if k == "l" else slice(0, 512)
+        H["lq" + k] = act(T.lq[:, c], T.li[:, c], F.Square, ["ld_l" + k, "even"], bias=T.pd[:, 4:5])
 
     def mask_pe(name):
         b = free_bank()
@@ -355,53 +357,42 @@ def rank_program(g, core, T, topo):
             h = ts(mask_ap(name), T[b][:, :], T.pd[:, 5:6], 0.0, A.add, A.is_equal, h, "cq")
         last[b] = H["m" + name] = h
 
-    def level1(off):
-        return T.msg[:, 64:4 * SLOT].indirect(off)
-
     def word_table():
-        h = copy(T.c1[:, :], level1(T.cl1[:, 0:2]), "a_msg", "e12", "cl1")
+        H["c1"] = copy(T.c1[:, :], T.msg[:, :, 64:68], "a_msg", "e12")
         for r in range(4):
-            H["g2w"] = tt(T.g2w[:, 64 * r:64 * r + 64], T.c1[:, :].indirect(T.cl0[:, :]), T.msg[:, SLOT * r:SLOT * r + 64], A.max, h)
+            H["g2w"] = tt(T.g2w[:, 64 * r:64 * r + 64], T.c1[:, :].indirect(T.cl0[:, :]), T.msg[:, r, 0:64], A.max, "c1", "cl0")
 
     def word_states():
-        H["y1"] = tt(T.y1[:, :], level1(T.cl2[:, :]), T.eet[:, :], A.mult, "cl2", "a_msg", "e12", "eet")
+        H["y1"] = tt(T.y1[:, :], T.c1[:, :].indirect(T.cl2[:, :]), T.eet[:, :], A.mult, "cl2", "c1", "eet")
 
     def level2_list():
-        h = ts(T.l2f[:, :], level1(T.cl1[:, 2:4]), 0.0, None, A.add, None, "a_msg", "e12", "cl1")
-        H["l2"] = copy(T.l2[:, :], T.l2f[:, 0:16], h)
+        H["l2"] = linear("s", T.l2[:, :], T.tc4[:, :, HEAD - 4:HEAD], 1, 0, "a_d4", "wb")
+
+    def level3_list(q="s"):
+        H["w3"] = linear(q, T.w3[:, :], T.tc4[:, :, 0:WE], 1, 0, "a_d4", "wb")
 
     def level2():
-        H["own2"] = copy(T.tab[:, 0:256].indirect(T.l2[:, :]), T.g2w[:, :], "g2w", "l2")
+        H["own2"] = act(T.tab[:, 0:256], T.g2w[:, :].indirect(T.l2[:, :]), F.Copy, ["g2w", "l2"])
 
     def level_cols(d, r):
         return T.tab[:, BASE[d] + 512 * r:BASE[d] + 512 * r + 512]
 
-    def cols3(r, late):
-        o = BASE[3] + 512 * r
-        return T.tab[:, o + EARLY:o + 512] if late else T.tab[:, o:o + EARLY]
+    def cols3(r, lo, hi):
+        return T.tab[:, BASE[3] + 512 * r + lo:BASE[3] + 512 * r + hi]
 
-    def late3():
-        H["late3"] = tt(cols3(R, True), T.g2w[:, :].indirect(T.wl[:, WE:32]), T.tc3b[:, :], A.max, "e3", "g2w", "wl")
-        out_to_ranks(cols3(R, True), "a_g3", "late3")
-        if not EARLY:
-            H["own3"] = H["late3"]
-
-    def lists3():
-        h = ts(T.w3f[:, :], T.tc3[:, :].indirect(T.cl3[:, :]), 0.0, None, A.add, None, "a_t3", "e3", "wb", "cl3")
-        H["w3"] = copy(T.w3[:, :], T.w3f[:, :], h)
+    def level3():
+        H["late3"] = tt(cols3(R, EARLY, 512), T.g2w[:, :].indirect(T.wl[:, WE:32]), T.tc3[:, :], A.max, "e3", "g2w", "wl")
+        out_to_ranks(cols3(R, EARLY, 512), "a_g3", "late3")
 
     def early3(r):
         off, hs = (T.wl[:, 0:WE], ["wl", "e3"]) if r == R else (T.w3[:, WE * r:WE * r + WE], ["w3"])
-        h = tt(cols3(r, False), T.g2w[:, :].indirect(off), T.tc3[:, SLOT3 * r + WE:SLOT3 * (r + 1)], A.max, "g2w", *hs)
-        made(3, h)
+        made(3, tt(cols3(r, 0, EARLY), T.g2w[:, :].indirect(off), T.tc4[:, r, WE:WE + EARLY], A.max, "g2w", *hs))
         if r == R:
-            assert EARLY == 512 or "late3" in H
-            H["own3"] = h
+            H["own3"] = H["tab3"][-1]
 
     def tabs(d):
-        levels = range(3 if EARLY else 4, d + 1)
-        assert all(len(H["tab%d" % k]) == 4 for k in levels)
-        return ["own2"] + (["late3", "a_g3"] if EARLY < 512 else []) + [h for k in levels for h in H["tab%d" % k]]
+        assert all(len(H["tab%d" % k]) == 4 for k in range(3, d + 1))
+        return ["own2", "late3", "a_g3"] + [h for k in range(3, d + 1) for h in H["tab%d" % k]]
 
     def source(d, r):
         return (T.tab[:, 0:BASE[d]].indirect(T["fl%d" % d][:, 32 * r:32 * r + 32]),
@@ -431,68 +422,77 @@ def rank_program(g, core, T, topo):
 
     def complete(d, r):
         src, hs = source(d, r)
-        made(d, tt(level_cols(d, r), src, T["tc%d" % d][:, 512 * r:512 * r + 512], A.max, pointers(d), *hs))
+        made(d, tt(level_cols(d, r), src, pointer_cols(T, d, r), A.max, *pointers(d), *hs))
 
-    def split_gather(d, r):
-        src, hs = source(d, r)
-        h = act(T.dx[:, :], src, F.Copy, hs + [H.get("dx")])
+    spare = {k: None for k in range(3)}
+
+    def split_gather(name, src, hs, other, ho):
+        k = list(spare)[0]
+        h = act(T.dx[:, 512 * k:512 * k + 512], src, F.Copy, list(hs) + [spare.pop(k)])
         b = free_bank()
-        wait("p", "ident", pointers(d), last.pop(b))
-        assert "split" not in H
-        H["split"] = (b, h, fin("p", P.matmul(T[b][:, :], T.ident[:, :], T["tc%d" % d][:, 512 * r:512 * r + 512], True, True)))
+        wait("p", "ident", last.pop(b), *ho)
+        H[name] = (k, b, h, fin("p", P.matmul(T[b][:, :], T.ident[:, :], other, True, True)))
 
-    def split_max(d, r):
-        b, h1, h2 = H.pop("split")
-        last[b] = H["dx"] = tt(level_cols(d, r), T.dx[:, :], T[b][:, :], A.max, h1, h2)
-        made(d, H["dx"])
+    def split_finish(name, out, op):
+        k, b, h1, h2 = H.pop(name)
+        last[b] = spare[k] = tt(out, T.dx[:, 512 * k:512 * k + 512], T[b][:, :], op, h1, h2)
+        return last[b]
+
+    def split_complete(d, r):
+        split_gather("split%d%d" % (d, r), *source(d, r), pointer_cols(T, d, r), pointers(d))
+
+    def split_completed(d, r):
+        made(d, split_finish("split%d%d" % (d, r), level_cols(d, r), A.max))
 
     def plain(q, r):
         src, hs = source(6, r)
         made(6, act(level_cols(6, r), src, F.Copy, hs) if q == "s" else copy(level_cols(6, r), src, *hs))
 
     def fail_rows(d):
-        wait("p", "xg%d" % d)
+        wait("p", *["xg%d" % k for k in range(3, d + 1)])
         assert d == 3 or "py%d" % (d - 1) in H
-        H["py%d" % d] = fin("p", P.matmul(T.py[:, :], sel(d - 3), T["xf%d" % d][:, :], d == 3, d == 7))
+        for i in range(512 * (d - 3) // 160, 512 * (d - 2) // 160):
+            H["py%d" % d] = fin("p", P.matmul(T.py[:, 0:160], sel(i), T.xf[:, 160 * i:160 * i + 160], i == 0, i == 15))
 
     def fail3():
-        H["xg3"] = act(T.xf3[:, :], T.y1[:, :].indirect(T.wl[:, :]), F.Copy, ["y1", "wl"])
+        H["xg3"] = act(T.xf[:, 0:512], T.y1[:, :].indirect(T.wl[:, :]), F.Copy, ["y1", "wl"])
 
     def fail_gather(d):
         j = (OWN[d] - 4) // 16
-        x = T["xf%d" % d]
+        o = 512 * (d - 3)
         if d == 4:
             src, hs = T.g2w[:, :].indirect(T.wl4[:, :]), ["g2w", "wl4"]
         else:
             src, hs = fail_cols(d - 1).indirect(T.pu[:, j:j + 32]), ["d%d" % (d - 1), "pu"]
-        H["xg%d" % d] = tt(x[:, :], src, mask_ap("l%d" % d), A.mult, "ml%d" % d, *hs)
-        H["xf%d" % d] = sums("pa", lambda i: x[:, i:512:16], 32, "xg%d" % d)
+        H["xg%d" % d] = tt(T.xf[:, o:o + 512], src, mask_ap("l%d" % d), A.mult, "ml%d" % d, *hs)
+        H["xf%d" % d] = sums("pa", lambda i: T.xf[:, o + i:o + 512:16], 32, "xg%d" % d)
 
     def fail_ln(d):
         last["pa"] = H["lnf%d" % d] = act(T.lnf[:, 32 * (d - 4):32 * (d - 3)], T.pa[:, 0:32], F.Ln, ["xf%d" % d])
 
-    def index(out, in_, shift, *hs):
-        return ts(out, in_, 1.0 / K, float(A0 + shift), A.mult, A.add, *hs)
+    def index(q, out, in_, shift, *hs):
+        return linear(q, out, in_, 1.0 / K, A0 + shift, *hs)
 
-    def fail_list(d):
+    def fail_list(d, q="v"):
         own = T["fl%d" % d][:, 32 * R:32 * R + 32]
-        src = T.lnf[:, 32 * (d - 4):32 * (d - 3)]
-        H["fl%d" % d] = index(own, src, 0, "lnf%d" % d)
+        H["fl%d" % d] = index(q, own, T.lnf[:, 32 * (d - 4):32 * (d - 3)], 0, "lnf%d" % d)
         if d < 7:
             out_to_ranks(own, "a_f%d" % d, "fl%d" % d)
-        else:
-            H["flp"] = index(T.flp[:, :], src, PAD[6] - BASE[6])
 
-    def xblock(name, n=1):
-        return T.xt[:, 512 * BLOCK[name]:512 * (BLOCK[name] + n)]
+    def fail_list_deep(q="v"):
+        H["flp"] = index(q, T.flp[:, :], T.lnf[:, 96:128], PAD - BASE[6], "lnf7")
 
-    def lnblock(name, n=1):
-        return T.ln[:, 32 * BLOCK[name]:32 * (BLOCK[name] + n)]
+    def xblock(name):
+        return T.xt[:, 512 * BLOCK[name]:512 * BLOCK[name] + 512]
 
-    def text_words():
-        h = ts(T.vf[:, 0:32], T.vi[:, 0:32], 16.0, None, A.mult, None, "ld_vi")
-        h = tt(T.vf[:, 32:64], T.vf[:, 0:32], T.vi[:, 32:64], A.add, h)
-        H["lt1"] = copy(T.lt[:, 32:64], T.vf[:, 32:64], h)
+    def lnblock(name):
+        k = BLOCK[name]
+        return T.ln[:, k:32 * RUN:RUN] if k < RUN else T.ln[:, 32 * k:32 * k + 32]
+
+    def text_words(q="v"):
+        h = linear(q, T.vf[:, 0:32], T.vi[:, 0:32], 16, 0, "ld_vi")
+        h = tt(T.vf[:, 32:64], T.vf[:, 0:32], T.vi[:, 32:64], A.add, h, "ld_vi")
+        H["lt1"] = linear(q, T.lt[:, 32:64], T.vf[:, 32:64], 1, 0, h)
 
     def text1():
         H["xt1"] = act(xblock("t1"), T.y1[:, :].indirect(T.lt[:, 32:64]), F.Copy, ["y1", "lt1"])
@@ -503,9 +503,18 @@ def rank_program(g, core, T, topo):
         src, hs = (T.g2w[:, :], ["g2w"]) if t == 2 else (T.tab[:, 0:BASE[d + 1]], tabs(d))
         H["xt%d" % t] = tt(xblock("t%d" % t), src.indirect(off), mask_ap("t%d" % t), A.mult, "lt%d" % (t - 1), "mt%d" % t, *hs)
 
+    def deep_source(off, h):
+        return T.tc6[:, :].indirect(off), [h, "e6", "fill"] + pointers(6)
+
     def deep_gather(t):
-        H["xp%d" % t] = tt(xblock("p%d" % t), T.tc6[:, :].indirect(T.ltp[:, 32 * t - 32:32 * t]), mask_ap("t%d" % t), A.mult,
-                           "ltp%d" % (t - 1), pointers(6), "e6", "fill", "mt%d" % t)
+        src, hs = deep_source(T.ltp[:, 32 * t - 32:32 * t], "ltp%d" % (t - 1))
+        H["xp%d" % t] = tt(xblock("p%d" % t), src, mask_ap("t%d" % t), A.mult, "mt%d" % t, *hs)
+
+    def split_deep(t):
+        split_gather("splitp%d" % t, *deep_source(T.ltp[:, 32 * t - 32:32 * t], "ltp%d" % (t - 1)), mask_ap("t%d" % t), ["mt%d" % t])
+
+    def split_deep_mask(t):
+        H["xp%d" % t] = split_finish("splitp%d" % t, xblock("p%d" % t), A.mult)
 
     def text_sums(*names):
         b = free_bank()
@@ -515,99 +524,87 @@ def rank_program(g, core, T, topo):
 
     def text_ln(name):
         b, h, names = H["s" + name]
-        last[b] = h = act(lnblock(name, len(names)), T[b][:, 0:32 * len(names)], F.Ln, [h])
-        for n in names:
-            H["ln" + n] = h
+        for k, n in reversed(list(enumerate(names))):
+            H["ln" + n] = act(lnblock(n), T[b][:, 32 * k:32 * k + 32], F.Ln, [h])
+        last[b] = H["ln" + name]
 
-    def text_list(t):
-        H["lt%d" % t] = index(T.lt[:, 32 * t:32 * t + 32], lnblock("t%d" % t), 0, "lnt%d" % t)
+    def text_list(t, q="v"):
+        H["lt%d" % t] = index(q, T.lt[:, 32 * t:32 * t + 32], lnblock("t%d" % t), 0, "lnt%d" % t)
 
-    def deep_list(t, n=1):
-        h = index(T.ltp[:, 32 * t:32 * (t + n)], lnblock("t%d" % t, n), PAD[6] - BASE[6], *["lnt%d" % k for k in range(t, t + n)])
-        for k in range(t, t + n):
-            H["ltp%d" % k] = h
-
-    def own_ap(d):
-        if d >= 6:
-            return T["g%d" % d][:, :]
-        if d == 1:
-            return T.msg[:, SLOT * R + 64:SLOT * R + 68]
-        return T.tab[:, BASE[d] + SIZE[d] * R:BASE[d] + SIZE[d] * R + SIZE[d]]
-
-    def number_step(q, k, out, in_, *hs):
-        if k == 1:
-            if q == "s":
-                return act(out, in_, F.Identity, hs, bias=float(MAGIC + A0), scale=1.0 / K)
-            return index(out, in_, MAGIC, *hs)
-        if q == "s":
-            return act(out, in_, F.Identity, hs, bias=float(FIRST - MAGIC))
-        return ts(out, in_, float(FIRST - MAGIC), None, A.add, None, *hs)
-
-    def yg_step(d, k, q="s"):
-        c = slice(0 if d == 3 and k else OWN[d], OWN[d] + SIZE[d])
-        if k == 0:
-            H["ya%d" % d] = act(T.ya[:, c], own_ap(d), F.Ln, ["e12" if d == 1 else "own%d" % d])
-        elif k == 1:
-            H["yb%d" % d] = number_step(q, 1, T.yb[:, c], T.ya[:, c], *(["ya1", "ya2", "ya3"] if d == 3 else ["ya%d" % d]))
-        else:
-            store(T.yg[:, c], T.yo[:, c], number_step(q, 2, T.yo[:, c], T.yb[:, c], "yb%d" % d))
-
-    def yf_low():
-        copy(T.yf12[:, 0:4], T.zz[:, 0:4], "zz")
-        h = ts(T.yf12[:, 4:68], T.lr[:, 0:64], 16.0, None, A.add, None, "ld_lr")
-        store(T.yf[:, 0:68], T.yf12[0:128:16, :], h)
-
-    def yf_step(k, q="s"):
-        if k == 0:
-            H["fa"] = act(T.fa[:, :], T.py[:, :], F.Ln, ["py7"], bias=TINY)
-        elif k == 1:
-            H["fb"] = number_step(q, 1, T.fb[:, :], T.fa[:, :], "fa")
-        else:
-            h = number_step(q, 2, T.fo[:, :], T.fb[:, :], "fb")
-            for d in range(3, 8):
-                store(T.yf[:, OWN[d]:OWN[d] + 512], T.fo[d - 3:128:16, :], h)
+    def deep_list(t, q="v"):
+        H["ltp%d" % t] = index(q, T.ltp[:, 32 * t:32 * t + 32], lnblock("t%d" % t), PAD - BASE[6], "lnt%d" % t)
 
     def level7_plain():
         H["h7"] = act(T.h7[:, :], T.tab[:, :].indirect(T.fl7[:, 32 * R:32 * R + 32]), F.Copy, tabs(6) + ["fl7"])
 
     def level7():
-        H["own7"] = tt(T.g7[:, :], T.tc6[:, :].indirect(T.flp[:, :]), T.h7[:, :], A.max, "h7", "flp", pointers(6), "e6", "fill")
+        src, hs = deep_source(T.flp[:, :], "flp")
+        H["own7"] = tt(T.g7[:, :], src, T.h7[:, :], A.max, "h7", *hs)
 
-    def largest(k):
-        if k == 1:
-            h = tt(T.rm[:, 0:128], T.ln[:, 0:128], T.ln[:, 128:256], A.max, *["lnt%d" % t for t in range(1, 9)])
-        elif k == 2:
-            h = tt(T.rm[:, 128:192], T.rm[:, 0:64], T.rm[:, 64:128], A.max, "rm1")
-        elif k == 3:
-            h = tt(T.rm[:, 0:64], T.rm[:, 128:192], lnblock("p6", 2), A.max, "rm2", "lnp6", "lnp7")
-        elif k == 4:
-            h = tt(T.rm[:, 64:96], T.rm[:, 0:32], T.rm[:, 32:64], A.max, "rm3")
+    def split_level7():
+        split_gather("split7", *deep_source(T.flp[:, :], "flp"), T.h7[:, :], ["h7"])
+
+    def split_level7_max():
+        H["own7"] = split_finish("split7", T.g7[:, :], A.max)
+
+    def own_ap(d):
+        if d >= 6:
+            return T["g%d" % d][:, :]
+        if d == 1:
+            return T.msg[:, R, 64:68]
+        return T.tab[:, BASE[d] + SIZE[d] * R:BASE[d] + SIZE[d] * R + SIZE[d]]
+
+    def number_step(q, k, out, in_, *hs):
+        return index(q, out, in_, MAGIC, *hs) if k == 1 else linear(q, out, in_, 1, FIRST - MAGIC, *hs)
+
+    def yg_step(d, k, q="s"):
+        c = slice(0 if d == 3 and k else OWN[d], OWN[d] + SIZE[d])
+        if k == 0:
+            H["ya%d" % d] = act(T.ya[:, c], own_ap(d), F.Ln, ["e12" if d == 1 else "own%d" % d] + ["late3"] * (d == 3))
+        elif k == 1:
+            H["yb%d" % d] = number_step(q, 1, T.yb[:, c], T.ya[:, c], *(["ya1", "ya2", "ya3"] if d == 3 else ["ya%d" % d]))
         else:
-            h = tt(T.rm[:, 96:128], T.rm[:, 64:96], lnblock("p8"), A.max, "rm4", "lnp8")
-        H["rm%d" % k] = h
+            store(T.yg[:, c], T.yo[:, c], number_step(q, 2, T.yo[:, c], T.yb[:, c], "yb%d" % d))
+
+    def yf_low(q="s"):
+        linear(q, T.yf12[:, 0:4], T.zz[:, 0:4], 1, 0, "zz")
+        store(T.yf[:, 0:68], T.yf12[0:128:16, :], linear(q, T.yf12[:, 4:68], T.lr[:, 0:64], 1, 16, "ld_lr"))
+
+    def yf_step(k, q="s"):
+        if k == 0:
+            H["fa"] = act(T.fa[:, :], T.py[:, 0:160], F.Ln, ["py7"])
+        elif k == 1:
+            H["fb"] = number_step(q, 1, T.fb[:, :], T.fa[:, :], "fa")
+        else:
+            store(T.yf[:, OWN[3]:OWN[7] + 512], T.fo[:, :], number_step(q, 2, T.fo[:, :], T.fb[:, :], "fb"))
+
+    def largest():
+        wait("v", "anew", *["ln" + n for n in BLOCK if BLOCK[n] < RUN])
+        H["rm"] = fin("v", V.tensor_tensor_scan(T.rm[:, :], T.anew[:, :], T.ln[:, 0:32 * RUN], 0.0, A.min, A.max))
 
     def text_out():
-        h = tt(T.last[:, 0:32], lnblock("t9"), lnblock("p9"), A.max, "lnt9", "lnp9")
-        h = tt(T.last[:, 32:64], T.rm[:, 96:128], T.last[:, 0:32], A.max, h, "rm5")
+        tt(T.last[:, 0:32], lnblock("t9"), lnblock("p9"), A.max, "lnt9", "lnp9")
+        h = tt(T.last[:, 32:64], T.rm[:, RUN - 1:32 * RUN:RUN], lnblock("t9"), A.max, "rm")
         h = number_step("v", 1, T.lastm[:, :], T.last[:, :], h)
         h = number_step("v", 2, T.oy[:, :], T.lastm[:, :], h)
         store(T.yl[:, :], T.oy[:, 0:32], h)
-        store(T.ym[:, :], T.oy[:, 32:64], h)
+        store(T.ym[:, :], T.oy[:, 32:64], h, "s")
 
     steps = {
-        "first": first_message, "maskc": mask_constants, "wordc": word_constants, "weights": mask_weights,
-        "float": to_float, "code": to_code, "helper": to_helper, "send": to_ranks,
+        "first": first_message, "sumc": sum_constants, "scanc": scan_constants, "maskc": mask_constants, "wordc": word_constants,
+        "weights": mask_weights, "code": to_code, "helper": to_helper, "send": to_ranks,
         "words": words, "wordlist": words_list, "words4": words4, "wordlist4": words4_list,
-        "letters": letters, "squares": squares, "pe": mask_pe, "mask": mask_out,
-        "g2w": word_table, "y1": word_states, "list2": level2_list, "level2": level2,
-        "late3": late3, "lists3": lists3, "early3": lambda k: early3((rest + [R])[k]),
+        "squares": squares, "pe": mask_pe, "mask": mask_out,
+        "g2w": word_table, "y1": word_states, "list2": level2_list, "level2": level2, "late3": level3,
+        "list3": level3_list, "early3": lambda k: early3((rest + [R])[k]),
         "D": fail_columns, "own_pe": own_pe, "own": complete_own, "other": lambda d, k: complete(d, rest[k]),
-        "sgather": lambda d, k: split_gather(d, rest[k]), "smax": lambda d, k: split_max(d, rest[k]),
+        "sother": lambda d, k: split_complete(d, rest[k]), "mother": lambda d, k: split_completed(d, rest[k]),
         "plain": lambda q, k: plain(q, rest[k]),
-        "rows": fail_rows, "fail3": fail3, "fail": fail_gather, "fln": fail_ln, "flist": fail_list,
-        "twords": text_words, "text1": text1, "text": text_gather, "deep": deep_gather, "sums": text_sums, "ln": text_ln,
-        "tlist": text_list, "dlist": deep_list, "yg": yg_step, "yf12": yf_low, "yf": yf_step,
-        "h7": level7_plain, "g7": level7, "max": largest, "out": text_out,
+        "rows": fail_rows, "fail3": fail3, "fail": fail_gather, "fln": fail_ln, "flist": fail_list, "plist": fail_list_deep,
+        "twords": text_words, "text1": text1, "text": text_gather, "deep": deep_gather, "sdeep": split_deep, "mdeep": split_deep_mask,
+        "sums": text_sums, "ln": text_ln, "tlist": text_list, "dlist": deep_list,
+        "h7": level7_plain, "g7": level7, "sg7": split_level7, "mg7": split_level7_max,
+        "yg": yg_step, "yf12": yf_low, "yf": yf_step, "max": largest, "out": text_out,
     }
     for step in ORDER.split():
         name, *args = step.split(".")

from concourse.bass import DstId, RemoteDMATransfer
from concourse.mybir import AluOpType as A, ActivationFunctionType as F

K = 0.008435
A0 = 5248
FIRST = 32
MAGIC = 12582912
SIZE = {1: 4, 2: 64, 3: 512, 4: 512, 5: 512, 6: 512, 7: 512}
OWN = {1: 0, 2: 4, 3: 68, 4: 580, 5: 1092, 6: 1604, 7: 2116}
BASE = {2: 0, 3: 256, 4: 2304, 5: 4352, 6: 6400, 7: 8448}
SLOT = 72
PAD = 16
EARLY = 256
WE = EARLY // 16
HEAD = WE + EARLY + 4
DIRECT = {4: 256, 5: 0, 6: 0}
BLOCK = {"t1": 0, "t2": 1, "t3": 2, "t4": 3, "t5": 4, "t6": 5, "t7": 6, "t8": 7, "p6": 8, "p7": 9, "p8": 10, "p9": 11, "t9": 12}
RUN = 12
ORDER = """
first maskc sumc code.3 squares.l code.4 words squares.t code.5 weights.v yf12.v wordlist helper.4 send.4 helper.5
pe.l4 pe.l6 pe.l5 pe.t2 mask.l6 mask.l4.v pe.t3 mask.l5.v pe.t8 pe.t7 twords.s mask.t2.v words4 wordc
g2w y1 late3 code.6 helper.6 scanc own_pe.4 wordlist4.v pe.l7 early3.3 fail.4 text.2 yg.1.0 text1 mask.l7.v mask.t3 mask.t7 fln.4
list3 early3.0 sums.t1.t2 early3.1 list2 flist.4.s early3.2 level2 yg.3.0 ln.t1 tlist.2.s
text.3 yg.2.0 pe.t4 D.4 sums.t3 own.4 yg.3.1 fail3 ln.t3 fail.5 yg.3.2 own_pe.5 other.4.2 tlist.3.s other.4.0 fln.5 other.4.1
pe.t5 mask.t4 text.4 flist.5.s yg.4.0
D.5 pe.t6 rows.3 fail.6 mask.t8 mask.t5 sums.t4 yg.4.1 fln.6 flist.6.s own.5 rows.4 rows.5 yg.5.0 ln.t4 mask.t6 other.5.2 pe.t9
own_pe.6 yg.4.2 tlist.4.s mask.t9 other.5.0 other.5.1
D.6 text.5 sums.t5 rows.6 plain.s.1 fail.7 plain.v.0 ln.t5 plain.s.2 fln.7 tlist.5.s rows.7 flist.7.s own.6
text.6 plist.s h7 sums.t6 g7 yg.5.1 ln.t6 dlist.5.s tlist.6.s yg.5.2 dlist.6.s yg.6.0 text.7 yf.0 deep.7 sums.t7 ln.t7 deep.6
tlist.7.s yg.6.1 dlist.7.s text.8 yg.7.0 deep.8 yg.6.2 sums.t8 ln.t8 dlist.8.s tlist.8.s yf.1 deep.9 yg.7.1 sums.p6.p7.p8 yf.2
sums.p9 text.9 ln.p6 ln.p9 yg.7.2 max sums.t9 ln.t9 out
"""


def _sb(cols, dtype):
    return ("sbuf", [128, cols], dtype)


SCRATCH = {
    "tab": _sb(8448, "bfloat16"), "msg": ("sbuf", [128, 4, SLOT], "bfloat16"), "c1": _sb(16, "bfloat16"),
    "g2w": _sb(256, "bfloat16"), "y1": _sb(256, "bfloat16"),
    "ti12": _sb(68, "int32"), "l1": _sb(4, "uint16"), "l2f": _sb(16, "float32"), "l2": _sb(16, "uint16"),
    "lr": _sb(576, "int32"), "w1": _sb(16, "bfloat16"), "w2": _sb(64, "bfloat16"), "xw": _sb(576, "bfloat16"), "wl": _sb(32, "uint16"),
    "xw4": _sb(512, "bfloat16"), "wl4": _sb(32, "uint16"), "pari": _sb(164, "int32"), "pu": _sb(164, "uint16"),
    "li": _sb(768, "int32"), "lq": _sb(768, "bfloat16"), "maskl": _sb(2048, "bfloat16"), "maskt": _sb(4096, "bfloat16"),
    "vi": _sb(64, "int32"), "vf": _sb(64, "float32"),
    "lt": _sb(288, "uint16"), "ltp": _sb(288, "uint16"), "flp": _sb(32, "uint16"),
    "xt": _sb(13 * 512, "bfloat16"), "ln": _sb(13 * 32, "float32"), "xf": _sb(2560, "bfloat16"), "lnf": _sb(128, "float32"),
    "rm": _sb(32 * RUN, "float32"), "anew": _sb(32 * RUN, "float32"),
    "last": _sb(64, "float32"), "lastm": _sb(64, "float32"), "oy": _sb(64, "float32"),
    "zz": _sb(16, "float32"), "yf12": _sb(68, "float32"), "fa": _sb(160, "float32"), "fb": _sb(160, "float32"), "fo": _sb(160, "float32"),
    "w3": _sb(4 * WE, "uint16"), "tc3": _sb(512 - EARLY, "bfloat16"), "tc4": ("sbuf", [128, 4, -(-(HEAD + 512) // 8) * 8], "bfloat16"), "tc5": _sb(2048, "bfloat16"),
    "tc6": _sb(PAD + 2048, "bfloat16"), "d4": _sb(512, "bfloat16"), "d5": _sb(512, "bfloat16"), "dx": _sb(1536, "bfloat16"),
    "g6": _sb(512, "bfloat16"), "h7": _sb(512, "bfloat16"), "g7": _sb(512, "bfloat16"),
    "ya": _sb(2628, "float32"), "yb": _sb(2628, "float32"), "yo": _sb(2628, "float32"),
    "pi": _sb(4, "int32"), "pf": _sb(4, "float32"), "pd": _sb(8, "float32"),
    "rown": _sb(144, "bfloat16"), "rowc": _sb(256, "bfloat16"), "cl2i": _sb(16, "int32"),
    "cl0": _sb(4, "uint16"), "cl2": _sb(16, "uint16"),
    "zs": _sb(144, "bfloat16"), "ident": _sb(128, "bfloat16"), "eet": _sb(256, "bfloat16"), "e2": _sb(8, "float32"),
    "b0": _sb(128, "bfloat16"), "blk": _sb(128, "bfloat16"), "b1": _sb(128, "bfloat16"), "wr": _sb(1024, "bfloat16"),
}
for _d in range(3, 7):
    SCRATCH["ti%d" % _d] = _sb(512, "int32")
for _d in range(4, 8):
    SCRATCH["fl%d" % _d] = _sb(128, "uint16")
BANKS = ("pm0", "pm1", "pm2", "pm3", "pm4", "po", "pa", "py")
for _b in BANKS:
    SCRATCH[_b] = ("psum", [128, 512], "float32")

LOADS = ["ti12", "ti3", "par", "lr", "ti4", "ti5", "ti6", "ll", "lt", "vi"]
SEMAPHORES = (["v", "s", "p", "gc", "out", "sent", "a_msg", "a_g3", "a_d4"] + ["ld_" + n for n in LOADS]
              + ["a_t%d" % d for d in range(4, 7)] + ["a_f%d" % d for d in range(4, 7)] + ["h%d" % d for d in range(4, 7)])


def helper_of(core, ranks, topo):
    for h in topo.cores_of(core):
        if h != core and topo.die(h) != topo.die(core) and all(topo.may_write(h, r) for r in ranks if r != core):
            return h
    return None


def others_of(T, r):
    n = len(T.cores)
    return [T.cores[(r + k) % n] for k in range(1, n)]


def pointer_cols(T, d, r, lo=0, hi=512):
    if d == 4:
        return T.tc4[:, r, HEAD + lo:HEAD + hi]
    o = 512 * r + (PAD if d == 6 else 0)
    return T["tc%d" % d][:, o + lo:o + hi]


def part(T, d, r, relayed):
    return pointer_cols(T, d, r, DIRECT[d], 512) if relayed else pointer_cols(T, d, r, -HEAD, DIRECT[d])


def bits(engines):
    m = 0
    for e in engines:
        m |= 1 << e
    return m


def dst_id(c, topo):
    rid, pid, _ = topo.addr(c)
    return DstId(rid=rid, pnc=pid)


def send(g, T, topo, core, dsts, ap, sem):
    g.remote_dma_fused([RemoteDMATransfer(dst_ids=[dst_id(c, topo) for c in dsts], dma_engine_mask=topo.mask(core, dsts[0]),
                                          remote_sem=T.sem[sem], srcs=[ap], dsts=[ap for c in dsts], alu_op=0)],
                       local_sem=T.sem["sent"])
    return len(topo.engines(core, dsts[0]))


def helper_program(g, core, T, topo, r):
    own = T.cores[r]
    others = others_of(T, r)
    near = spare_engines(own, core, others[0], topo)
    n = 0
    for d in range(4, 7):
        g.wait_ge(T.sem["h%d" % d], len(near))
        n += send(g, T, topo, core, others, part(T, d, r, True), "a_t%d" % d)
    g.wait_ge(T.sem["sent"], n)


def spare_engines(core, helper, other, topo):
    far = set(topo.engines(core, other))
    return [e for e in topo.engines(core, helper) if e not in far]


def rank_program(g, core, T, topo):
    rank = T.rank_of(core)
    if rank is None:
        for i, c in enumerate(T.cores):
            if helper_of(c, T.cores, topo) == core:
                helper_program(g, core, T, topo, i)
        return
    R = rank
    others = others_of(T, R)
    rest = [r for r in range(4) if r != R]
    helper = helper_of(core, T.cores, topo)
    V, S, P = g.vector, g.scalar, g.tensor
    queue = {"v": V, "s": S, "p": P, "gc": g, "y": g.sync}
    cnt = {"v": 0, "s": 0, "p": 0, "gc": 0, "out": 0, "sent": 0}
    seen = {}
    H = {}
    last = {b: None for b in BANKS}

    def free_bank():
        return [b for b in last if b.startswith("pm")][0]

    def wait(q, *hs):
        for h in hs:
            if h is None:
                continue
            sem, val = H[h] if isinstance(h, str) else h
            if seen.get((q, sem), 0) < val:
                queue[q].wait_ge(T.sem[sem], val)
                seen[(q, sem)] = val

    def fin(q, ins):
        cnt[q] += 1
        ins.then_inc(T.sem[q], 1)
        return (q, cnt[q])

    def ts(out, in_, s1, s2, op0, op1, *hs):
        wait("v", *hs)
        return fin("v", V.tensor_scalar(out, in_, s1, None, op0) if op1 is None else V.tensor_scalar(out, in_, s1, s2, op0, op1))

    def tt(out, a, b, op, *hs):
        wait("v", *hs)
        return fin("v", V.tensor_tensor(out, a, b, op))

    def copy(out, in_, *hs):
        wait("v", *hs)
        return fin("v", V.tensor_copy(out, in_))

    def act(out, in_, func, hs, **kw):
        wait("s", *hs)
        return fin("s", S.activation(out, in_, func, **kw))

    def linear(q, out, in_, scale, bias, *hs):
        if q == "s":
            return act(out, in_, F.Identity, hs, bias=float(bias), scale=float(scale))
        return ts(out, in_, float(scale), float(bias), A.mult, A.add, *hs)

    def load(name, pairs):
        for out, in_ in pairs:
            g.sync.dma_start(out, in_).then_inc(T.sem["ld_" + name], 16)
        H["ld_" + name] = ("ld_" + name, 16 * len(pairs))

    def store(out, in_, h, q="y"):
        wait(q, h)
        queue[q].dma_start(out, in_).then_inc(T.sem["out"], 16)
        cnt["out"] += 16

    H["zz"] = fin("v", V.memset(T.zz[:, :], 0.0))
    H["lr0"] = fin("v", V.memset(T.lr[:, :], 0))
    load("ti12", [(T.ti12[:, :], T.tri[:, 0:68])])
    load("ti3", [(T.ti3[:, :], T.tri[:, OWN[3]:OWN[4]])])
    load("par", [(T.pari[:, :], T.par[:, :])])
    wait("y", "lr0")
    load("lr", [(T.lr[0:128:16, :], T.let[:, 0:576])])
    load("ll", [(T.li[k:128:2, 512:768], T.let[:, 576:2624]) for k in range(2)])
    load("ti4", [(T.ti4[:, :], T.tri[:, OWN[4]:OWN[5]])])
    load("lt", [(T.li[k:128:2, 0:512], T.txt[:, 1024:5120]) for k in range(2)])
    for d in (5, 6):
        load("ti%d" % d, [(T["ti%d" % d][:, :], T.tri[:, OWN[d]:OWN[d + 1]])])
    load("vi", [(T.vi[:, 32 * t:32 * t + 32], T.txt[:, 512 * t:512 * t + 512]) for t in range(2)])

    def code(out, in_, *hs):
        return act(out, in_, F.Exp, hs, bias=-K * (FIRST + A0), scale=K)

    H["fill"] = code(T.tc6[:, 0:PAD], T.zz[:, :], "zz")

    flag = {"allow_small_or_imprecise_dtypes": True}
    H["pcol"] = fin("gc", g.iota(T.pi[:, 0:1], [[0, 1]], 0, 1))
    H["rowc"] = fin("gc", g.iota(T.rowc[:, :], [[0, 16], [1, 16]], 0, 0, **flag))
    H["rown"] = fin("gc", g.iota(T.rown[:, :], [[1, 144]], 0, 0, **flag))
    H["cl2i"] = fin("gc", g.iota(T.cl2i[:, :], [[1, 16]], 0, 0))
    H["w1"] = fin("gc", g.iota(T.w1[:, :], [[1, 16]], 4 * R, 0, **flag))
    p0 = T.pi[:, 0:1]
    ts(T.pi[:, 1:2], p0, 15, None, A.bitwise_and, None, "pcol")
    ts(T.pi[:, 2:3], p0, 15, 1, A.bitwise_and, A.logical_shift_right)
    h = ts(T.pi[:, 3:4], p0, 1, None, A.bitwise_and, None)
    H["pf"] = copy(T.pf[:, :], T.pi[:, :], h)
    pp, cc, half, odd = [T.pf[:, k:k + 1] for k in range(4)]
    h = ts(T.pd[:, 3:4], odd, 2.0, -1.0, A.mult, A.add, "pf")
    h = ts(T.b0[:, :], T.rowc[:, 0:128], T.pd[:, 3:4], odd, A.mult, A.add, h, "rowc")
    wait("gc", h)
    h = fin("gc", g.affine_select(T.blk[:, :], T.b0[:, :], [[-16, 8], [0, 16]], A.is_ge, 0.0, 0, 1))
    wait("gc", h)
    H["b1"] = fin("gc", g.affine_select(T.b1[:, :], T.blk[:, :], [[16, 8], [0, 16]], A.is_ge, 0.0, 15, -1))

    def sum_constants():
        h = ts(T.pd[:, 0:1], pp, cc, 15.0, A.subtract, A.add)
        H["e2"] = ts(T.e2[:, :], T.rowc[:, 0:8], half, None, A.is_equal, None)
        H["zs"] = ts(T.zs[:, :], T.rown[:, :], T.pd[:, 0:1], None, A.is_equal, None, h, "rown")

    def mask_constants():
        H["even"] = ts(T.pd[:, 4:5], odd, -1.0, 1.0, A.mult, A.add)
        H["cq"] = ts(T.pd[:, 5:6], cc, 1.0, cc, A.add, A.mult)
        H["bq"] = ts(T.pd[:, 6:7], T.pd[:, 5:6], -1.0, 1.0, A.mult, A.add, "cq")

    def scan_constants():
        H["anew"] = fin("gc", g.iota(T.anew[:, :], [[0, 32], [2000, RUN]], -1000, 0, **flag))

    def word_constants():
        H["cl0"] = ts(T.cl0[:, :], T.zz[:, 0:4], cc, None, A.add, None, "zz")
        H["cl2"] = copy(T.cl2[:, :], T.cl2i[:, :], "cl2i")
        H["eet"] = ts(T.eet[:, :], T.rowc[:, :], cc, None, A.is_equal, None, "rowc")
        H["ident"] = ts(T.ident[:, :], T.rown[:, 0:128], pp, None, A.is_equal, None, "rown")

    def mask_weights(q="s"):
        for r in range(8):
            out, col = T.wr[:, 128 * r:128 * r + 128], T.e2[:, r:r + 1]
            if q == "s":
                H["wr"] = act(out, T.b1[:, :], F.Copy, ["b1", "e2"], scale=col)
            else:
                H["wr"] = ts(out, T.b1[:, :], col, None, A.mult, None, "b1", "e2")

    def sel(i):
        return T.zs[:, 15 - i:143 - i]

    def out_to_ranks(ap, sem, *hs):
        wait("gc", *hs)
        cnt["sent"] += send(g, T, topo, core, others, ap, sem)
        arrives(sem, core)

    def arrives(sem, sender):
        H[sem] = (sem, len(others) * len(topo.engines(sender, others[0])))

    def own_tc(d):
        return pointer_cols(T, d, R)

    def to_code(d):
        if d == 3:
            code(T.tc4[:, R, WE:WE + EARLY], T.ti3[:, 0:EARLY], "ld_ti3")
            H["e3"] = code(T.tc3[:, :], T.ti3[:, EARLY:512])
        else:
            H["e%d" % d] = code(own_tc(d), T["ti%d" % d][:, :], "ld_ti%d" % d)

    def to_ranks(d):
        out_to_ranks(part(T, d, R, False), "a_d%d" % d, "e3", "e%d" % d, "wb")

    def to_helper(d):
        eng = spare_engines(core, helper, others[0], topo)
        wait("gc", "e%d" % d)
        rid, pid, _ = topo.addr(helper)
        g.remote_dma(part(T, d, R, True), part(T, d, R, True), T.sem["h%d" % d], T.sem["sent"], pid, rid, bits(eng))
        cnt["sent"] += len(eng)
        arrives("a_t%d" % d, helper)

    def pointers(d):
        return ["a_t%d" % d] + (["a_d%d" % d] if DIRECT[d] else [])

    def first_message():
        h = ts(T.l1[:, :], T.ti12[:, 0:4], float(4 - FIRST - 64 * R), None, A.add, None, "ld_ti12")
        code(T.msg[:, R, 64:68], T.ti12[:, 0:4], "ld_ti12")
        H["e12"] = code(T.msg[:, R, 0:64], T.ti12[:, :].indirect(T.l1[:, :]), h)
        out_to_ranks(T.msg[:, R, 0:68], "a_msg", "e12")

    def sums(bank, x, n, *hs):
        wait("p", "zs", last.pop(bank), *hs)
        for i in range(16):
            h = fin("p", P.matmul(T[bank][:, 0:n], sel(i), x(i), i == 0, i == 15))
        return h

    def words():
        H["pu"] = copy(T.pu[:, :], T.pari[:, :], "ld_par")
        H["w2"] = ts(T.w2[:, :], T.lr[:, 0:64], 16.0, None, A.mult, None, "ld_lr")
        tt(T.xw[:, 0:64], T.w1[:, :].indirect(T.pu[:, 0:4]), T.lr[:, 0:64], A.add, "w1", "pu")
        H["xw3"] = tt(T.xw[:, 64:576], T.w2[:, :].indirect(T.pu[:, 4:36]), T.lr[:, 64:576], A.add, "w2")
        H["xw"] = sums("pa", lambda i: T.xw[:, i:576:16], 36, "xw3")

    def words_list():
        copy(pointer_cols(T, 4, R, -4, 0), T.pa[:, 0:4], "xw")
        H["wb"] = copy(T.tc4[:, R, 0:WE], T.pa[:, 4:4 + WE])
        last["pa"] = H["wl"] = copy(T.wl[:, :], T.pa[:, 4:36])

    def words4():
        h = act(T.xw4[:, :], T.xw[:, 64:576].indirect(T.pu[:, 36:68]), F.Copy, ["xw3"])
        H["xw4"] = sums("pa", lambda i: T.xw4[:, i:512:16], 32, h)

    def words4_list(q="v"):
        last["pa"] = H["wl4"] = linear(q, T.wl4[:, :], T.pa[:, 0:32], 1, 0, "xw4")

    def squares(k):
        c = slice(512, 768) if k == "l" else slice(0, 512)
        H["lq" + k] = act(T.lq[:, c], T.li[:, c], F.Square, ["ld_l" + k, "even"], bias=T.pd[:, 4:5])

    def mask_pe(name):
        b = free_bank()
        k = int(name[1])
        wait("p", "wr", "lq" + name[0], last.pop(b))
        if name[0] == "l":
            for u in range(2):
                r = 2 * (k - 4) + u
                h = fin("p", P.matmul(T[b][:, 256 * u:256 * u + 256], T.wr[:, 128 * r:128 * r + 128], T.lq[:, 512:768], True, True))
        else:
            r = k - 2
            for i in range(16):
                h = fin("p", P.matmul(T[b][:, i:512:16], T.wr[:, 128 * r:128 * r + 128], T.lq[:, 32 * i:32 * i + 32], True, True))
        H["pm" + name] = (b, h)

    def mask_ap(name):
        k = int(name[1])
        return T.maskl[:, 512 * (k - 4):512 * (k - 3)] if name[0] == "l" else T.maskt[:, 512 * (k - 2):512 * (k - 1)]

    def mask_out(name, q="s"):
        b, h = H["pm" + name]
        if q == "s":
            h = act(mask_ap(name), T[b][:, :], F.Relu, [h, "bq"], bias=T.pd[:, 6:7], scale=-1.0)
        else:
            h = ts(mask_ap(name), T[b][:, :], T.pd[:, 5:6], 0.0, A.add, A.is_equal, h, "cq")
        last[b] = H["m" + name] = h

    def word_table():
        H["c1"] = copy(T.c1[:, :], T.msg[:, :, 64:68], "a_msg", "e12")
        for r in range(4):
            H["g2w"] = tt(T.g2w[:, 64 * r:64 * r + 64], T.c1[:, :].indirect(T.cl0[:, :]), T.msg[:, r, 0:64], A.max, "c1", "cl0")

    def word_states():
        H["y1"] = tt(T.y1[:, :], T.c1[:, :].indirect(T.cl2[:, :]), T.eet[:, :], A.mult, "cl2", "c1", "eet")

    def level2_list():
        H["l2"] = linear("s", T.l2[:, :], T.tc4[:, :, HEAD - 4:HEAD], 1, 0, "a_d4", "wb")

    def level3_list(q="s"):
        H["w3"] = linear(q, T.w3[:, :], T.tc4[:, :, 0:WE], 1, 0, "a_d4", "wb")

    def level2():
        H["own2"] = act(T.tab[:, 0:256], T.g2w[:, :].indirect(T.l2[:, :]), F.Copy, ["g2w", "l2"])

    def level_cols(d, r):
        return T.tab[:, BASE[d] + 512 * r:BASE[d] + 512 * r + 512]

    def cols3(r, lo, hi):
        return T.tab[:, BASE[3] + 512 * r + lo:BASE[3] + 512 * r + hi]

    def level3():
        H["late3"] = tt(cols3(R, EARLY, 512), T.g2w[:, :].indirect(T.wl[:, WE:32]), T.tc3[:, :], A.max, "e3", "g2w", "wl")
        out_to_ranks(cols3(R, EARLY, 512), "a_g3", "late3")

    def early3(r):
        off, hs = (T.wl[:, 0:WE], ["wl", "e3"]) if r == R else (T.w3[:, WE * r:WE * r + WE], ["w3"])
        made(3, tt(cols3(r, 0, EARLY), T.g2w[:, :].indirect(off), T.tc4[:, r, WE:WE + EARLY], A.max, "g2w", *hs))
        if r == R:
            H["own3"] = H["tab3"][-1]

    def tabs(d):
        assert all(len(H["tab%d" % k]) == 4 for k in range(3, d + 1))
        return ["own2", "late3", "a_g3"] + [h for k in range(3, d + 1) for h in H["tab%d" % k]]

    def source(d, r):
        return (T.tab[:, 0:BASE[d]].indirect(T["fl%d" % d][:, 32 * r:32 * r + 32]),
                tabs(d - 1) + ["fl%d" % d if r == R else "a_f%d" % d])

    def made(d, h):
        H.setdefault("tab%d" % d, []).append(h)

    def fail_cols(d):
        return level_cols(6, R) if d == 6 else T["d%d" % d][:, :]

    def fail_columns(d):
        src, hs = source(d, R)
        H["d%d" % d] = act(fail_cols(d), src, F.Copy, hs)
        if d == 6:
            made(6, H["d6"])

    def own_pe(d):
        wait("p", "ident", "e%d" % d, last.pop("po"))
        H["po%d" % d] = fin("p", P.matmul(T.po[:, :], T.ident[:, :], own_tc(d), True, True))

    def complete_own(d):
        out = T.g6[:, :] if d == 6 else level_cols(d, R)
        last["po"] = H["own%d" % d] = tt(out, fail_cols(d), T.po[:, :], A.max, "d%d" % d, "po%d" % d)
        if d < 6:
            made(d, H["own%d" % d])

    def complete(d, r):
        src, hs = source(d, r)
        made(d, tt(level_cols(d, r), src, pointer_cols(T, d, r), A.max, *pointers(d), *hs))

    spare = {k: None for k in range(3)}

    def split_gather(name, src, hs, other, ho):
        k = list(spare)[0]
        h = act(T.dx[:, 512 * k:512 * k + 512], src, F.Copy, list(hs) + [spare.pop(k)])
        b = free_bank()
        wait("p", "ident", last.pop(b), *ho)
        H[name] = (k, b, h, fin("p", P.matmul(T[b][:, :], T.ident[:, :], other, True, True)))

    def split_finish(name, out, op):
        k, b, h1, h2 = H.pop(name)
        last[b] = spare[k] = tt(out, T.dx[:, 512 * k:512 * k + 512], T[b][:, :], op, h1, h2)
        return last[b]

    def split_complete(d, r):
        split_gather("split%d%d" % (d, r), *source(d, r), pointer_cols(T, d, r), pointers(d))

    def split_completed(d, r):
        made(d, split_finish("split%d%d" % (d, r), level_cols(d, r), A.max))

    def plain(q, r):
        src, hs = source(6, r)
        made(6, act(level_cols(6, r), src, F.Copy, hs) if q == "s" else copy(level_cols(6, r), src, *hs))

    def fail_rows(d):
        wait("p", *["xg%d" % k for k in range(3, d + 1)])
        assert d == 3 or "py%d" % (d - 1) in H
        for i in range(512 * (d - 3) // 160, 512 * (d - 2) // 160):
            H["py%d" % d] = fin("p", P.matmul(T.py[:, 0:160], sel(i), T.xf[:, 160 * i:160 * i + 160], i == 0, i == 15))

    def fail3():
        H["xg3"] = act(T.xf[:, 0:512], T.y1[:, :].indirect(T.wl[:, :]), F.Copy, ["y1", "wl"])

    def fail_gather(d):
        j = (OWN[d] - 4) // 16
        o = 512 * (d - 3)
        if d == 4:
            src, hs = T.g2w[:, :].indirect(T.wl4[:, :]), ["g2w", "wl4"]
        else:
            src, hs = fail_cols(d - 1).indirect(T.pu[:, j:j + 32]), ["d%d" % (d - 1), "pu"]
        H["xg%d" % d] = tt(T.xf[:, o:o + 512], src, mask_ap("l%d" % d), A.mult, "ml%d" % d, *hs)
        H["xf%d" % d] = sums("pa", lambda i: T.xf[:, o + i:o + 512:16], 32, "xg%d" % d)

    def fail_ln(d):
        last["pa"] = H["lnf%d" % d] = act(T.lnf[:, 32 * (d - 4):32 * (d - 3)], T.pa[:, 0:32], F.Ln, ["xf%d" % d])

    def index(q, out, in_, shift, *hs):
        return linear(q, out, in_, 1.0 / K, A0 + shift, *hs)

    def fail_list(d, q="v"):
        own = T["fl%d" % d][:, 32 * R:32 * R + 32]
        H["fl%d" % d] = index(q, own, T.lnf[:, 32 * (d - 4):32 * (d - 3)], 0, "lnf%d" % d)
        if d < 7:
            out_to_ranks(own, "a_f%d" % d, "fl%d" % d)

    def fail_list_deep(q="v"):
        H["flp"] = index(q, T.flp[:, :], T.lnf[:, 96:128], PAD - BASE[6], "lnf7")

    def xblock(name):
        return T.xt[:, 512 * BLOCK[name]:512 * BLOCK[name] + 512]

    def lnblock(name):
        k = BLOCK[name]
        return T.ln[:, k:32 * RUN:RUN] if k < RUN else T.ln[:, 32 * k:32 * k + 32]

    def text_words(q="v"):
        h = linear(q, T.vf[:, 0:32], T.vi[:, 0:32], 16, 0, "ld_vi")
        h = tt(T.vf[:, 32:64], T.vf[:, 0:32], T.vi[:, 32:64], A.add, h, "ld_vi")
        H["lt1"] = linear(q, T.lt[:, 32:64], T.vf[:, 32:64], 1, 0, h)

    def text1():
        H["xt1"] = act(xblock("t1"), T.y1[:, :].indirect(T.lt[:, 32:64]), F.Copy, ["y1", "lt1"])

    def text_gather(t):
        off = T.lt[:, 32 * t - 32:32 * t]
        d = min(t, 6)
        src, hs = (T.g2w[:, :], ["g2w"]) if t == 2 else (T.tab[:, 0:BASE[d + 1]], tabs(d))
        H["xt%d" % t] = tt(xblock("t%d" % t), src.indirect(off), mask_ap("t%d" % t), A.mult, "lt%d" % (t - 1), "mt%d" % t, *hs)

    def deep_source(off, h):
        return T.tc6[:, :].indirect(off), [h, "e6", "fill"] + pointers(6)

    def deep_gather(t):
        src, hs = deep_source(T.ltp[:, 32 * t - 32:32 * t], "ltp%d" % (t - 1))
        H["xp%d" % t] = tt(xblock("p%d" % t), src, mask_ap("t%d" % t), A.mult, "mt%d" % t, *hs)

    def split_deep(t):
        split_gather("splitp%d" % t, *deep_source(T.ltp[:, 32 * t - 32:32 * t], "ltp%d" % (t - 1)), mask_ap("t%d" % t), ["mt%d" % t])

    def split_deep_mask(t):
        H["xp%d" % t] = split_finish("splitp%d" % t, xblock("p%d" % t), A.mult)

    def text_sums(*names):
        b = free_bank()
        o = 512 * BLOCK[names[0]]
        h = sums(b, lambda i: T.xt[:, o + i:o + 512 * len(names):16], 32 * len(names), *["x" + n for n in names])
        H["s" + names[0]] = (b, h, names)

    def text_ln(name):
        b, h, names = H["s" + name]
        for k, n in reversed(list(enumerate(names))):
            H["ln" + n] = act(lnblock(n), T[b][:, 32 * k:32 * k + 32], F.Ln, [h])
        last[b] = H["ln" + name]

    def text_list(t, q="v"):
        H["lt%d" % t] = index(q, T.lt[:, 32 * t:32 * t + 32], lnblock("t%d" % t), 0, "lnt%d" % t)

    def deep_list(t, q="v"):
        H["ltp%d" % t] = index(q, T.ltp[:, 32 * t:32 * t + 32], lnblock("t%d" % t), PAD - BASE[6], "lnt%d" % t)

    def level7_plain():
        H["h7"] = act(T.h7[:, :], T.tab[:, :].indirect(T.fl7[:, 32 * R:32 * R + 32]), F.Copy, tabs(6) + ["fl7"])

    def level7():
        src, hs = deep_source(T.flp[:, :], "flp")
        H["own7"] = tt(T.g7[:, :], src, T.h7[:, :], A.max, "h7", *hs)

    def split_level7():
        split_gather("split7", *deep_source(T.flp[:, :], "flp"), T.h7[:, :], ["h7"])

    def split_level7_max():
        H["own7"] = split_finish("split7", T.g7[:, :], A.max)

    def own_ap(d):
        if d >= 6:
            return T["g%d" % d][:, :]
        if d == 1:
            return T.msg[:, R, 64:68]
        return T.tab[:, BASE[d] + SIZE[d] * R:BASE[d] + SIZE[d] * R + SIZE[d]]

    def number_step(q, k, out, in_, *hs):
        return index(q, out, in_, MAGIC, *hs) if k == 1 else linear(q, out, in_, 1, FIRST - MAGIC, *hs)

    def yg_step(d, k, q="s"):
        c = slice(0 if d == 3 and k else OWN[d], OWN[d] + SIZE[d])
        if k == 0:
            H["ya%d" % d] = act(T.ya[:, c], own_ap(d), F.Ln, ["e12" if d == 1 else "own%d" % d] + ["late3"] * (d == 3))
        elif k == 1:
            H["yb%d" % d] = number_step(q, 1, T.yb[:, c], T.ya[:, c], *(["ya1", "ya2", "ya3"] if d == 3 else ["ya%d" % d]))
        else:
            store(T.yg[:, c], T.yo[:, c], number_step(q, 2, T.yo[:, c], T.yb[:, c], "yb%d" % d))

    def yf_low(q="s"):
        linear(q, T.yf12[:, 0:4], T.zz[:, 0:4], 1, 0, "zz")
        store(T.yf[:, 0:68], T.yf12[0:128:16, :], linear(q, T.yf12[:, 4:68], T.lr[:, 0:64], 1, 16, "ld_lr"))

    def yf_step(k, q="s"):
        if k == 0:
            H["fa"] = act(T.fa[:, :], T.py[:, 0:160], F.Ln, ["py7"])
        elif k == 1:
            H["fb"] = number_step(q, 1, T.fb[:, :], T.fa[:, :], "fa")
        else:
            store(T.yf[:, OWN[3]:OWN[7] + 512], T.fo[:, :], number_step(q, 2, T.fo[:, :], T.fb[:, :], "fb"))

    def largest():
        wait("v", "anew", *["ln" + n for n in BLOCK if BLOCK[n] < RUN])
        H["rm"] = fin("v", V.tensor_tensor_scan(T.rm[:, :], T.anew[:, :], T.ln[:, 0:32 * RUN], 0.0, A.min, A.max))

    def text_out():
        tt(T.last[:, 0:32], lnblock("t9"), lnblock("p9"), A.max, "lnt9", "lnp9")
        h = tt(T.last[:, 32:64], T.rm[:, RUN - 1:32 * RUN:RUN], lnblock("t9"), A.max, "rm")
        h = number_step("v", 1, T.lastm[:, :], T.last[:, :], h)
        h = number_step("v", 2, T.oy[:, :], T.lastm[:, :], h)
        store(T.yl[:, :], T.oy[:, 0:32], h)
        store(T.ym[:, :], T.oy[:, 32:64], h, "s")

    steps = {
        "first": first_message, "sumc": sum_constants, "scanc": scan_constants, "maskc": mask_constants, "wordc": word_constants,
        "weights": mask_weights, "code": to_code, "helper": to_helper, "send": to_ranks,
        "words": words, "wordlist": words_list, "words4": words4, "wordlist4": words4_list,
        "squares": squares, "pe": mask_pe, "mask": mask_out,
        "g2w": word_table, "y1": word_states, "list2": level2_list, "level2": level2, "late3": level3,
        "list3": level3_list, "early3": lambda k: early3((rest + [R])[k]),
        "D": fail_columns, "own_pe": own_pe, "own": complete_own, "other": lambda d, k: complete(d, rest[k]),
        "sother": lambda d, k: split_complete(d, rest[k]), "mother": lambda d, k: split_completed(d, rest[k]),
        "plain": lambda q, k: plain(q, rest[k]),
        "rows": fail_rows, "fail3": fail3, "fail": fail_gather, "fln": fail_ln, "flist": fail_list, "plist": fail_list_deep,
        "twords": text_words, "text1": text1, "text": text_gather, "deep": deep_gather, "sdeep": split_deep, "mdeep": split_deep_mask,
        "sums": text_sums, "ln": text_ln, "tlist": text_list, "dlist": deep_list,
        "h7": level7_plain, "g7": level7, "sg7": split_level7, "mg7": split_level7_max,
        "yg": yg_step, "yf12": yf_low, "yf": yf_step, "max": largest, "out": text_out,
    }
    for step in ORDER.split():
        name, *args = step.split(".")
        steps[name](*[int(a) if a.isdigit() else a for a in args])
    wait("gc", ("v", cnt["v"]), ("s", cnt["s"]), ("p", cnt["p"]), ("gc", cnt["gc"]), ("out", cnt["out"]), ("sent", cnt["sent"]))
